import numpy as np
import ml_dtypes


def mxq(x, axis, fmt="e4m3"):
    dtype, down = {"e4m3": (ml_dtypes.float8_e4m3fn, 7), "e5m2": (ml_dtypes.float8_e5m2, 14)}[fmt]
    v = np.moveaxis(np.asarray(x, np.float32).astype(ml_dtypes.bfloat16).astype(np.float64), axis, -1)
    blocks = v.reshape(v.shape[:-1] + (-1, 32))
    amax = np.abs(blocks).max(-1, keepdims=True)
    byte = np.maximum(np.where(amax > 0, np.frexp(amax)[1] - 1 + 127, 0) - down, 1)
    scale = np.exp2(byte - 127.0)
    codes = (blocks / scale).astype(np.float32).astype(dtype).astype(np.float64)
    return np.moveaxis((codes * scale).reshape(v.shape), -1, axis)


WIDE = False


def mx_kscale(k):
    if not WIDE:
        return np.ones(k)
    levels = np.array([10, -10, 5, -5, 0])
    if k % 512:
        return np.exp2(np.random.permutation(np.resize(levels, k // 32))).repeat(32)
    a = np.empty((k // 512, 16))
    for p in range(k // 512):
        a[p, :8] = np.random.permutation(np.resize(levels, 8))
        for g in range(8):
            far = levels[np.abs(levels - a[p, g]) >= 10]
            a[p, g + 8] = far[np.random.randint(len(far))]
    return np.exp2(a.ravel()).repeat(32)


def f64(x):
    return np.asarray(x).astype(np.float64)


def striped(idx):
    return np.tile(idx.reshape(-1, 16).T, (8, 1)).astype(np.uint16)


def unstriped(offs):
    return offs[:16].T.reshape(-1).astype(np.int64)


E2M1 = np.array([0.0, 0.5, 1.0, 1.5, 2.0, 3.0, 4.0, 6.0, -0.0, -0.5, -1.0, -1.5, -2.0, -3.0, -4.0, -6.0])


def pack_weight(w, fmt):
    k, n = w.shape
    w = f64(np.asarray(w, np.float32).astype(ml_dtypes.bfloat16)).reshape(k // 32, 32, n)
    amax = np.abs(w).max(1)
    if fmt == "e4m3":
        byte = np.frexp(amax)[1] - 1 + 127 - 7
    else:
        mant, ex = np.frexp(amax / 6.0)
        byte = np.where(mant > 0.5, ex, ex - 1) + 127
    byte = np.clip(np.where(amax > 0, byte, 1), 1, 254)
    scaled = (w * np.exp2(127.0 - byte)[:, None, :]).reshape(k, n).astype(np.float32)
    by_word = np.ascontiguousarray(scaled.reshape(k // 512, 128, 4, n).transpose(0, 1, 3, 2))
    if fmt == "e4m3":
        words = by_word.astype(ml_dtypes.float8_e4m3fn).view(np.uint8)
    else:
        c = by_word.astype(ml_dtypes.float4_e2m1fn).view(np.uint8) & 0xF
        words = (c[..., 0::2] | (c[..., 1::2] << 4)).reshape(k // 512, 128, 2 * n)
    return np.ascontiguousarray(words), np.ascontiguousarray(byte.astype(np.uint8).reshape(k // 512, 16, n))


def unpack_weight(words, scales, fmt):
    g, _, n = scales.shape
    words = np.ascontiguousarray(words).reshape(g, 128, n, -1)
    if fmt == "e4m3":
        vals = words.view(ml_dtypes.float8_e4m3fn).astype(np.float64)
    else:
        nib = np.empty((g, 128, n, 4), np.uint8)
        nib[..., 0::2] = words & 0xF
        nib[..., 1::2] = words >> 4
        vals = E2M1[nib]
    vals = vals * np.repeat(np.exp2(scales.astype(np.float64) - 127.0), 8, axis=1)[..., None]
    return vals.transpose(0, 1, 3, 2).reshape(g * 512, n)


def relu(v):
    return np.maximum(v, 0.0)


K, T, E, H, N = 2560, 512, 2, 512, 256
COUNTS = (128, 384)
STARTS = np.cumsum((0,) + COUNTS)


def by_expert(wq, xq):
    return np.concatenate([wq[e].T @ xq[:, STARTS[e]:STARTS[e + 1]] for e in range(E)], axis=1)


def setup_inputs():
    n = np.random.standard_normal
    s = mx_kscale(K)[:, None]
    u = mx_kscale(H)
    expert = np.random.permutation(np.repeat(np.arange(E), COUNTS))
    slot_token = np.argsort(expert, kind="stable")
    w1 = [pack_weight(m, "e2m1") for m in n((E, K, H)) / np.sqrt(K) / s[None]]
    w3 = [pack_weight(m, "e2m1") for m in n((E, K, H)) / np.sqrt(K) / s[None] * u[None, None, :]]
    w2 = [pack_weight(m, "e2m1") for m in n((E, H, N)) / np.sqrt(H) / u[None, :, None]]
    return {
        "xT": (n((K, T)) * s).astype(np.float32),
        "w1_words": np.stack([m[0] for m in w1]),
        "w1_scales": np.stack([m[1] for m in w1]),
        "w3_words": np.stack([m[0] for m in w3]),
        "w3_scales": np.stack([m[1] for m in w3]),
        "w2_words": np.stack([m[0] for m in w2]),
        "w2_scales": np.stack([m[1] for m in w2]),
        "gate": np.tile(np.random.uniform(0.2, 1.0, T), (N, 1)).astype(np.float32),
        "offs": striped(slot_token),
    }


def reference(xT, w1_words, w1_scales, w3_words, w3_scales, w2_words, w2_scales, gate, offs):
    idx = unstriped(offs)
    w1 = np.stack([unpack_weight(w1_words[e], w1_scales[e], "e2m1") for e in range(E)])
    w3 = np.stack([unpack_weight(w3_words[e], w3_scales[e], "e2m1") for e in range(E)])
    w2 = np.stack([unpack_weight(w2_words[e], w2_scales[e], "e2m1") for e in range(E)])
    xq = mxq(f64(xT)[:, idx], 0, "e4m3")
    h = relu(by_expert(w1, xq))
    h = h * by_expert(w3, xq)
    y = by_expert(w2, mxq(h, 0, "e4m3"))
    out = np.zeros((N, T))
    out[:, idx] = f64(gate) * y
    return out

@@ -1,0 +1,216 @@
+from contextlib import ExitStack
+
+import concourse.mybir as mybir
+from concourse.masks import make_identity
+
+FLOPS = 2818572288
+
+F32 = mybir.dt.float32
+BF16 = mybir.dt.bfloat16
+I32 = mybir.dt.int32
+U32 = mybir.dt.uint32
+U16 = mybir.dt.uint16
+U8 = mybir.dt.uint8
+E4M3 = mybir.dt.float8_e4m3fn_x4
+E2M1 = mybir.dt.float4_e2m1fn_x4
+COPY = mybir.ActivationFunctionType.Copy
+RELU = mybir.ActivationFunctionType.Relu
+MULT = mybir.AluOpType.mult
+
+P = 128
+T = 512
+E = 2
+H = 512
+N = 256
+PASSES = 5
+TILES = 4
+TILE_EXPERT = (0, 1, 1, 1)
+CAST_CUTS = (((0, 128, 256), (256, 320, 512)),) + (((0, 512, 512),),) * 4
+LIST_CUTS = ((0, 128), (128, 512))
+LAST_CUTS = ((128, 384), (384, 512), (0, 128))
+TILE_ORDER = (1, 2, 3, 0)
+
+
+def interleave(ap_in, ap_out):
+    return (
+        ap_out.rearrange("p (c i) t -> p c t i", i=4),
+        ap_in.rearrange("p t (c i) -> p c t i", i=4),
+    )
+
+
+def tile_moe_rag_glu_relu_kernel(
+    tc, xT, w1_words, w1_scales, w3_words, w3_scales, w2_words, w2_scales, gate, offs, out
+):
+    nc = tc.nc
+    with ExitStack() as ctx:
+        held = ctx.enter_context(tc.tile_pool(name="held", bufs=1))
+        ring = ctx.enter_context(tc.tile_pool(name="ring", bufs=2))
+        psum = ctx.enter_context(tc.psum_pool(name="psum", bufs=1))
+
+        offsets = held.tile([P, T // 16], U16, name="offsets")
+        x_raw = {}
+        tok_scales = [held.tile([P, T], U8, name=f"tok_scales{s}", align_bytes=64) for s in range(PASSES)]
+        slot_codes = [held.tile([P, T], U32, name=f"slot_codes{s}", align_bytes=64) for s in range(PASSES)]
+        slot_scales = [held.tile([P, T], U8, name=f"slot_scales{s}", align_bytes=64) for s in range(PASSES)]
+        words = [
+            [held.tile([P, E, 2 * H], U8, name=f"words{w}_{s}", align_bytes=64) for w in range(2)]
+            for s in range(PASSES)
+        ]
+        planes = [held.tile([P, E * PASSES, H], U8, name=f"planes{w}", align_bytes=64) for w in range(2)]
+        w2_codes = held.tile([P, E, 2 * N], U8, name="w2_codes", align_bytes=64)
+        w2_plane = held.tile([P, E, N], U8, name="w2_plane", align_bytes=64)
+        gates = held.tile([P, 2, T], F32, name="gates")
+        identity = held.tile([P, P], F32, name="identity")
+        y_slots = held.tile([P, 2, T], F32, name="y_slots")
+        y_tokens = [held.tile([P, T], F32, name=f"y_tokens{t}") for t in range(2)]
+        banks = [[psum.tile([P, H], F32, name=f"bank{w}_{m}", tag=f"bank{w}_{m}") for w in range(2)] for m in range(TILES)]
+
+        w_dram = (w1_words, w3_words)
+
+        def load_x(s, cols=slice(0, T)):
+            if s not in x_raw:
+                x_raw[s] = ring.tile([P, 4, T], F32, name="x_raw", bufs=3)
+            nc.sync.dma_start(
+                out=x_raw[s][:, :, cols],
+                in_=xT[4 * P * s : 4 * P * (s + 1), cols].rearrange("(p j) w -> p j w", j=4),
+            )
+
+        def load_w(s, experts):
+            for w in range(2):
+                nc.sync.dma_start(
+                    out=words[s][w][:, experts, :].bitcast(I32),
+                    in_=w_dram[w][experts, s].rearrange("e p b -> p e b").bitcast(I32),
+                )
+
+        nc.vector.memset(planes[0][:].bitcast(I32), 0)
+        nc.gpsimd.memset(planes[1][:].bitcast(I32), 0)
+        both = slice(0, E)
+        load_x(0, slice(0, 256))
+        load_x(0, slice(256, 512))
+        nc.sync.dma_start(offsets[:], offs)
+        for w, dram in enumerate((w1_scales, w3_scales)):
+            by_row = dram.rearrange("e s (q r) i -> r q (e s) i", r=4)
+            for r in range(4):
+                nc.sync.dma_start(out=planes[w][r:P:32].bitcast(I32), in_=by_row[r].bitcast(I32))
+            if w == 0:
+                load_x(1)
+        load_w(0, both)
+        load_x(2)
+        load_w(1, both)
+        load_x(3)
+        load_x(4)
+        load_w(2, both)
+        load_w(3, both)
+        nc.sync.dma_start(
+            out=w2_codes[:].bitcast(I32), in_=w2_words[:, 0].rearrange("e p b -> p e b").bitcast(I32)
+        )
+        load_w(4, slice(1, 2))
+        load_w(4, slice(0, 1))
+        nc.sync.dma_start(out=gates[:], in_=gate.rearrange("(t p) s -> p t s", p=P))
+
+        for s in range(PASSES):
+            nc.vector.memset(tok_scales[s][:].bitcast(I32), 0)
+        nc.vector.memset(w2_plane[:].bitcast(I32), 0)
+        by_row = w2_scales.rearrange("e s (q r) i -> r q (e s) i", r=4)
+        for r in range(4):
+            nc.gpsimd.dma_start(out=w2_plane[r:P:32].bitcast(I32), in_=by_row[r].bitcast(I32))
+        make_identity(nc, identity[:])
+
+        tok_codes = {}
+
+        def tokens(s):
+            x_bf = ring.tile([P, T, 4], BF16, name="x_bf", align_bytes=64)
+            tok_codes[s] = ring.tile([P, T], U32, name="tok_codes", align_bytes=64)
+            for a, cut, b in CAST_CUTS[s]:
+                if a < cut:
+                    dst, src = interleave(x_raw[s][:, :, a:cut], x_bf[:, a:cut, :])
+                    nc.scalar.activation(dst, src, COPY)
+                if cut < b:
+                    dst, src = interleave(x_raw[s][:, :, cut:b], x_bf[:, cut:b, :])
+                    nc.vector.tensor_copy(dst, src)
+                nc.vector.quantize_mx(
+                    out=tok_codes[s][:, a:b].bitcast(E4M3),
+                    scales=tok_scales[s][:, a:b],
+                    in_=x_bf[:, a:b, :].rearrange("p w j -> p (w j)"),
+                )
+
+        def gather(s, cuts):
+            for a, b in cuts:
+                picked = offsets[:, a // 16 : b // 16]
+                nc.vector.tensor_copy(slot_codes[s][:, a:b], tok_codes[s][:].indirect(picked))
+                nc.vector.tensor_copy(slot_scales[s][:, a:b], tok_scales[s][:].indirect(picked))
+
+        def multiply(s, m):
+            e = TILE_EXPERT[m]
+            cols = slice(P * m, P * (m + 1))
+            for w in range(2):
+                nc.tensor.matmul_mx(
+                    out=banks[m][w][:],
+                    lhsT=slot_codes[s][:, cols].bitcast(E4M3),
+                    lhsT_scale=slot_scales[s][:, cols],
+                    rhs=words[s][w][:, e, :].bitcast(E2M1),
+                    rhs_scale=planes[w][:, e * PASSES + s, :],
+                    start=(s == 0),
+                    stop=(s == PASSES - 1),
+                )
+
+        tokens(0)
+        for s in range(PASSES):
+            if s + 1 < PASSES:
+                tokens(s + 1)
+            gather(s, LIST_CUTS if s < PASSES - 1 else LAST_CUTS)
+            for m in TILE_ORDER if s == PASSES - 1 else range(TILES):
+                multiply(s, m)
+
+        h, h_in, turned, h_codes, h_scales, y, a_pos = {}, {}, {}, {}, {}, {}, {}
+        for m in TILE_ORDER:
+            a_pos[m] = held.tile([P, H], F32, name=f"a_pos{m}")
+            nc.scalar.activation(a_pos[m][:], banks[m][0][:], RELU)
+        for m in TILE_ORDER:
+            h[m] = held.tile([P, 2, P, 2], BF16, name=f"h{m}", align_bytes=64)
+            nc.vector.tensor_tensor(
+                h[m][:],
+                banks[m][1][:].rearrange("p (q u v) -> p u q v", u=2, v=2),
+                a_pos[m][:].rearrange("p (q u v) -> p u q v", u=2, v=2),
+                MULT,
+            )
+        for m in TILE_ORDER:
+            turned[m] = psum.tile([P, 2, P], F32, name=f"turned{m}", tag=f"bank0_{m}")
+            pairs = h[m][:].rearrange("p u q v -> p (u q v)").bitcast(F32)
+            for u in range(2):
+                nc.tensor.transpose(turned[m][:, u, :], pairs[:, P * u : P * (u + 1)], identity[:])
+        for m in TILE_ORDER:
+            h_in[m] = held.tile([P, P, 4], BF16, name=f"h_in{m}", align_bytes=64)
+            nc.scalar.copy(
+                h_in[m][:].rearrange("p c d -> p (c d)").bitcast(F32).rearrange("p (c u) -> p c u", u=2),
+                turned[m][:].rearrange("p u c -> p c u"),
+            )
+        for m in TILE_ORDER:
+            h_codes[m] = held.tile([P, P], U32, name=f"h_codes{m}", align_bytes=64)
+            h_scales[m] = held.tile([P, P], U8, name=f"h_scales{m}", align_bytes=64)
+            nc.vector.quantize_mx(
+                out=h_codes[m][:].bitcast(E4M3), scales=h_scales[m][:], in_=h_in[m][:].rearrange("p c d -> p (c d)")
+            )
+        for m in TILE_ORDER:
+            e = TILE_EXPERT[m]
+            y[m] = psum.tile([P, 2, P], F32, name=f"y{m}", tag=f"bank1_{m}")
+            for t in range(2):
+                nc.tensor.matmul_mx(
+                    out=y[m][:, t, :],
+                    lhsT=w2_codes[:, e, 2 * P * t : 2 * P * (t + 1)].bitcast(E2M1),
+                    lhsT_scale=w2_plane[:, e, P * t : P * (t + 1)],
+                    rhs=h_codes[m][:].bitcast(E4M3),
+                    rhs_scale=h_scales[m][:],
+                    start=True,
+                    stop=True,
+                )
+        for m in TILE_ORDER:
+            nc.scalar.copy(y_slots[:, :, P * m : P * (m + 1)], y[m][:])
+        for a, b in ((128, 384), (384, 512), (0, 128)):
+            for t in range(2):
+                cols = slice(a, b)
+                nc.vector.tensor_tensor(
+                    y_tokens[t][:].indirect(offsets[:, a // 16 : b // 16]), y_slots[:, t, cols], gates[:, t, cols], MULT
+                )
+        for t in range(2):
+            nc.sync.dma_start(out=out[P * t : P * (t + 1), :], in_=y_tokens[t][:])

@@ -25,10 +25,11 @@ N = 256
 PASSES = 5
 TILES = 4
 TILE_EXPERT = (0, 1, 1, 1)
-CAST_CUTS = (((0, 128, 256), (256, 320, 512)),) + (((0, 512, 512),),) * 4
-LIST_CUTS = ((0, 128), (128, 512))
-LAST_CUTS = ((128, 384), (384, 512), (0, 128))
+CAST_CUTS = (((0, 128, 256), (256, 320, 512)),) + (((0, 256, 256), (256, 512, 512)),) * 4
+LIST_CUTS = ((128, 512), (0, 128))
+LAST_CUTS = ((128, 256), (256, 512), (0, 128))
 TILE_ORDER = (1, 2, 3, 0)
+TURN_BANK = {1: 1, 2: 2, 3: 3, 0: 0}
 
 
 def interleave(ap_in, ap_out):
@@ -52,14 +53,13 @@ def tile_moe_rag_glu_relu_kernel(
         tok_scales = [held.tile([P, T], U8, name=f"tok_scales{s}", align_bytes=64) for s in range(PASSES)]
         slot_codes = [held.tile([P, T], U32, name=f"slot_codes{s}", align_bytes=64) for s in range(PASSES)]
         slot_scales = [held.tile([P, T], U8, name=f"slot_scales{s}", align_bytes=64) for s in range(PASSES)]
-        words = [
-            [held.tile([P, E, 2 * H], U8, name=f"words{w}_{s}", align_bytes=64) for w in range(2)]
-            for s in range(PASSES)
+        words = {}
+        planes = [
+            [held.tile([P, PASSES, H], U8, name=f"planes{e}_{w}", align_bytes=64) for w in range(2)] for e in range(E)
         ]
-        planes = [held.tile([P, E * PASSES, H], U8, name=f"planes{w}", align_bytes=64) for w in range(2)]
         w2_codes = held.tile([P, E, 2 * N], U8, name="w2_codes", align_bytes=64)
         w2_plane = held.tile([P, E, N], U8, name="w2_plane", align_bytes=64)
-        gates = held.tile([P, 2, T], F32, name="gates")
+        gates = held.tile([P, T], F32, name="gates")
         identity = held.tile([P, P], F32, name="identity")
         y_slots = held.tile([P, 2, T], F32, name="y_slots")
         y_tokens = [held.tile([P, T], F32, name=f"y_tokens{t}") for t in range(2)]
@@ -69,44 +69,50 @@ def tile_moe_rag_glu_relu_kernel(
 
         def load_x(s, cols=slice(0, T)):
             if s not in x_raw:
-                x_raw[s] = ring.tile([P, 4, T], F32, name="x_raw", bufs=3)
+                x_raw[s] = held.tile([P, 4, T], F32, name=f"x_raw{s}")
             nc.sync.dma_start(
                 out=x_raw[s][:, :, cols],
                 in_=xT[4 * P * s : 4 * P * (s + 1), cols].rearrange("(p j) w -> p j w", j=4),
             )
 
-        def load_w(s, experts):
+        def load_w(e, first, last):
             for w in range(2):
+                part = held.tile([P, last - first, 2 * H], U8, name=f"words{e}_{w}_{first}", align_bytes=64)
                 nc.sync.dma_start(
-                    out=words[s][w][:, experts, :].bitcast(I32),
-                    in_=w_dram[w][experts, s].rearrange("e p b -> p e b").bitcast(I32),
+                    out=part[:].bitcast(I32),
+                    in_=w_dram[w][e, first:last].rearrange("s p b -> p s b").bitcast(I32),
                 )
+                for s in range(first, last):
+                    words[e, w, s] = part[:, s - first, :]
 
-        nc.vector.memset(planes[0][:].bitcast(I32), 0)
-        nc.gpsimd.memset(planes[1][:].bitcast(I32), 0)
-        both = slice(0, E)
+        def load_scales(e):
+            for w, dram in enumerate((w1_scales, w3_scales)):
+                by_row = dram[e].rearrange("s (q r) i -> r q s i", r=4)
+                for r in range(4):
+                    nc.sync.dma_start(out=planes[e][w][r:P:32].bitcast(I32), in_=by_row[r].bitcast(I32))
+
+        for e in (1, 0):
+            for w in range(2):
+                nc.vector.memset(planes[e][w][:].bitcast(I32), 0)
         load_x(0, slice(0, 256))
         load_x(0, slice(256, 512))
         nc.sync.dma_start(offsets[:], offs)
-        for w, dram in enumerate((w1_scales, w3_scales)):
-            by_row = dram.rearrange("e s (q r) i -> r q (e s) i", r=4)
-            for r in range(4):
-                nc.sync.dma_start(out=planes[w][r:P:32].bitcast(I32), in_=by_row[r].bitcast(I32))
-            if w == 0:
-                load_x(1)
-        load_w(0, both)
+        load_x(1)
         load_x(2)
-        load_w(1, both)
+        load_scales(1)
+        load_w(1, 0, 1)
         load_x(3)
+        load_w(1, 1, 3)
         load_x(4)
-        load_w(2, both)
-        load_w(3, both)
+        load_w(1, 3, 5)
         nc.sync.dma_start(
             out=w2_codes[:].bitcast(I32), in_=w2_words[:, 0].rearrange("e p b -> p e b").bitcast(I32)
         )
-        load_w(4, slice(1, 2))
-        load_w(4, slice(0, 1))
-        nc.sync.dma_start(out=gates[:], in_=gate.rearrange("(t p) s -> p t s", p=P))
+        load_scales(0)
+        load_w(0, 0, 2)
+        nc.sync.dma_start(out=gates[:], in_=gate[0:P, :])
+        load_w(0, 2, 4)
+        load_w(0, 4, 5)
 
         for s in range(PASSES):
             nc.vector.memset(tok_scales[s][:].bitcast(I32), 0)
@@ -148,8 +154,8 @@ def tile_moe_rag_glu_relu_kernel(
                     out=banks[m][w][:],
                     lhsT=slot_codes[s][:, cols].bitcast(E4M3),
                     lhsT_scale=slot_scales[s][:, cols],
-                    rhs=words[s][w][:, e, :].bitcast(E2M1),
-                    rhs_scale=planes[w][:, e * PASSES + s, :],
+                    rhs=words[e, w, s].bitcast(E2M1),
+                    rhs_scale=planes[e][w][:, s, :],
                     start=(s == 0),
                     stop=(s == PASSES - 1),
                 )
@@ -159,8 +165,10 @@ def tile_moe_rag_glu_relu_kernel(
             if s + 1 < PASSES:
                 tokens(s + 1)
             gather(s, LIST_CUTS if s < PASSES - 1 else LAST_CUTS)
-            for m in TILE_ORDER if s == PASSES - 1 else range(TILES):
+            for m in TILE_ORDER[:-1]:
                 multiply(s, m)
+        for s in range(PASSES):
+            multiply(s, 0)
 
         h, h_in, turned, h_codes, h_scales, y, a_pos = {}, {}, {}, {}, {}, {}, {}
         for m in TILE_ORDER:
@@ -175,7 +183,7 @@ def tile_moe_rag_glu_relu_kernel(
                 MULT,
             )
         for m in TILE_ORDER:
-            turned[m] = psum.tile([P, 2, P], F32, name=f"turned{m}", tag=f"bank0_{m}")
+            turned[m] = psum.tile([P, 2, P], F32, name=f"turned{m}", tag=f"bank0_{TURN_BANK[m]}")
             pairs = h[m][:].rearrange("p u q v -> p (u q v)").bitcast(F32)
             for u in range(2):
                 nc.tensor.transpose(turned[m][:, u, :], pairs[:, P * u : P * (u + 1)], identity[:])
@@ -206,11 +214,11 @@ def tile_moe_rag_glu_relu_kernel(
                 )
         for m in TILE_ORDER:
             nc.scalar.copy(y_slots[:, :, P * m : P * (m + 1)], y[m][:])
-        for a, b in ((128, 384), (384, 512), (0, 128)):
+        for a, b in ((128, 256), (256, 384), (384, 512), (0, 128)):
             for t in range(2):
                 cols = slice(a, b)
                 nc.vector.tensor_tensor(
-                    y_tokens[t][:].indirect(offsets[:, a // 16 : b // 16]), y_slots[:, t, cols], gates[:, t, cols], MULT
+                    y_tokens[t][:].indirect(offsets[:, a // 16 : b // 16]), y_slots[:, t, cols], gates[:, cols], MULT
                 )
         for t in range(2):
             nc.sync.dma_start(out=out[P * t : P * (t + 1), :], in_=y_tokens[t][:])

@@ -25,11 +25,14 @@ N = 256
 PASSES = 5
 TILES = 4
 TILE_EXPERT = (0, 1, 1, 1)
-CAST_CUTS = (((0, 128, 256), (256, 320, 512)),) + (((0, 256, 256), (256, 512, 512)),) * 4
-LIST_CUTS = ((128, 512), (0, 128))
-LAST_CUTS = ((128, 256), (256, 512), (0, 128))
-TILE_ORDER = (1, 2, 3, 0)
-TURN_BANK = {1: 1, 2: 2, 3: 3, 0: 0}
+CAST_CUTS = (((0, 128, 256), (256, 320, 512)),) + (((0, 384, 512),),) + (((0, 512, 512),),) * 3
+LIST_CUTS = ((0, 512),)
+SPARE = 192
+PACKED = 1
+LAST_CUTS = ((256, 384), (384, 512), (0, 256))
+TILE_ORDER = (2, 3, 1, 0)
+BACK_CUTS = ((256, 512), (128, 256), (0, 128))
+Y_BANK = {2: "bank1_2", 3: "bank1_3", 1: "bank0_0", 0: "bank1_0"}
 
 
 def interleave(ap_in, ap_out):
@@ -50,7 +53,8 @@ def tile_moe_rag_glu_relu_kernel(
 
         offsets = held.tile([P, T // 16], U16, name="offsets")
         x_raw = {}
-        tok_scales = [held.tile([P, T], U8, name=f"tok_scales{s}", align_bytes=64) for s in range(PASSES)]
+        tok_codes = held.tile([P, PASSES * T + SPARE], U32, name="tok_codes", align_bytes=64)
+        tok_scales = held.tile([P, PASSES * T + SPARE], U8, name="tok_scales", align_bytes=64)
         slot_codes = [held.tile([P, T], U32, name=f"slot_codes{s}", align_bytes=64) for s in range(PASSES)]
         slot_scales = [held.tile([P, T], U8, name=f"slot_scales{s}", align_bytes=64) for s in range(PASSES)]
         words = {}
@@ -61,8 +65,7 @@ def tile_moe_rag_glu_relu_kernel(
         w2_plane = held.tile([P, E, N], U8, name="w2_plane", align_bytes=64)
         gates = held.tile([P, T], F32, name="gates")
         identity = held.tile([P, P], F32, name="identity")
-        y_slots = held.tile([P, 2, T], F32, name="y_slots")
-        y_tokens = [held.tile([P, T], F32, name=f"y_tokens{t}") for t in range(2)]
+        y_slots = {a: held.tile([P, 2, b - a], F32, name=f"y_slots{a}") for a, b in BACK_CUTS}
         banks = [[psum.tile([P, H], F32, name=f"bank{w}_{m}", tag=f"bank{w}_{m}") for w in range(2)] for m in range(TILES)]
 
         w_dram = (w1_words, w3_words)
@@ -75,8 +78,8 @@ def tile_moe_rag_glu_relu_kernel(
                 in_=xT[4 * P * s : 4 * P * (s + 1), cols].rearrange("(p j) w -> p j w", j=4),
             )
 
-        def load_w(e, first, last):
-            for w in range(2):
+        def load_w(e, first, last, matrices=(0, 1)):
+            for w in matrices:
                 part = held.tile([P, last - first, 2 * H], U8, name=f"words{e}_{w}_{first}", align_bytes=64)
                 nc.sync.dma_start(
                     out=part[:].bitcast(I32),
@@ -85,48 +88,54 @@ def tile_moe_rag_glu_relu_kernel(
                 for s in range(first, last):
                     words[e, w, s] = part[:, s - first, :]
 
-        def load_scales(e):
-            for w, dram in enumerate((w1_scales, w3_scales)):
-                by_row = dram[e].rearrange("s (q r) i -> r q s i", r=4)
-                for r in range(4):
-                    nc.sync.dma_start(out=planes[e][w][r:P:32].bitcast(I32), in_=by_row[r].bitcast(I32))
+        def load_scales(e, w):
+            by_row = (w1_scales, w3_scales)[w][e].rearrange("s (q r) i -> r q s i", r=4)
+            for r in range(4):
+                nc.sync.dma_start(out=planes[e][w][r:P:32].bitcast(I32), in_=by_row[r].bitcast(I32))
 
-        for e in (1, 0):
-            for w in range(2):
-                nc.vector.memset(planes[e][w][:].bitcast(I32), 0)
+        for w in range(2):
+            nc.vector.memset(planes[1][w][:].bitcast(I32), 0)
+            nc.gpsimd.memset(planes[0][w][:].bitcast(I32), 0)
         load_x(0, slice(0, 256))
         load_x(0, slice(256, 512))
         nc.sync.dma_start(offsets[:], offs)
         load_x(1)
+        load_scales(1, 0)
         load_x(2)
-        load_scales(1)
+        load_scales(1, 1)
         load_w(1, 0, 1)
         load_x(3)
         load_w(1, 1, 3)
         load_x(4)
+        load_scales(0, 0)
         load_w(1, 3, 5)
+        load_w(0, 0, 5, (0,))
         nc.sync.dma_start(
             out=w2_codes[:].bitcast(I32), in_=w2_words[:, 0].rearrange("e p b -> p e b").bitcast(I32)
         )
-        load_scales(0)
-        load_w(0, 0, 2)
         nc.sync.dma_start(out=gates[:], in_=gate[0:P, :])
-        load_w(0, 2, 4)
-        load_w(0, 4, 5)
+        load_scales(0, 1)
+        load_w(0, 0, 5, (1,))
 
-        for s in range(PASSES):
-            nc.vector.memset(tok_scales[s][:].bitcast(I32), 0)
+        nc.vector.memset(tok_scales[:].bitcast(I32), 0)
+        nc.vector.memset(tok_codes[:, PASSES * T :].bitcast(I32), 0)
+        for s in range(1, PACKED):
+            nc.vector.memset(slot_scales[s][:].bitcast(I32), 0)
         nc.vector.memset(w2_plane[:].bitcast(I32), 0)
         by_row = w2_scales.rearrange("e s (q r) i -> r q (e s) i", r=4)
         for r in range(4):
             nc.gpsimd.dma_start(out=w2_plane[r:P:32].bitcast(I32), in_=by_row[r].bitcast(I32))
         make_identity(nc, identity[:])
 
-        tok_codes = {}
+        def code_col(s):
+            return (PASSES - 1 - s) * T
+
+        def scale_col(s):
+            return (PASSES - 1 - max(s, PACKED - 1)) * T
 
         def tokens(s):
             x_bf = ring.tile([P, T, 4], BF16, name="x_bf", align_bytes=64)
-            tok_codes[s] = ring.tile([P, T], U32, name="tok_codes", align_bytes=64)
+            row = 4 * s if s < PACKED else 0
             for a, cut, b in CAST_CUTS[s]:
                 if a < cut:
                     dst, src = interleave(x_raw[s][:, :, a:cut], x_bf[:, a:cut, :])
@@ -135,16 +144,25 @@ def tile_moe_rag_glu_relu_kernel(
                     dst, src = interleave(x_raw[s][:, :, cut:b], x_bf[:, cut:b, :])
                     nc.vector.tensor_copy(dst, src)
                 nc.vector.quantize_mx(
-                    out=tok_codes[s][:, a:b].bitcast(E4M3),
-                    scales=tok_scales[s][:, a:b],
+                    out=tok_codes[:, code_col(s) + a : code_col(s) + b].bitcast(E4M3),
+                    scales=tok_scales[row:P, scale_col(s) + a : scale_col(s) + b],
                     in_=x_bf[:, a:b, :].rearrange("p w j -> p (w j)"),
                 )
 
         def gather(s, cuts):
             for a, b in cuts:
                 picked = offsets[:, a // 16 : b // 16]
-                nc.vector.tensor_copy(slot_codes[s][:, a:b], tok_codes[s][:].indirect(picked))
-                nc.vector.tensor_copy(slot_scales[s][:, a:b], tok_scales[s][:].indirect(picked))
+                if s >= PACKED - 1:
+                    window = tok_scales[:, scale_col(s) : scale_col(s) + T + SPARE]
+                    nc.vector.tensor_copy(slot_scales[s if s >= PACKED else 0][:, a:b], window.indirect(picked))
+                window = tok_codes[:, code_col(s) : code_col(s) + T + SPARE]
+                nc.vector.tensor_copy(slot_codes[s][:, a:b], window.indirect(picked))
+            if s == PACKED - 1:
+                for a in range(1, PACKED):
+                    nc.gpsimd.dma_start(
+                        out=slot_scales[a][0:100, :].bitcast(I32),
+                        in_=slot_scales[0][4 * a : 4 * a + 100, :].bitcast(I32),
+                    )
 
         def multiply(s, m):
             e = TILE_EXPERT[m]
@@ -160,65 +178,85 @@ def tile_moe_rag_glu_relu_kernel(
                     stop=(s == PASSES - 1),
                 )
 
-        tokens(0)
         for s in range(PASSES):
-            if s + 1 < PASSES:
-                tokens(s + 1)
+            tokens(s)
             gather(s, LIST_CUTS if s < PASSES - 1 else LAST_CUTS)
+        for s in range(PASSES):
             for m in TILE_ORDER[:-1]:
                 multiply(s, m)
-        for s in range(PASSES):
-            multiply(s, 0)
 
         h, h_in, turned, h_codes, h_scales, y, a_pos = {}, {}, {}, {}, {}, {}, {}
-        for m in TILE_ORDER:
-            a_pos[m] = held.tile([P, H], F32, name=f"a_pos{m}")
-            nc.scalar.activation(a_pos[m][:], banks[m][0][:], RELU)
-        for m in TILE_ORDER:
-            h[m] = held.tile([P, 2, P, 2], BF16, name=f"h{m}", align_bytes=64)
-            nc.vector.tensor_tensor(
-                h[m][:],
-                banks[m][1][:].rearrange("p (q u v) -> p u q v", u=2, v=2),
-                a_pos[m][:].rearrange("p (q u v) -> p u q v", u=2, v=2),
-                MULT,
-            )
-        for m in TILE_ORDER:
-            turned[m] = psum.tile([P, 2, P], F32, name=f"turned{m}", tag=f"bank0_{TURN_BANK[m]}")
-            pairs = h[m][:].rearrange("p u q v -> p (u q v)").bitcast(F32)
-            for u in range(2):
-                nc.tensor.transpose(turned[m][:, u, :], pairs[:, P * u : P * (u + 1)], identity[:])
-        for m in TILE_ORDER:
-            h_in[m] = held.tile([P, P, 4], BF16, name=f"h_in{m}", align_bytes=64)
-            nc.scalar.copy(
-                h_in[m][:].rearrange("p c d -> p (c d)").bitcast(F32).rearrange("p (c u) -> p c u", u=2),
-                turned[m][:].rearrange("p u c -> p c u"),
-            )
-        for m in TILE_ORDER:
-            h_codes[m] = held.tile([P, P], U32, name=f"h_codes{m}", align_bytes=64)
-            h_scales[m] = held.tile([P, P], U8, name=f"h_scales{m}", align_bytes=64)
-            nc.vector.quantize_mx(
-                out=h_codes[m][:].bitcast(E4M3), scales=h_scales[m][:], in_=h_in[m][:].rearrange("p c d -> p (c d)")
-            )
-        for m in TILE_ORDER:
-            e = TILE_EXPERT[m]
-            y[m] = psum.tile([P, 2, P], F32, name=f"y{m}", tag=f"bank1_{m}")
-            for t in range(2):
-                nc.tensor.matmul_mx(
-                    out=y[m][:, t, :],
-                    lhsT=w2_codes[:, e, 2 * P * t : 2 * P * (t + 1)].bitcast(E2M1),
-                    lhsT_scale=w2_plane[:, e, P * t : P * (t + 1)],
-                    rhs=h_codes[m][:].bitcast(E4M3),
-                    rhs_scale=h_scales[m][:],
-                    start=True,
-                    stop=True,
-                )
-        for m in TILE_ORDER:
-            nc.scalar.copy(y_slots[:, :, P * m : P * (m + 1)], y[m][:])
-        for a, b in ((128, 256), (256, 384), (384, 512), (0, 128)):
-            for t in range(2):
-                cols = slice(a, b)
+
+        def hidden(tiles):
+            for m in tiles:
+                a_pos[m] = held.tile([P, H], F32, name=f"a_pos{m}", tag=f"a_pos{m}")
+                nc.scalar.activation(a_pos[m][:], banks[m][0][:], RELU)
+            for m in tiles:
+                h[m] = held.tile([P, 2, P, 2], BF16, name=f"h{m}", align_bytes=64)
                 nc.vector.tensor_tensor(
-                    y_tokens[t][:].indirect(offsets[:, a // 16 : b // 16]), y_slots[:, t, cols], gates[:, cols], MULT
+                    h[m][:],
+                    banks[m][1][:].rearrange("p (q u v) -> p u q v", u=2, v=2),
+                    a_pos[m][:].rearrange("p (q u v) -> p u q v", u=2, v=2),
+                    MULT,
                 )
+
+        def hidden_codes(tiles):
+            for m in tiles:
+                turned[m] = psum.tile([P, 2, P], F32, name=f"turned{m}", tag=f"bank0_{m}")
+                pairs = h[m][:].rearrange("p u q v -> p (u q v)").bitcast(F32)
+                for u in range(2):
+                    nc.tensor.transpose(turned[m][:, u, :], pairs[:, P * u : P * (u + 1)], identity[:])
+            for m in tiles:
+                h_in[m] = held.tile([P, P, 4], BF16, name=f"h_in{m}", align_bytes=64)
+                nc.scalar.copy(
+                    h_in[m][:].rearrange("p c d -> p (c d)").bitcast(F32).rearrange("p (c u) -> p c u", u=2),
+                    turned[m][:].rearrange("p u c -> p c u"),
+                )
+            for m in tiles:
+                h_codes[m] = held.tile([P, P], U32, name=f"h_codes{m}", align_bytes=64)
+                h_scales[m] = held.tile([P, P], U8, name=f"h_scales{m}", align_bytes=64)
+                nc.vector.quantize_mx(
+                    out=h_codes[m][:].bitcast(E4M3), scales=h_scales[m][:], in_=h_in[m][:].rearrange("p c d -> p (c d)")
+                )
+
+        def second_product(tiles):
+            for m in tiles:
+                e = TILE_EXPERT[m]
+                y[m] = psum.tile([P, 2, P], F32, name=f"y{m}", tag=Y_BANK[m])
+                for t in range(2):
+                    nc.tensor.matmul_mx(
+                        out=y[m][:, t, :],
+                        lhsT=w2_codes[:, e, 2 * P * t : 2 * P * (t + 1)].bitcast(E2M1),
+                        lhsT_scale=w2_plane[:, e, P * t : P * (t + 1)],
+                        rhs=h_codes[m][:].bitcast(E4M3),
+                        rhs_scale=h_scales[m][:],
+                        start=True,
+                        stop=True,
+                    )
+            for m in tiles:
+                a = max(a for a, b in BACK_CUTS if a <= P * m)
+                nc.scalar.copy(y_slots[a][:, :, P * m - a : P * (m + 1) - a], y[m][:])
+
+        y_tokens = {}
+
+        def scatter(t, a, b):
+            nc.vector.tensor_tensor(
+                y_tokens[t][:].indirect(offsets[:, a // 16 : b // 16]), y_slots[a][:, t, :], gates[:, a:b], MULT
+            )
+
+        hidden((2, 3, 1))
+        hidden_codes((2, 3, 1))
+        second_product((2, 3))
+        y_tokens[0] = held.tile([P, T], F32, name="y_tokens0")
+        scatter(0, 256, 512)
+        for s in range(PASSES):
+            multiply(s, 0)
+        hidden((0,))
+        y_tokens[1] = held.tile([P, T], F32, name="y_tokens1", tag="a_pos0")
+        scatter(1, 256, 512)
+        hidden_codes((0,))
+        second_product((1, 0))
+        for t, (a, b) in ((0, BACK_CUTS[1]), (1, BACK_CUTS[1]), (0, BACK_CUTS[2]), (1, BACK_CUTS[2])):
+            scatter(t, a, b)
         for t in range(2):
             nc.sync.dma_start(out=out[P * t : P * (t + 1), :], in_=y_tokens[t][:])

@@ -25,14 +25,15 @@ N = 256
 PASSES = 5
 TILES = 4
 TILE_EXPERT = (0, 1, 1, 1)
-CAST_CUTS = (((0, 128, 256), (256, 320, 512)),) + (((0, 384, 512),),) + (((0, 512, 512),),) * 3
+CAST_CUTS = (((0, 128, 256), (256, 320, 384), (384, 448, 512)),) + (((0, 384, 512),),) + (((0, 512, 512),),) * 3
 LIST_CUTS = ((0, 512),)
 SPARE = 192
 PACKED = 1
 LAST_CUTS = ((256, 384), (384, 512), (0, 256))
+LAST_FIRST = (4, 0, 1, 2, 3)
 TILE_ORDER = (2, 3, 1, 0)
 BACK_CUTS = ((256, 512), (128, 256), (0, 128))
-Y_BANK = {2: "bank1_2", 3: "bank1_3", 1: "bank0_0", 0: "bank1_0"}
+Y_BANK = {2: "bank1_2", 1: "bank0_0", 0: "bank1_0"}
 
 
 def interleave(ap_in, ap_out):
@@ -96,8 +97,10 @@ def tile_moe_rag_glu_relu_kernel(
         for w in range(2):
             nc.vector.memset(planes[1][w][:].bitcast(I32), 0)
             nc.gpsimd.memset(planes[0][w][:].bitcast(I32), 0)
+        nc.gpsimd.memset(w2_plane[:].bitcast(I32), 0)
         load_x(0, slice(0, 256))
-        load_x(0, slice(256, 512))
+        load_x(0, slice(256, 384))
+        load_x(0, slice(384, 512))
         nc.sync.dma_start(offsets[:], offs)
         load_x(1)
         load_scales(1, 0)
@@ -107,12 +110,15 @@ def tile_moe_rag_glu_relu_kernel(
         load_x(3)
         load_w(1, 1, 3)
         load_x(4)
-        load_scales(0, 0)
         load_w(1, 3, 5)
+        load_scales(0, 0)
         load_w(0, 0, 5, (0,))
         nc.sync.dma_start(
             out=w2_codes[:].bitcast(I32), in_=w2_words[:, 0].rearrange("e p b -> p e b").bitcast(I32)
         )
+        by_row = w2_scales.rearrange("e s (q r) i -> r q (e s) i", r=4)
+        for r in range(4):
+            nc.sync.dma_start(out=w2_plane[r:P:32].bitcast(I32), in_=by_row[r].bitcast(I32))
         nc.sync.dma_start(out=gates[:], in_=gate[0:P, :])
         load_scales(0, 1)
         load_w(0, 0, 5, (1,))
@@ -121,10 +127,6 @@ def tile_moe_rag_glu_relu_kernel(
         nc.vector.memset(tok_codes[:, PASSES * T :].bitcast(I32), 0)
         for s in range(1, PACKED):
             nc.vector.memset(slot_scales[s][:].bitcast(I32), 0)
-        nc.vector.memset(w2_plane[:].bitcast(I32), 0)
-        by_row = w2_scales.rearrange("e s (q r) i -> r q (e s) i", r=4)
-        for r in range(4):
-            nc.gpsimd.dma_start(out=w2_plane[r:P:32].bitcast(I32), in_=by_row[r].bitcast(I32))
         make_identity(nc, identity[:])
 
         def code_col(s):
@@ -164,7 +166,7 @@ def tile_moe_rag_glu_relu_kernel(
                         in_=slot_scales[0][4 * a : 4 * a + 100, :].bitcast(I32),
                     )
 
-        def multiply(s, m):
+        def multiply(s, m, order=range(PASSES)):
             e = TILE_EXPERT[m]
             cols = slice(P * m, P * (m + 1))
             for w in range(2):
@@ -174,8 +176,8 @@ def tile_moe_rag_glu_relu_kernel(
                     lhsT_scale=slot_scales[s][:, cols],
                     rhs=words[e, w, s].bitcast(E2M1),
                     rhs_scale=planes[e][w][:, s, :],
-                    start=(s == 0),
-                    stop=(s == PASSES - 1),
+                    start=(s == order[0]),
+                    stop=(s == order[-1]),
                 )
 
         for s in range(PASSES):
@@ -200,42 +202,43 @@ def tile_moe_rag_glu_relu_kernel(
                     MULT,
                 )
 
-        def hidden_codes(tiles):
-            for m in tiles:
-                turned[m] = psum.tile([P, 2, P], F32, name=f"turned{m}", tag=f"bank0_{m}")
-                pairs = h[m][:].rearrange("p u q v -> p (u q v)").bitcast(F32)
-                for u in range(2):
-                    nc.tensor.transpose(turned[m][:, u, :], pairs[:, P * u : P * (u + 1)], identity[:])
-            for m in tiles:
-                h_in[m] = held.tile([P, P, 4], BF16, name=f"h_in{m}", align_bytes=64)
-                nc.scalar.copy(
-                    h_in[m][:].rearrange("p c d -> p (c d)").bitcast(F32).rearrange("p (c u) -> p c u", u=2),
-                    turned[m][:].rearrange("p u c -> p c u"),
-                )
-            for m in tiles:
-                h_codes[m] = held.tile([P, P], U32, name=f"h_codes{m}", align_bytes=64)
-                h_scales[m] = held.tile([P, P], U8, name=f"h_scales{m}", align_bytes=64)
+        def hidden_codes(groups):
+            for group in groups:
+                for m in group:
+                    turned[m] = psum.tile([P, 2, P], F32, name=f"turned{m}", tag=f"bank0_{m}")
+                    pairs = h[m][:].rearrange("p u q v -> p (u q v)").bitcast(F32)
+                    for u in range(2):
+                        nc.tensor.transpose(turned[m][:, u, :], pairs[:, P * u : P * (u + 1)], identity[:])
+            for group in groups:
+                h_in[group] = held.tile([P, P * len(group) * 4], BF16, name=f"h_in{group[0]}", align_bytes=64)
+                for n, m in enumerate(group):
+                    nc.scalar.copy(
+                        h_in[group][:, 4 * P * n : 4 * P * (n + 1)].bitcast(F32).rearrange("p (c u) -> p c u", u=2),
+                        turned[m][:].rearrange("p u c -> p c u"),
+                    )
+            for group in groups:
+                h_codes[group] = held.tile([P, P * len(group)], U32, name=f"h_codes{group[0]}", align_bytes=64)
+                h_scales[group] = held.tile([P, P * len(group)], U8, name=f"h_scales{group[0]}", align_bytes=64)
                 nc.vector.quantize_mx(
-                    out=h_codes[m][:].bitcast(E4M3), scales=h_scales[m][:], in_=h_in[m][:].rearrange("p c d -> p (c d)")
+                    out=h_codes[group][:].bitcast(E4M3), scales=h_scales[group][:], in_=h_in[group][:]
                 )
 
-        def second_product(tiles):
-            for m in tiles:
-                e = TILE_EXPERT[m]
-                y[m] = psum.tile([P, 2, P], F32, name=f"y{m}", tag=Y_BANK[m])
+        def second_product(groups):
+            for group in groups:
+                e = TILE_EXPERT[group[0]]
+                y[group] = psum.tile([P, 2, P * len(group)], F32, name=f"y{group[0]}", tag=Y_BANK[group[0]])
                 for t in range(2):
                     nc.tensor.matmul_mx(
-                        out=y[m][:, t, :],
+                        out=y[group][:, t, :],
                         lhsT=w2_codes[:, e, 2 * P * t : 2 * P * (t + 1)].bitcast(E2M1),
                         lhsT_scale=w2_plane[:, e, P * t : P * (t + 1)],
-                        rhs=h_codes[m][:].bitcast(E4M3),
-                        rhs_scale=h_scales[m][:],
+                        rhs=h_codes[group][:].bitcast(E4M3),
+                        rhs_scale=h_scales[group][:],
                         start=True,
                         stop=True,
                     )
-            for m in tiles:
-                a = max(a for a, b in BACK_CUTS if a <= P * m)
-                nc.scalar.copy(y_slots[a][:, :, P * m - a : P * (m + 1) - a], y[m][:])
+            for group in groups:
+                nc.scalar.copy(y_slots[P * group[0]][:], y[group][:])
 
         y_tokens = {}
 
@@ -245,17 +248,17 @@ def tile_moe_rag_glu_relu_kernel(
             )
 
         hidden((2, 3, 1))
-        hidden_codes((2, 3, 1))
-        second_product((2, 3))
+        hidden_codes(((2, 3), (1,)))
+        second_product(((2, 3),))
         y_tokens[0] = held.tile([P, T], F32, name="y_tokens0")
         scatter(0, 256, 512)
-        for s in range(PASSES):
-            multiply(s, 0)
+        for s in LAST_FIRST:
+            multiply(s, 0, LAST_FIRST)
         hidden((0,))
         y_tokens[1] = held.tile([P, T], F32, name="y_tokens1", tag="a_pos0")
         scatter(1, 256, 512)
-        hidden_codes((0,))
-        second_product((1, 0))
+        hidden_codes(((0,),))
+        second_product(((1,), (0,)))
         for t, (a, b) in ((0, BACK_CUTS[1]), (1, BACK_CUTS[1]), (0, BACK_CUTS[2]), (1, BACK_CUTS[2])):
             scatter(t, a, b)
         for t in range(2):

@@ -26,14 +26,11 @@ PASSES = 5
 TILES = 4
 TILE_EXPERT = (0, 1, 1, 1)
 CAST_CUTS = (((0, 128, 256), (256, 320, 384), (384, 448, 512)),) + (((0, 384, 512),),) + (((0, 512, 512),),) * 3
-LIST_CUTS = ((0, 512),)
 SPARE = 192
-PACKED = 1
-LAST_CUTS = ((256, 384), (384, 512), (0, 256))
-LAST_FIRST = (4, 0, 1, 2, 3)
-TILE_ORDER = (2, 3, 1, 0)
-BACK_CUTS = ((256, 512), (128, 256), (0, 128))
-Y_BANK = {2: "bank1_2", 1: "bank0_0", 0: "bank1_0"}
+TILE_ORDER = (2, 3, 1)
+TURN_BANK = {2: "spare", 3: "bank0_3", 1: "bank0_1", 0: "spare"}
+Y_BANK = {2: "bank1_2", 3: "bank1_3", 1: "bank0_1", 0: "bank0_3"}
+LATE = 3
 
 
 def interleave(ap_in, ap_out):
@@ -49,25 +46,26 @@ def tile_moe_rag_glu_relu_kernel(
     nc = tc.nc
     with ExitStack() as ctx:
         held = ctx.enter_context(tc.tile_pool(name="held", bufs=1))
-        ring = ctx.enter_context(tc.tile_pool(name="ring", bufs=2))
         psum = ctx.enter_context(tc.psum_pool(name="psum", bufs=1))
 
         offsets = held.tile([P, T // 16], U16, name="offsets")
         x_raw = {}
         tok_codes = held.tile([P, PASSES * T + SPARE], U32, name="tok_codes", align_bytes=64)
         tok_scales = held.tile([P, PASSES * T + SPARE], U8, name="tok_scales", align_bytes=64)
-        slot_codes = [held.tile([P, T], U32, name=f"slot_codes{s}", align_bytes=64) for s in range(PASSES)]
-        slot_scales = [held.tile([P, T], U8, name=f"slot_scales{s}", align_bytes=64) for s in range(PASSES)]
+        slot_codes, slot_scales = {}, {}
         words = {}
+        w1_planes = held.tile([P, E, PASSES, H], U8, name="w1_planes", align_bytes=64)
         planes = [
-            [held.tile([P, PASSES, H], U8, name=f"planes{e}_{w}", align_bytes=64) for w in range(2)] for e in range(E)
+            [w1_planes[:, e], held.tile([P, PASSES, H], U8, name=f"w3_planes{e}", align_bytes=64)] for e in range(E)
         ]
         w2_codes = held.tile([P, E, 2 * N], U8, name="w2_codes", align_bytes=64)
         w2_plane = held.tile([P, E, N], U8, name="w2_plane", align_bytes=64)
         gates = held.tile([P, T], F32, name="gates")
         identity = held.tile([P, P], F32, name="identity")
-        y_slots = {a: held.tile([P, 2, b - a], F32, name=f"y_slots{a}") for a, b in BACK_CUTS}
-        banks = [[psum.tile([P, H], F32, name=f"bank{w}_{m}", tag=f"bank{w}_{m}") for w in range(2)] for m in range(TILES)]
+        y_slots = {}
+        banks = {
+            (m, w): psum.tile([P, H], F32, name=f"bank{w}_{m}", tag=f"bank{w}_{m}") for w in range(2) for m in TILE_ORDER
+        }
 
         w_dram = (w1_words, w3_words)
 
@@ -103,41 +101,39 @@ def tile_moe_rag_glu_relu_kernel(
         load_x(0, slice(384, 512))
         nc.sync.dma_start(offsets[:], offs)
         load_x(1)
-        load_scales(1, 0)
-        load_x(2)
-        load_scales(1, 1)
         load_w(1, 0, 1)
+        load_x(2)
+        w1_rows = w1_scales.rearrange("e s (q r) i -> r q (e s) i", r=4)
+        for r in range(4):
+            nc.sync.dma_start(
+                out=w1_planes[r:P:32].rearrange("p e s i -> p (e s) i").bitcast(I32), in_=w1_rows[r].bitcast(I32)
+            )
         load_x(3)
+        load_scales(1, 1)
         load_w(1, 1, 3)
         load_x(4)
         load_w(1, 3, 5)
-        load_scales(0, 0)
-        load_w(0, 0, 5, (0,))
-        nc.sync.dma_start(
-            out=w2_codes[:].bitcast(I32), in_=w2_words[:, 0].rearrange("e p b -> p e b").bitcast(I32)
-        )
+        load_w(0, 0, 3, (0,))
         by_row = w2_scales.rearrange("e s (q r) i -> r q (e s) i", r=4)
         for r in range(4):
             nc.sync.dma_start(out=w2_plane[r:P:32].bitcast(I32), in_=by_row[r].bitcast(I32))
+        nc.sync.dma_start(
+            out=w2_codes[:].bitcast(I32), in_=w2_words[:, 0].rearrange("e p b -> p e b").bitcast(I32)
+        )
+        load_w(0, 3, 5, (0,))
         nc.sync.dma_start(out=gates[:], in_=gate[0:P, :])
         load_scales(0, 1)
         load_w(0, 0, 5, (1,))
 
         nc.vector.memset(tok_scales[:].bitcast(I32), 0)
         nc.vector.memset(tok_codes[:, PASSES * T :].bitcast(I32), 0)
-        for s in range(1, PACKED):
-            nc.vector.memset(slot_scales[s][:].bitcast(I32), 0)
         make_identity(nc, identity[:])
 
-        def code_col(s):
+        def first_col(s):
             return (PASSES - 1 - s) * T
 
-        def scale_col(s):
-            return (PASSES - 1 - max(s, PACKED - 1)) * T
-
         def tokens(s):
-            x_bf = ring.tile([P, T, 4], BF16, name="x_bf", align_bytes=64)
-            row = 4 * s if s < PACKED else 0
+            x_bf = held.tile([P, T, 4], BF16, name="x_bf", tag=f"x_bf{s % 2}", align_bytes=64)
             for a, cut, b in CAST_CUTS[s]:
                 if a < cut:
                     dst, src = interleave(x_raw[s][:, :, a:cut], x_bf[:, a:cut, :])
@@ -146,120 +142,161 @@ def tile_moe_rag_glu_relu_kernel(
                     dst, src = interleave(x_raw[s][:, :, cut:b], x_bf[:, cut:b, :])
                     nc.vector.tensor_copy(dst, src)
                 nc.vector.quantize_mx(
-                    out=tok_codes[:, code_col(s) + a : code_col(s) + b].bitcast(E4M3),
-                    scales=tok_scales[row:P, scale_col(s) + a : scale_col(s) + b],
+                    out=tok_codes[:, first_col(s) + a : first_col(s) + b].bitcast(E4M3),
+                    scales=tok_scales[:, first_col(s) + a : first_col(s) + b],
                     in_=x_bf[:, a:b, :].rearrange("p w j -> p (w j)"),
                 )
 
-        def gather(s, cuts):
-            for a, b in cuts:
-                picked = offsets[:, a // 16 : b // 16]
-                if s >= PACKED - 1:
-                    window = tok_scales[:, scale_col(s) : scale_col(s) + T + SPARE]
-                    nc.vector.tensor_copy(slot_scales[s if s >= PACKED else 0][:, a:b], window.indirect(picked))
-                window = tok_codes[:, code_col(s) : code_col(s) + T + SPARE]
-                nc.vector.tensor_copy(slot_codes[s][:, a:b], window.indirect(picked))
-            if s == PACKED - 1:
-                for a in range(1, PACKED):
-                    nc.gpsimd.dma_start(
-                        out=slot_scales[a][0:100, :].bitcast(I32),
-                        in_=slot_scales[0][4 * a : 4 * a + 100, :].bitcast(I32),
-                    )
+        def gather(s, picked, codes, scales):
+            cols = slice(first_col(s), first_col(s) + T + SPARE)
+            nc.vector.tensor_copy(scales, tok_scales[:, cols].indirect(picked))
+            nc.vector.tensor_copy(codes, tok_codes[:, cols].indirect(picked))
 
-        def multiply(s, m, order=range(PASSES)):
+        def gather_pass(s, first):
+            codes = held.tile([P, T - P * first], U32, name=f"slot_codes{s}", align_bytes=64)
+            scales = held.tile([P, T - P * first], U8, name=f"slot_scales{s}", align_bytes=64)
+            gather(s, offsets[:, 8 * first :], codes[:], scales[:])
+            for m in range(first, TILES):
+                slot_codes[s, m] = codes[:, P * (m - first) : P * (m - first + 1)]
+                slot_scales[s, m] = scales[:, P * (m - first) : P * (m - first + 1)]
+
+        def gather_late(table, found, passes, pool, tag):
+            late = pool.tile([P, len(passes), P], table.dtype, name=f"late_{tag}", tag=tag, align_bytes=64)
+            for n, s in enumerate(passes):
+                cols = slice(first_col(s), first_col(s) + T + SPARE)
+                nc.vector.tensor_copy(late[:, n, :], table[:, cols].indirect(offsets[:, 0:8]))
+                found[s, 0] = late[:, n, :]
+
+        def gather_tile(m):
+            s = PASSES - 1
+            codes = held.tile([P, P], U32, name=f"last_codes{m}", align_bytes=64)
+            scales = held.tile([P, P], U8, name=f"last_scales{m}", align_bytes=64)
+            gather(s, offsets[:, 8 * m : 8 * (m + 1)], codes[:], scales[:])
+            slot_codes[s, m] = codes[:]
+            slot_scales[s, m] = scales[:]
+
+        def multiply(s, m, w):
             e = TILE_EXPERT[m]
-            cols = slice(P * m, P * (m + 1))
-            for w in range(2):
-                nc.tensor.matmul_mx(
-                    out=banks[m][w][:],
-                    lhsT=slot_codes[s][:, cols].bitcast(E4M3),
-                    lhsT_scale=slot_scales[s][:, cols],
-                    rhs=words[e, w, s].bitcast(E2M1),
-                    rhs_scale=planes[e][w][:, s, :],
-                    start=(s == order[0]),
-                    stop=(s == order[-1]),
-                )
+            nc.tensor.matmul_mx(
+                out=banks[m, w][:],
+                lhsT=slot_codes[s, m].bitcast(E4M3),
+                lhsT_scale=slot_scales[s, m],
+                rhs=words[e, w, s].bitcast(E2M1),
+                rhs_scale=planes[e][w][:, s, :],
+                start=(s == 0),
+                stop=(s == PASSES - 1),
+            )
 
-        for s in range(PASSES):
+        for s in range(PASSES - 1):
             tokens(s)
-            gather(s, LIST_CUTS if s < PASSES - 1 else LAST_CUTS)
+            gather_pass(s, int(s >= LATE))
+        tokens(PASSES - 1)
+        for m in TILE_ORDER:
+            gather_tile(m)
+        gather_late(tok_scales[:], slot_scales, range(LATE, PASSES), held, "x_bf0")
         for s in range(PASSES):
-            for m in TILE_ORDER[:-1]:
-                multiply(s, m)
+            for m in TILE_ORDER:
+                for w in range(2):
+                    multiply(s, m, w)
 
         h, h_in, turned, h_codes, h_scales, y, a_pos = {}, {}, {}, {}, {}, {}, {}
 
-        def hidden(tiles):
-            for m in tiles:
-                a_pos[m] = held.tile([P, H], F32, name=f"a_pos{m}", tag=f"a_pos{m}")
-                nc.scalar.activation(a_pos[m][:], banks[m][0][:], RELU)
-            for m in tiles:
-                h[m] = held.tile([P, 2, P, 2], BF16, name=f"h{m}", align_bytes=64)
-                nc.vector.tensor_tensor(
-                    h[m][:],
-                    banks[m][1][:].rearrange("p (q u v) -> p u q v", u=2, v=2),
-                    a_pos[m][:].rearrange("p (q u v) -> p u q v", u=2, v=2),
-                    MULT,
+        def relu(m):
+            a_pos[m] = held.tile([P, H], F32, name=f"a_pos{m}", tag=f"a_pos{m}", align_bytes=64)
+            nc.scalar.activation(a_pos[m][:], banks[m, 0][:], RELU)
+
+        def gated(m):
+            h[m] = held.tile([P, 2, P, 2], BF16, name=f"h{m}", tag=f"h{m}", align_bytes=64)
+            nc.vector.tensor_tensor(
+                h[m][:],
+                banks[m, 1][:].rearrange("p (q u v) -> p u q v", u=2, v=2),
+                a_pos[m][:].rearrange("p (q u v) -> p u q v", u=2, v=2),
+                MULT,
+            )
+
+        def turn(m):
+            turned[m] = psum.tile([P, 2, P], F32, name=f"turned{m}", tag=TURN_BANK[m])
+            pairs = h[m][:].rearrange("p u q v -> p (u q v)").bitcast(F32)
+            for u in range(2):
+                nc.tensor.transpose(turned[m][:, u, :], pairs[:, P * u : P * (u + 1)], identity[:])
+            h_in[m] = held.tile([P, 4 * P], BF16, name=f"h_in{m}", tag=f"h_in{m}", align_bytes=64)
+            nc.scalar.copy(
+                h_in[m][:].bitcast(F32).rearrange("p (c u) -> p c u", u=2),
+                turned[m][:].rearrange("p u c -> p c u"),
+            )
+
+        def hidden_codes(m):
+            h_codes[m] = held.tile([P, P], U32, name=f"h_codes{m}", align_bytes=64)
+            h_scales[m] = held.tile([P, P], U8, name=f"h_scales{m}", align_bytes=64)
+            nc.vector.quantize_mx(out=h_codes[m][:].bitcast(E4M3), scales=h_scales[m][:], in_=h_in[m][:])
+
+        def second_product(m):
+            e = TILE_EXPERT[m]
+            y[m] = psum.tile([P, 2, P], F32, name=f"y{m}", tag=Y_BANK[m])
+            for t in range(2):
+                nc.tensor.matmul_mx(
+                    out=y[m][:, t, :],
+                    lhsT=w2_codes[:, e, 2 * P * t : 2 * P * (t + 1)].bitcast(E2M1),
+                    lhsT_scale=w2_plane[:, e, P * t : P * (t + 1)],
+                    rhs=h_codes[m][:].bitcast(E4M3),
+                    rhs_scale=h_scales[m][:],
+                    start=True,
+                    stop=True,
                 )
 
-        def hidden_codes(groups):
-            for group in groups:
-                for m in group:
-                    turned[m] = psum.tile([P, 2, P], F32, name=f"turned{m}", tag=f"bank0_{m}")
-                    pairs = h[m][:].rearrange("p u q v -> p (u q v)").bitcast(F32)
-                    for u in range(2):
-                        nc.tensor.transpose(turned[m][:, u, :], pairs[:, P * u : P * (u + 1)], identity[:])
-            for group in groups:
-                h_in[group] = held.tile([P, P * len(group) * 4], BF16, name=f"h_in{group[0]}", align_bytes=64)
-                for n, m in enumerate(group):
-                    nc.scalar.copy(
-                        h_in[group][:, 4 * P * n : 4 * P * (n + 1)].bitcast(F32).rearrange("p (c u) -> p c u", u=2),
-                        turned[m][:].rearrange("p u c -> p c u"),
-                    )
-            for group in groups:
-                h_codes[group] = held.tile([P, P * len(group)], U32, name=f"h_codes{group[0]}", align_bytes=64)
-                h_scales[group] = held.tile([P, P * len(group)], U8, name=f"h_scales{group[0]}", align_bytes=64)
-                nc.vector.quantize_mx(
-                    out=h_codes[group][:].bitcast(E4M3), scales=h_scales[group][:], in_=h_in[group][:]
-                )
-
-        def second_product(groups):
-            for group in groups:
-                e = TILE_EXPERT[group[0]]
-                y[group] = psum.tile([P, 2, P * len(group)], F32, name=f"y{group[0]}", tag=Y_BANK[group[0]])
-                for t in range(2):
-                    nc.tensor.matmul_mx(
-                        out=y[group][:, t, :],
-                        lhsT=w2_codes[:, e, 2 * P * t : 2 * P * (t + 1)].bitcast(E2M1),
-                        lhsT_scale=w2_plane[:, e, P * t : P * (t + 1)],
-                        rhs=h_codes[group][:].bitcast(E4M3),
-                        rhs_scale=h_scales[group][:],
-                        start=True,
-                        stop=True,
-                    )
-            for group in groups:
-                nc.scalar.copy(y_slots[P * group[0]][:], y[group][:])
+        def unload(m, tag=None):
+            both = held.tile([P, 2, P], F32, name=f"y_slots{m}", tag=tag or f"y_slots{m}", align_bytes=64)
+            nc.scalar.copy(both[:], y[m][:])
+            for t in range(2):
+                y_slots[m, t] = both[:, t, :]
 
         y_tokens = {}
 
-        def scatter(t, a, b):
+        def scatter(t, m):
             nc.vector.tensor_tensor(
-                y_tokens[t][:].indirect(offsets[:, a // 16 : b // 16]), y_slots[a][:, t, :], gates[:, a:b], MULT
+                y_tokens[t][:].indirect(offsets[:, 8 * m : 8 * (m + 1)]),
+                y_slots[m, t],
+                gates[:, P * m : P * (m + 1)],
+                MULT,
             )
 
-        hidden((2, 3, 1))
-        hidden_codes(((2, 3), (1,)))
-        second_product(((2, 3),))
+        for m in TILE_ORDER:
+            relu(m)
+        for m in TILE_ORDER:
+            gated(m)
+        banks[0, 0] = psum.tile([P, H], F32, name="bank0_0", tag="bank0_2")
+        for s in range(LATE):
+            multiply(s, 0, 0)
+        for m in TILE_ORDER:
+            turn(m)
+        for m in TILE_ORDER:
+            hidden_codes(m)
+        gather_late(tok_codes[:], slot_codes, range(LATE, PASSES), held, "a_pos2")
+        for s in range(LATE, PASSES):
+            multiply(s, 0, 0)
+        relu(0)
         y_tokens[0] = held.tile([P, T], F32, name="y_tokens0")
-        scatter(0, 256, 512)
-        for s in LAST_FIRST:
-            multiply(s, 0, LAST_FIRST)
-        hidden((0,))
-        y_tokens[1] = held.tile([P, T], F32, name="y_tokens1", tag="a_pos0")
-        scatter(1, 256, 512)
-        hidden_codes(((0,),))
-        second_product(((1,), (0,)))
-        for t, (a, b) in ((0, BACK_CUTS[1]), (1, BACK_CUTS[1]), (0, BACK_CUTS[2]), (1, BACK_CUTS[2])):
-            scatter(t, a, b)
+        for m in TILE_ORDER[:2]:
+            second_product(m)
+            unload(m)
+        banks[0, 1] = psum.tile([P, H], F32, name="bank1_0", tag="bank0_1")
+        for s in range(PASSES):
+            multiply(s, 0, 1)
+        gated(0)
+        for m in TILE_ORDER[:2]:
+            scatter(0, m)
+        y_tokens[1] = held.tile([P, T], F32, name="y_tokens1", tag="a_pos0", align_bytes=64)
+        turn(0)
+        hidden_codes(0)
+        for m in TILE_ORDER[:2]:
+            scatter(1, m)
+        second_product(1)
+        unload(1)
+        second_product(0)
+        unload(0)
+        scatter(0, 1)
+        scatter(1, 1)
+        scatter(0, 0)
+        scatter(1, 0)
         for t in range(2):
             nc.sync.dma_start(out=out[P * t : P * (t + 1), :], in_=y_tokens[t][:])

@@ -54,9 +54,8 @@ def tile_moe_rag_glu_relu_kernel(
         tok_scales = held.tile([P, PASSES * T + SPARE], U8, name="tok_scales", align_bytes=64)
         slot_codes, slot_scales = {}, {}
         words = {}
-        w1_planes = held.tile([P, E, PASSES, H], U8, name="w1_planes", align_bytes=64)
         planes = [
-            [w1_planes[:, e], held.tile([P, PASSES, H], U8, name=f"w3_planes{e}", align_bytes=64)] for e in range(E)
+            [held.tile([P, PASSES, H], U8, name=f"planes{e}_{w}", align_bytes=64) for w in range(2)] for e in range(E)
         ]
         w2_codes = held.tile([P, E, 2 * N], U8, name="w2_codes", align_bytes=64)
         w2_plane = held.tile([P, E, N], U8, name="w2_plane", align_bytes=64)
@@ -101,26 +100,22 @@ def tile_moe_rag_glu_relu_kernel(
         load_x(0, slice(384, 512))
         nc.sync.dma_start(offsets[:], offs)
         load_x(1)
-        load_w(1, 0, 1)
         load_x(2)
-        w1_rows = w1_scales.rearrange("e s (q r) i -> r q (e s) i", r=4)
-        for r in range(4):
-            nc.sync.dma_start(
-                out=w1_planes[r:P:32].rearrange("p e s i -> p (e s) i").bitcast(I32), in_=w1_rows[r].bitcast(I32)
-            )
-        load_x(3)
+        load_w(1, 0, 1)
+        load_scales(1, 0)
         load_scales(1, 1)
+        load_x(3)
         load_w(1, 1, 3)
         load_x(4)
         load_w(1, 3, 5)
-        load_w(0, 0, 3, (0,))
-        by_row = w2_scales.rearrange("e s (q r) i -> r q (e s) i", r=4)
-        for r in range(4):
-            nc.sync.dma_start(out=w2_plane[r:P:32].bitcast(I32), in_=by_row[r].bitcast(I32))
+        load_scales(0, 0)
+        load_w(0, 0, 5, (0,))
         nc.sync.dma_start(
             out=w2_codes[:].bitcast(I32), in_=w2_words[:, 0].rearrange("e p b -> p e b").bitcast(I32)
         )
-        load_w(0, 3, 5, (0,))
+        by_row = w2_scales.rearrange("e s (q r) i -> r q (e s) i", r=4)
+        for r in range(4):
+            nc.sync.dma_start(out=w2_plane[r:P:32].bitcast(I32), in_=by_row[r].bitcast(I32))
         nc.sync.dma_start(out=gates[:], in_=gate[0:P, :])
         load_scales(0, 1)
         load_w(0, 0, 5, (1,))
@@ -202,7 +197,7 @@ def tile_moe_rag_glu_relu_kernel(
         h, h_in, turned, h_codes, h_scales, y, a_pos = {}, {}, {}, {}, {}, {}, {}
 
         def relu(m):
-            a_pos[m] = held.tile([P, H], F32, name=f"a_pos{m}", tag=f"a_pos{m}", align_bytes=64)
+            a_pos[m] = held.tile([P, H], F32, name=f"a_pos{m}", tag=f"slot{m}", align_bytes=64)
             nc.scalar.activation(a_pos[m][:], banks[m, 0][:], RELU)
 
         def gated(m):
@@ -226,7 +221,7 @@ def tile_moe_rag_glu_relu_kernel(
             )
 
         def hidden_codes(m):
-            h_codes[m] = held.tile([P, P], U32, name=f"h_codes{m}", align_bytes=64)
+            h_codes[m] = held.tile([P, P], U32, name=f"h_codes{m}", tag="slot0" if m == 2 else f"h_codes{m}", align_bytes=64)
             h_scales[m] = held.tile([P, P], U8, name=f"h_scales{m}", align_bytes=64)
             nc.vector.quantize_mx(out=h_codes[m][:].bitcast(E4M3), scales=h_scales[m][:], in_=h_in[m][:])
 
@@ -271,21 +266,21 @@ def tile_moe_rag_glu_relu_kernel(
             turn(m)
         for m in TILE_ORDER:
             hidden_codes(m)
-        gather_late(tok_codes[:], slot_codes, range(LATE, PASSES), held, "a_pos2")
+        gather_late(tok_codes[:], slot_codes, range(LATE, PASSES), held, "h_in2")
         for s in range(LATE, PASSES):
             multiply(s, 0, 0)
-        relu(0)
         y_tokens[0] = held.tile([P, T], F32, name="y_tokens0")
         for m in TILE_ORDER[:2]:
             second_product(m)
             unload(m)
+        relu(0)
         banks[0, 1] = psum.tile([P, H], F32, name="bank1_0", tag="bank0_1")
         for s in range(PASSES):
             multiply(s, 0, 1)
         gated(0)
         for m in TILE_ORDER[:2]:
             scatter(0, m)
-        y_tokens[1] = held.tile([P, T], F32, name="y_tokens1", tag="a_pos0", align_bytes=64)
+        y_tokens[1] = held.tile([P, T], F32, name="y_tokens1", tag="slot0", align_bytes=64)
         turn(0)
         hidden_codes(0)
         for m in TILE_ORDER[:2]:

@@ -25,7 +25,7 @@ N = 256
 PASSES = 5
 TILES = 4
 TILE_EXPERT = (0, 1, 1, 1)
-CAST_CUTS = (((0, 128, 256), (256, 320, 384), (384, 448, 512)),) + (((0, 384, 512),),) + (((0, 512, 512),),) * 3
+CAST_CUTS = (((0, 128, 256), (256, 384, 512)),) + tuple(((0, c, 512),) for c in (384,512,512,192))
 SPARE = 192
 TILE_ORDER = (2, 3, 1)
 TURN_BANK = {2: "spare", 3: "bank0_3", 1: "bank0_1", 0: "spare"}
@@ -96,15 +96,14 @@ def tile_moe_rag_glu_relu_kernel(
             nc.gpsimd.memset(planes[0][w][:].bitcast(I32), 0)
         nc.gpsimd.memset(w2_plane[:].bitcast(I32), 0)
         load_x(0, slice(0, 256))
-        load_x(0, slice(256, 384))
-        load_x(0, slice(384, 512))
+        load_x(0, slice(256, 512))
         nc.sync.dma_start(offsets[:], offs)
         load_x(1)
         load_x(2)
+        load_x(3)
         load_w(1, 0, 1)
         load_scales(1, 0)
         load_scales(1, 1)
-        load_x(3)
         load_w(1, 1, 3)
         load_x(4)
         load_w(1, 3, 5)
@@ -197,7 +196,7 @@ def tile_moe_rag_glu_relu_kernel(
         h, h_in, turned, h_codes, h_scales, y, a_pos = {}, {}, {}, {}, {}, {}, {}
 
         def relu(m):
-            a_pos[m] = held.tile([P, H], F32, name=f"a_pos{m}", tag=f"slot{m}", align_bytes=64)
+            a_pos[m] = held.tile([P, H], F32, name=f"a_pos{m}", tag="slot0" if m == 0 else f"a_pos{m}", align_bytes=64)
             nc.scalar.activation(a_pos[m][:], banks[m, 0][:], RELU)
 
         def gated(m):
@@ -266,7 +265,7 @@ def tile_moe_rag_glu_relu_kernel(
             turn(m)
         for m in TILE_ORDER:
             hidden_codes(m)
-        gather_late(tok_codes[:], slot_codes, range(LATE, PASSES), held, "h_in2")
+        gather_late(tok_codes[:], slot_codes, range(LATE, PASSES), held, "a_pos2")
         for s in range(LATE, PASSES):
             multiply(s, 0, 0)
         y_tokens[0] = held.tile([P, T], F32, name="y_tokens0")

@@ -52,7 +52,7 @@ def tile_moe_rag_glu_relu_kernel(
         x_raw = {}
         tok_codes = held.tile([P, PASSES * T + SPARE], U32, name="tok_codes", align_bytes=64)
         tok_scales = held.tile([P, PASSES * T + SPARE], U8, name="tok_scales", align_bytes=64)
-        slot_codes, slot_scales = {}, {}
+        slot_codes, slot_scales, pass_scales = {}, {}, {}
         words = {}
         planes = [
             [held.tile([P, PASSES, H], U8, name=f"planes{e}_{w}", align_bytes=64) for w in range(2)] for e in range(E)
@@ -78,7 +78,8 @@ def tile_moe_rag_glu_relu_kernel(
 
         def load_w(e, first, last, matrices=(0, 1)):
             for w in matrices:
-                part = held.tile([P, last - first, 2 * H], U8, name=f"words{e}_{w}_{first}", align_bytes=64)
+                name = f"words{e}_{w}_{first}"
+                part = held.tile([P, last - first, 2 * H], U8, name=name, tag=name, align_bytes=64)
                 nc.sync.dma_start(
                     out=part[:].bitcast(I32),
                     in_=w_dram[w][e, first:last].rearrange("s p b -> p s b").bitcast(I32),
@@ -100,8 +101,8 @@ def tile_moe_rag_glu_relu_kernel(
         nc.sync.dma_start(offsets[:], offs)
         load_x(1)
         load_x(2)
-        load_x(3)
         load_w(1, 0, 1)
+        load_x(3)
         load_scales(1, 0)
         load_scales(1, 1)
         load_w(1, 1, 3)
@@ -150,6 +151,7 @@ def tile_moe_rag_glu_relu_kernel(
             codes = held.tile([P, T - P * first], U32, name=f"slot_codes{s}", align_bytes=64)
             scales = held.tile([P, T - P * first], U8, name=f"slot_scales{s}", align_bytes=64)
             gather(s, offsets[:, 8 * first :], codes[:], scales[:])
+            pass_scales[s] = scales[:]
             for m in range(first, TILES):
                 slot_codes[s, m] = codes[:, P * (m - first) : P * (m - first + 1)]
                 slot_scales[s, m] = scales[:, P * (m - first) : P * (m - first + 1)]
@@ -188,6 +190,17 @@ def tile_moe_rag_glu_relu_kernel(
         for m in TILE_ORDER:
             gather_tile(m)
         gather_late(tok_scales[:], slot_scales, range(LATE, PASSES), held, "x_bf0")
+        warm = psum.tile([P, H], F32, name="warm", tag="spare")
+        for n in range(3):
+            nc.tensor.matmul_mx(
+                out=warm[:],
+                lhsT=slot_codes[0, n].bitcast(E4M3),
+                lhsT_scale=slot_scales[0, n],
+                rhs=words[1, 0, 0].bitcast(E2M1),
+                rhs_scale=pass_scales[1],
+                start=True,
+                stop=True,
+            )
         for s in range(PASSES):
             for m in TILE_ORDER:
                 for w in range(2):
@@ -271,12 +284,13 @@ def tile_moe_rag_glu_relu_kernel(
         y_tokens[0] = held.tile([P, T], F32, name="y_tokens0")
         for m in TILE_ORDER[:2]:
             second_product(m)
-            unload(m)
+        unload(2)
         relu(0)
         banks[0, 1] = psum.tile([P, H], F32, name="bank1_0", tag="bank0_1")
         for s in range(PASSES):
             multiply(s, 0, 1)
         gated(0)
+        unload(3, "words0_1_0")
         for m in TILE_ORDER[:2]:
             scatter(0, m)
         y_tokens[1] = held.tile([P, T], F32, name="y_tokens1", tag="slot0", align_bytes=64)

@@ -25,7 +25,7 @@ N = 256
 PASSES = 5
 TILES = 4
 TILE_EXPERT = (0, 1, 1, 1)
-CAST_CUTS = (((0, 128, 256), (256, 384, 512)),) + tuple(((0, c, 512),) for c in (384,512,512,192))
+CAST_CUTS = (((0, 96, 256), (256, 352, 512)),) + tuple(((0, c, 512),) for c in (320, 512, 512, 256))
 SPARE = 192
 TILE_ORDER = (2, 3, 1)
 TURN_BANK = {2: "spare", 3: "bank0_3", 1: "bank0_1", 0: "spare"}
@@ -92,6 +92,8 @@ def tile_moe_rag_glu_relu_kernel(
             for r in range(4):
                 nc.sync.dma_start(out=planes[e][w][r:P:32].bitcast(I32), in_=by_row[r].bitcast(I32))
 
+        gate_rows = held.tile([P, P], F32, name="gate_rows")
+        nc.gpsimd.memset(gate_rows[:], 0.0)
         for w in range(2):
             nc.vector.memset(planes[1][w][:].bitcast(I32), 0)
             nc.gpsimd.memset(planes[0][w][:].bitcast(I32), 0)
@@ -100,6 +102,7 @@ def tile_moe_rag_glu_relu_kernel(
         load_x(0, slice(256, 512))
         nc.sync.dma_start(offsets[:], offs)
         load_x(1)
+        nc.sync.dma_start(out=gate_rows[0:TILES, :], in_=gate[0].rearrange("(m j) -> m j", j=P))
         load_x(2)
         load_w(1, 0, 1)
         load_x(3)
@@ -116,13 +119,22 @@ def tile_moe_rag_glu_relu_kernel(
         by_row = w2_scales.rearrange("e s (q r) i -> r q (e s) i", r=4)
         for r in range(4):
             nc.sync.dma_start(out=w2_plane[r:P:32].bitcast(I32), in_=by_row[r].bitcast(I32))
-        nc.sync.dma_start(out=gates[:], in_=gate[0:P, :])
         load_scales(0, 1)
-        load_w(0, 0, 5, (1,))
+        load_w(0, 0, 3, (1,))
+        load_w(0, 3, 5, (1,))
 
         nc.vector.memset(tok_scales[:].bitcast(I32), 0)
         nc.vector.memset(tok_codes[:, PASSES * T :].bitcast(I32), 0)
         make_identity(nc, identity[:])
+
+        by_slot = psum.tile([P, P], F32, name="by_slot", tag="spare")
+        nc.tensor.transpose(by_slot[:], gate_rows[:], identity[:])
+        gate_cols = held.tile([P, TILES], F32, name="gate_cols")
+        nc.scalar.copy(gate_cols[:], by_slot[:, 0:TILES])
+        spread = psum.tile([P, TILES, P], F32, name="spread", tag="spread")
+        for m in range(TILES):
+            nc.tensor.transpose(spread[:, m, :], gate_cols[:, m : m + 1].to_broadcast([P, P]), identity[:])
+        nc.scalar.copy(gates[:], spread[:].rearrange("p m j -> p (m j)"))
 
         def first_col(s):
             return (PASSES - 1 - s) * T
@@ -190,17 +202,21 @@ def tile_moe_rag_glu_relu_kernel(
         for m in TILE_ORDER:
             gather_tile(m)
         gather_late(tok_scales[:], slot_scales, range(LATE, PASSES), held, "x_bf0")
-        warm = psum.tile([P, H], F32, name="warm", tag="spare")
-        for n in range(3):
-            nc.tensor.matmul_mx(
-                out=warm[:],
-                lhsT=slot_codes[0, n].bitcast(E4M3),
-                lhsT_scale=slot_scales[0, n],
-                rhs=words[1, 0, 0].bitcast(E2M1),
-                rhs_scale=pass_scales[1],
-                start=True,
-                stop=True,
-            )
+
+        def keep_warm(count, tag):
+            warm = psum.tile([P, H], F32, name="warm", tag=tag)
+            for n in range(count):
+                nc.tensor.matmul_mx(
+                    out=warm[:],
+                    lhsT=slot_codes[0, n % TILES].bitcast(E4M3),
+                    lhsT_scale=slot_scales[0, n % TILES],
+                    rhs=words[1, 0, 0].bitcast(E2M1),
+                    rhs_scale=pass_scales[1],
+                    start=True,
+                    stop=True,
+                )
+
+        keep_warm(6, "spare")
         for s in range(PASSES):
             for m in TILE_ORDER:
                 for w in range(2):
@@ -257,7 +273,7 @@ def tile_moe_rag_glu_relu_kernel(
             for t in range(2):
                 y_slots[m, t] = both[:, t, :]
 
-        y_tokens = {}
+        y_tokens = [held.tile([P, T], F32, name=f"y_tokens{t}") for t in range(2)]
 
         def scatter(t, m):
             nc.vector.tensor_tensor(
@@ -276,12 +292,12 @@ def tile_moe_rag_glu_relu_kernel(
             multiply(s, 0, 0)
         for m in TILE_ORDER:
             turn(m)
+        keep_warm(1, "bank1_3")
         for m in TILE_ORDER:
             hidden_codes(m)
         gather_late(tok_codes[:], slot_codes, range(LATE, PASSES), held, "a_pos2")
         for s in range(LATE, PASSES):
             multiply(s, 0, 0)
-        y_tokens[0] = held.tile([P, T], F32, name="y_tokens0")
         for m in TILE_ORDER[:2]:
             second_product(m)
         unload(2)
@@ -290,14 +306,12 @@ def tile_moe_rag_glu_relu_kernel(
         for s in range(PASSES):
             multiply(s, 0, 1)
         gated(0)
-        unload(3, "words0_1_0")
-        for m in TILE_ORDER[:2]:
-            scatter(0, m)
-        y_tokens[1] = held.tile([P, T], F32, name="y_tokens1", tag="slot0", align_bytes=64)
+        unload(3, "words0_1_3")
         turn(0)
         hidden_codes(0)
         for m in TILE_ORDER[:2]:
-            scatter(1, m)
+            for t in range(2):
+                scatter(t, m)
         second_product(1)
         unload(1)
         second_product(0)

@@ -28,9 +28,11 @@ TILE_EXPERT = (0, 1, 1, 1)
 CAST_CUTS = (((0, 96, 256), (256, 352, 512)),) + tuple(((0, c, 512),) for c in (320, 512, 512, 256))
 SPARE = 192
 TILE_ORDER = (2, 3, 1)
-TURN_BANK = {2: "spare", 3: "bank0_3", 1: "bank0_1", 0: "spare"}
-Y_BANK = {2: "bank1_2", 3: "bank1_3", 1: "bank0_1", 0: "bank0_3"}
+TURN_BANK = {2: "spare", 3: "bank0_2", 1: "bank1_2", 0: "spare"}
+Y_BANK = {2: "bank1_1", 3: "bank1_3", 1: "bank0_1", 0: "bank0_2"}
+EARLY = 3
 LATE = 3
+WARM_UPS = 3
 
 
 def interleave(ap_in, ap_out):
@@ -46,20 +48,20 @@ def tile_moe_rag_glu_relu_kernel(
     nc = tc.nc
     with ExitStack() as ctx:
         held = ctx.enter_context(tc.tile_pool(name="held", bufs=1))
+        reused = ctx.enter_context(tc.tile_pool(name="reused", bufs=1))
         psum = ctx.enter_context(tc.psum_pool(name="psum", bufs=1))
 
         offsets = held.tile([P, T // 16], U16, name="offsets")
         x_raw = {}
         tok_codes = held.tile([P, PASSES * T + SPARE], U32, name="tok_codes", align_bytes=64)
         tok_scales = held.tile([P, PASSES * T + SPARE], U8, name="tok_scales", align_bytes=64)
-        slot_codes, slot_scales, pass_scales = {}, {}, {}
+        slot_codes, slot_scales, whole = {}, {}, {}
         words = {}
         planes = [
             [held.tile([P, PASSES, H], U8, name=f"planes{e}_{w}", align_bytes=64) for w in range(2)] for e in range(E)
         ]
         w2_codes = held.tile([P, E, 2 * N], U8, name="w2_codes", align_bytes=64)
         w2_plane = held.tile([P, E, N], U8, name="w2_plane", align_bytes=64)
-        gates = held.tile([P, T], F32, name="gates")
         identity = held.tile([P, P], F32, name="identity")
         y_slots = {}
         banks = {
@@ -70,7 +72,7 @@ def tile_moe_rag_glu_relu_kernel(
 
         def load_x(s, cols=slice(0, T)):
             if s not in x_raw:
-                x_raw[s] = held.tile([P, 4, T], F32, name=f"x_raw{s}")
+                x_raw[s] = held.tile([P, 4, T], F32, name=f"x_raw{s}", tag=f"x_raw{s}", align_bytes=64)
             nc.sync.dma_start(
                 out=x_raw[s][:, :, cols],
                 in_=xT[4 * P * s : 4 * P * (s + 1), cols].rearrange("(p j) w -> p j w", j=4),
@@ -94,10 +96,10 @@ def tile_moe_rag_glu_relu_kernel(
 
         gate_rows = held.tile([P, P], F32, name="gate_rows")
         nc.gpsimd.memset(gate_rows[:], 0.0)
+        nc.gpsimd.memset(w2_plane[:].bitcast(I32), 0)
         for w in range(2):
             nc.vector.memset(planes[1][w][:].bitcast(I32), 0)
             nc.gpsimd.memset(planes[0][w][:].bitcast(I32), 0)
-        nc.gpsimd.memset(w2_plane[:].bitcast(I32), 0)
         load_x(0, slice(0, 256))
         load_x(0, slice(256, 512))
         nc.sync.dma_start(offsets[:], offs)
@@ -108,17 +110,17 @@ def tile_moe_rag_glu_relu_kernel(
         load_x(3)
         load_scales(1, 0)
         load_scales(1, 1)
-        load_w(1, 1, 3)
+        load_w(1, 1, EARLY)
         load_x(4)
-        load_w(1, 3, 5)
-        load_scales(0, 0)
-        load_w(0, 0, 5, (0,))
+        load_w(1, EARLY, PASSES)
         nc.sync.dma_start(
             out=w2_codes[:].bitcast(I32), in_=w2_words[:, 0].rearrange("e p b -> p e b").bitcast(I32)
         )
         by_row = w2_scales.rearrange("e s (q r) i -> r q (e s) i", r=4)
         for r in range(4):
             nc.sync.dma_start(out=w2_plane[r:P:32].bitcast(I32), in_=by_row[r].bitcast(I32))
+        load_scales(0, 0)
+        load_w(0, 0, 5, (0,))
         load_scales(0, 1)
         load_w(0, 0, 3, (1,))
         load_w(0, 3, 5, (1,))
@@ -134,13 +136,15 @@ def tile_moe_rag_glu_relu_kernel(
         spread = psum.tile([P, TILES, P], F32, name="spread", tag="spread")
         for m in range(TILES):
             nc.tensor.transpose(spread[:, m, :], gate_cols[:, m : m + 1].to_broadcast([P, P]), identity[:])
-        nc.scalar.copy(gates[:], spread[:].rearrange("p m j -> p (m j)"))
 
         def first_col(s):
             return (PASSES - 1 - s) * T
 
         def tokens(s):
-            x_bf = held.tile([P, T, 4], BF16, name="x_bf", tag=f"x_bf{s % 2}", align_bytes=64)
+            if s == PASSES - 1:
+                x_bf = reused.tile([P, T, 4], BF16, name="x_bf_last", align_bytes=64, offset=0)
+            else:
+                x_bf = held.tile([P, T, 4], BF16, name="x_bf", tag=f"x_bf{s % 2}", align_bytes=64)
             for a, cut, b in CAST_CUTS[s]:
                 if a < cut:
                     dst, src = interleave(x_raw[s][:, :, a:cut], x_bf[:, a:cut, :])
@@ -154,36 +158,19 @@ def tile_moe_rag_glu_relu_kernel(
                     in_=x_bf[:, a:b, :].rearrange("p w j -> p (w j)"),
                 )
 
-        def gather(s, picked, codes, scales):
+        def gather(table, found, s, first, last, tag=None, offset=None):
+            name = f"slots{table.shape[1]}_{int(table.dtype == U8)}_{s}_{first}"
+            if offset is None:
+                picked = held.tile([P, P * (last - first)], table.dtype, name=name, tag=tag or name, align_bytes=64)
+            else:
+                picked = reused.tile([P, P * (last - first)], table.dtype, name=name, align_bytes=64, offset=offset)
             cols = slice(first_col(s), first_col(s) + T + SPARE)
-            nc.vector.tensor_copy(scales, tok_scales[:, cols].indirect(picked))
-            nc.vector.tensor_copy(codes, tok_codes[:, cols].indirect(picked))
+            nc.vector.tensor_copy(picked[:], table[:, cols].indirect(offsets[:, 8 * first : 8 * last]))
+            whole[s, table.dtype == U8] = picked[:]
+            for m in range(first, last):
+                found[s, m] = picked[:, P * (m - first) : P * (m - first + 1)]
 
-        def gather_pass(s, first):
-            codes = held.tile([P, T - P * first], U32, name=f"slot_codes{s}", align_bytes=64)
-            scales = held.tile([P, T - P * first], U8, name=f"slot_scales{s}", align_bytes=64)
-            gather(s, offsets[:, 8 * first :], codes[:], scales[:])
-            pass_scales[s] = scales[:]
-            for m in range(first, TILES):
-                slot_codes[s, m] = codes[:, P * (m - first) : P * (m - first + 1)]
-                slot_scales[s, m] = scales[:, P * (m - first) : P * (m - first + 1)]
-
-        def gather_late(table, found, passes, pool, tag):
-            late = pool.tile([P, len(passes), P], table.dtype, name=f"late_{tag}", tag=tag, align_bytes=64)
-            for n, s in enumerate(passes):
-                cols = slice(first_col(s), first_col(s) + T + SPARE)
-                nc.vector.tensor_copy(late[:, n, :], table[:, cols].indirect(offsets[:, 0:8]))
-                found[s, 0] = late[:, n, :]
-
-        def gather_tile(m):
-            s = PASSES - 1
-            codes = held.tile([P, P], U32, name=f"last_codes{m}", align_bytes=64)
-            scales = held.tile([P, P], U8, name=f"last_scales{m}", align_bytes=64)
-            gather(s, offsets[:, 8 * m : 8 * (m + 1)], codes[:], scales[:])
-            slot_codes[s, m] = codes[:]
-            slot_scales[s, m] = scales[:]
-
-        def multiply(s, m, w):
+        def multiply(s, m, w, order=tuple(range(PASSES))):
             e = TILE_EXPERT[m]
             nc.tensor.matmul_mx(
                 out=banks[m, w][:],
@@ -191,17 +178,29 @@ def tile_moe_rag_glu_relu_kernel(
                 lhsT_scale=slot_scales[s, m],
                 rhs=words[e, w, s].bitcast(E2M1),
                 rhs_scale=planes[e][w][:, s, :],
-                start=(s == 0),
-                stop=(s == PASSES - 1),
+                start=(s == order[0]),
+                stop=(s == order[-1]),
             )
 
-        for s in range(PASSES - 1):
+        tokens(0)
+        gather(tok_scales[:], slot_scales, 0, 0, TILES)
+        gather(tok_codes[:], slot_codes, 0, 0, TILES)
+        for s in range(1, LATE):
             tokens(s)
-            gather_pass(s, int(s >= LATE))
-        tokens(PASSES - 1)
-        for m in TILE_ORDER:
-            gather_tile(m)
-        gather_late(tok_scales[:], slot_scales, range(LATE, PASSES), held, "x_bf0")
+            gather(tok_scales[:], slot_scales, s, 0, TILES)
+            gather(tok_codes[:], slot_codes, s, 0, TILES)
+        tokens(LATE)
+        gather(tok_scales[:], slot_scales, LATE, 1, TILES)
+        gather(tok_codes[:], slot_codes, LATE, 1, TILES)
+        tokens(LATE + 1)
+        gates = reused.tile([P, T], F32, name="gates", align_bytes=64, offset=0)
+        nc.scalar.copy(gates[:], spread[:].rearrange("p m j -> p (m j)"))
+        for first, last in ((2, 3), (3, 4), (1, 2)):
+            gather(tok_scales[:], slot_scales, PASSES - 1, first, last)
+            gather(tok_codes[:], slot_codes, PASSES - 1, first, last)
+
+        for s in range(LATE, PASSES):
+            gather(tok_scales[:], slot_scales, s, 0, 1, offset=4 * T + P * s)
 
         def keep_warm(count, tag):
             warm = psum.tile([P, H], F32, name="warm", tag=tag)
@@ -211,12 +210,12 @@ def tile_moe_rag_glu_relu_kernel(
                     lhsT=slot_codes[0, n % TILES].bitcast(E4M3),
                     lhsT_scale=slot_scales[0, n % TILES],
                     rhs=words[1, 0, 0].bitcast(E2M1),
-                    rhs_scale=pass_scales[1],
+                    rhs_scale=whole[1, True],
                     start=True,
                     stop=True,
                 )
 
-        keep_warm(6, "spare")
+        keep_warm(WARM_UPS, "spare")
         for s in range(PASSES):
             for m in TILE_ORDER:
                 for w in range(2):
@@ -225,7 +224,7 @@ def tile_moe_rag_glu_relu_kernel(
         h, h_in, turned, h_codes, h_scales, y, a_pos = {}, {}, {}, {}, {}, {}, {}
 
         def relu(m):
-            a_pos[m] = held.tile([P, H], F32, name=f"a_pos{m}", tag="slot0" if m == 0 else f"a_pos{m}", align_bytes=64)
+            a_pos[m] = held.tile([P, H], F32, name=f"a_pos{m}", tag=f"a_pos{m}", align_bytes=64)
             nc.scalar.activation(a_pos[m][:], banks[m, 0][:], RELU)
 
         def gated(m):
@@ -249,7 +248,7 @@ def tile_moe_rag_glu_relu_kernel(
             )
 
         def hidden_codes(m):
-            h_codes[m] = held.tile([P, P], U32, name=f"h_codes{m}", tag="slot0" if m == 2 else f"h_codes{m}", align_bytes=64)
+            h_codes[m] = held.tile([P, P], U32, name=f"h_codes{m}", tag=f"h_codes{m}", align_bytes=64)
             h_scales[m] = held.tile([P, P], U8, name=f"h_scales{m}", align_bytes=64)
             nc.vector.quantize_mx(out=h_codes[m][:].bitcast(E4M3), scales=h_scales[m][:], in_=h_in[m][:])
 
@@ -273,6 +272,11 @@ def tile_moe_rag_glu_relu_kernel(
             for t in range(2):
                 y_slots[m, t] = both[:, t, :]
 
+        def unload_half(m, t, tag):
+            half = held.tile([P, P], F32, name=f"y_half{m}_{t}", tag=tag, align_bytes=64)
+            nc.scalar.copy(half[:], y[m][:, t, :])
+            y_slots[m, t] = half[:]
+
         y_tokens = [held.tile([P, T], F32, name=f"y_tokens{t}") for t in range(2)]
 
         def scatter(t, m):
@@ -287,38 +291,32 @@ def tile_moe_rag_glu_relu_kernel(
             relu(m)
         for m in TILE_ORDER:
             gated(m)
-        banks[0, 0] = psum.tile([P, H], F32, name="bank0_0", tag="bank0_2")
-        for s in range(LATE):
-            multiply(s, 0, 0)
-        for m in TILE_ORDER:
             turn(m)
-        keep_warm(1, "bank1_3")
-        for m in TILE_ORDER:
             hidden_codes(m)
-        gather_late(tok_codes[:], slot_codes, range(LATE, PASSES), held, "a_pos2")
-        for s in range(LATE, PASSES):
-            multiply(s, 0, 0)
-        for m in TILE_ORDER[:2]:
+        for tag in ("bank0_1", "bank1_3", "spare"):
+            keep_warm(1, tag)
+        for s, m in zip(range(LATE, PASSES), (3, 1)):
+            gather(tok_codes[:], slot_codes, s, 0, 1, f"a_pos{m}")
+        for m in TILE_ORDER:
             second_product(m)
         unload(2)
-        relu(0)
-        banks[0, 1] = psum.tile([P, H], F32, name="bank1_0", tag="bank0_1")
-        for s in range(PASSES):
-            multiply(s, 0, 1)
+        unload(3)
+        order = (0, 1, 2, 3, 4)
+        for w in range(2):
+            banks[0, w] = psum.tile([P, H], F32, name=f"bank{w}_0", tag=("spread", "bank0_3")[w])
+            for s in order:
+                multiply(s, 0, w, order)
+            if w == 0:
+                relu(0)
         gated(0)
-        unload(3, "words0_1_3")
         turn(0)
         hidden_codes(0)
-        for m in TILE_ORDER[:2]:
+        second_product(0)
+        unload_half(1, 0, "words0_1_3")
+        unload_half(1, 1, "h0")
+        unload(0)
+        for m in TILE_ORDER + (0,):
             for t in range(2):
                 scatter(t, m)
-        second_product(1)
-        unload(1)
-        second_product(0)
-        unload(0)
-        scatter(0, 1)
-        scatter(1, 1)
-        scatter(0, 0)
-        scatter(1, 0)
         for t in range(2):
             nc.sync.dma_start(out=out[P * t : P * (t + 1), :], in_=y_tokens[t][:])

@@ -28,11 +28,11 @@ TILE_EXPERT = (0, 1, 1, 1)
 CAST_CUTS = (((0, 96, 256), (256, 352, 512)),) + tuple(((0, c, 512),) for c in (320, 512, 512, 256))
 SPARE = 192
 TILE_ORDER = (2, 3, 1)
-TURN_BANK = {2: "spare", 3: "bank0_2", 1: "bank1_2", 0: "spare"}
-Y_BANK = {2: "bank1_1", 3: "bank1_3", 1: "bank0_1", 0: "bank0_2"}
+TURN_BANK = {2: "spare", 3: "bank0_2", 1: "bank0_1", 0: "spare"}
+Y_BANK = {2: "bank1_2", 3: "bank1_3", 1: "bank1_1", 0: "bank0_2"}
 EARLY = 3
 LATE = 3
-WARM_UPS = 3
+WARM_UPS = 4
 
 
 def interleave(ap_in, ap_out):
@@ -248,7 +248,7 @@ def tile_moe_rag_glu_relu_kernel(
             )
 
         def hidden_codes(m):
-            h_codes[m] = held.tile([P, P], U32, name=f"h_codes{m}", tag=f"h_codes{m}", align_bytes=64)
+            h_codes[m] = held.tile([P, P], U32, name=f"h_codes{m}", tag="words0_1_3" if m == 1 else f"h_codes{m}", align_bytes=64)
             h_scales[m] = held.tile([P, P], U8, name=f"h_scales{m}", align_bytes=64)
             nc.vector.quantize_mx(out=h_codes[m][:].bitcast(E4M3), scales=h_scales[m][:], in_=h_in[m][:])
 
@@ -289,30 +289,33 @@ def tile_moe_rag_glu_relu_kernel(
 
         for m in TILE_ORDER:
             relu(m)
-        for m in TILE_ORDER:
-            gated(m)
+        for tag in ("bank0_1", "bank1_1"):
+            if tag == "bank1_1":
+                for m in TILE_ORDER:
+                    gated(m)
+            keep_warm(1, tag)
+        for m in TILE_ORDER[:2]:
             turn(m)
             hidden_codes(m)
-        for tag in ("bank0_1", "bank1_3", "spare"):
-            keep_warm(1, tag)
+        turn(1)
         for s, m in zip(range(LATE, PASSES), (3, 1)):
             gather(tok_codes[:], slot_codes, s, 0, 1, f"a_pos{m}")
-        for m in TILE_ORDER:
+        for m in TILE_ORDER[:2]:
             second_product(m)
-        unload(2)
-        unload(3)
-        order = (0, 1, 2, 3, 4)
+            unload(m)
         for w in range(2):
             banks[0, w] = psum.tile([P, H], F32, name=f"bank{w}_0", tag=("spread", "bank0_3")[w])
-            for s in order:
-                multiply(s, 0, w, order)
+            for s in range(PASSES):
+                multiply(s, 0, w)
             if w == 0:
                 relu(0)
+        hidden_codes(1)
         gated(0)
         turn(0)
+        second_product(1)
         hidden_codes(0)
         second_product(0)
-        unload_half(1, 0, "words0_1_3")
+        unload_half(1, 0, "y_half1")
         unload_half(1, 1, "h0")
         unload(0)
         for m in TILE_ORDER + (0,):

@@ -225,16 +225,18 @@ def tile_moe_rag_glu_relu_kernel(
 
         def relu(m):
             a_pos[m] = held.tile([P, H], F32, name=f"a_pos{m}", tag=f"a_pos{m}", align_bytes=64)
-            nc.scalar.activation(a_pos[m][:], banks[m, 0][:], RELU)
+            nc.scalar.activation(
+                a_pos[m][:].rearrange("p (u q v) -> p u q v", u=2, v=2),
+                banks[m, 0][:].rearrange("p (q u v) -> p u q v", u=2, v=2),
+                RELU,
+            )
 
         def gated(m):
             h[m] = held.tile([P, 2, P, 2], BF16, name=f"h{m}", tag=f"h{m}", align_bytes=64)
-            nc.vector.tensor_tensor(
-                h[m][:],
-                banks[m, 1][:].rearrange("p (q u v) -> p u q v", u=2, v=2),
-                a_pos[m][:].rearrange("p (q u v) -> p u q v", u=2, v=2),
-                MULT,
-            )
+            b_sums = banks[m, 1][:].rearrange("p (q u v) -> p u q v", u=2, v=2)
+            a_values = a_pos[m][:].rearrange("p (u q v) -> p u q v", u=2, v=2)
+            for u in (slice(0, 1), slice(1, 2)) if m == 0 else (slice(0, 2),):
+                nc.vector.tensor_tensor(h[m][:, u], b_sums[:, u], a_values[:, u], MULT)
 
         def turn(m):
             turned[m] = psum.tile([P, 2, P], F32, name=f"turned{m}", tag=TURN_BANK[m])
@@ -317,7 +319,8 @@ def tile_moe_rag_glu_relu_kernel(
         second_product(0)
         unload_half(1, 0, "y_half1")
         unload_half(1, 1, "h0")
-        unload(0)
+        for t in range(2):
+            unload_half(0, t, f"y_half0_{t}")
         for m in TILE_ORDER + (0,):
             for t in range(2):
                 scatter(t, m)

@@ -25,7 +25,7 @@ N = 256
 PASSES = 5
 TILES = 4
 TILE_EXPERT = (0, 1, 1, 1)
-CAST_CUTS = (((0, 96, 256), (256, 352, 512)),) + tuple(((0, c, 512),) for c in (320, 512, 512, 256))
+CAST_CUTS = (((0, 96, 256), (256, 352, 512)),) + tuple(((0, c, 512),) for c in (320, 512, 512, 288))
 SPARE = 192
 TILE_ORDER = (2, 3, 1)
 TURN_BANK = {2: "spare", 3: "bank0_2", 1: "bank0_1", 0: "spare"}
@@ -110,9 +110,11 @@ def tile_moe_rag_glu_relu_kernel(
         load_x(3)
         load_scales(1, 0)
         load_scales(1, 1)
-        load_w(1, 1, EARLY)
+        load_w(1, 1, EARLY, (0,))
+        load_w(1, 1, EARLY - 1, (1,))
         load_x(4)
-        load_w(1, EARLY, PASSES)
+        load_w(1, EARLY - 1, PASSES, (1,))
+        load_w(1, EARLY, PASSES, (0,))
         nc.sync.dma_start(
             out=w2_codes[:].bitcast(I32), in_=w2_words[:, 0].rearrange("e p b -> p e b").bitcast(I32)
         )
@@ -225,17 +227,16 @@ def tile_moe_rag_glu_relu_kernel(
 
         def relu(m):
             a_pos[m] = held.tile([P, H], F32, name=f"a_pos{m}", tag=f"a_pos{m}", align_bytes=64)
-            nc.scalar.activation(
-                a_pos[m][:].rearrange("p (u q v) -> p u q v", u=2, v=2),
-                banks[m, 0][:].rearrange("p (q u v) -> p u q v", u=2, v=2),
-                RELU,
-            )
+            a_values = a_pos[m][:].rearrange("p (u q v) -> p u q v", u=2, v=2)
+            a_sums = banks[m, 0][:].rearrange("p (q u v) -> p u q v", u=2, v=2)
+            for u in (slice(0, 1), slice(1, 2)) if m == 2 else (slice(0, 2),):
+                nc.scalar.activation(a_values[:, u], a_sums[:, u], RELU)
 
         def gated(m):
             h[m] = held.tile([P, 2, P, 2], BF16, name=f"h{m}", tag=f"h{m}", align_bytes=64)
             b_sums = banks[m, 1][:].rearrange("p (q u v) -> p u q v", u=2, v=2)
             a_values = a_pos[m][:].rearrange("p (u q v) -> p u q v", u=2, v=2)
-            for u in (slice(0, 1), slice(1, 2)) if m == 0 else (slice(0, 2),):
+            for u in (slice(0, 1), slice(1, 2)) if m in (0, 2) else (slice(0, 2),):
                 nc.vector.tensor_tensor(h[m][:, u], b_sums[:, u], a_values[:, u], MULT)
 
         def turn(m):

@@ -49,6 +49,7 @@ def tile_moe_rag_glu_relu_kernel(
     with ExitStack() as ctx:
         held = ctx.enter_context(tc.tile_pool(name="held", bufs=1))
         reused = ctx.enter_context(tc.tile_pool(name="reused", bufs=1))
+        last_w3 = ctx.enter_context(tc.tile_pool(name="last_w3", bufs=1))
         psum = ctx.enter_context(tc.psum_pool(name="psum", bufs=1))
 
         offsets = held.tile([P, T // 16], U16, name="offsets")
@@ -81,7 +82,10 @@ def tile_moe_rag_glu_relu_kernel(
         def load_w(e, first, last, matrices=(0, 1)):
             for w in matrices:
                 name = f"words{e}_{w}_{first}"
-                part = held.tile([P, last - first, 2 * H], U8, name=name, tag=name, align_bytes=64)
+                if (e, w, last) == (0, 1, PASSES):
+                    part = last_w3.tile([P, last - first, 2 * H], U8, name=name, align_bytes=64, offset=0)
+                else:
+                    part = held.tile([P, last - first, 2 * H], U8, name=name, tag=name, align_bytes=64)
                 nc.sync.dma_start(
                     out=part[:].bitcast(I32),
                     in_=w_dram[w][e, first:last].rearrange("s p b -> p s b").bitcast(I32),
@@ -251,7 +255,10 @@ def tile_moe_rag_glu_relu_kernel(
             )
 
         def hidden_codes(m):
-            h_codes[m] = held.tile([P, P], U32, name=f"h_codes{m}", tag="words0_1_3" if m == 1 else f"h_codes{m}", align_bytes=64)
+            if m == 1:
+                h_codes[m] = last_w3.tile([P, P], U32, name="h_codes1", align_bytes=64, offset=0)
+            else:
+                h_codes[m] = held.tile([P, P], U32, name=f"h_codes{m}", align_bytes=64)
             h_scales[m] = held.tile([P, P], U8, name=f"h_scales{m}", align_bytes=64)
             nc.vector.quantize_mx(out=h_codes[m][:].bitcast(E4M3), scales=h_scales[m][:], in_=h_in[m][:])
 
@@ -305,7 +312,8 @@ def tile_moe_rag_glu_relu_kernel(
             gather(tok_codes[:], slot_codes, s, 0, 1, f"a_pos{m}")
         for m in TILE_ORDER[:2]:
             second_product(m)
-            unload(m)
+        unload(2)
+        unload_half(3, 0, "y_half3")
         for w in range(2):
             banks[0, w] = psum.tile([P, H], F32, name=f"bank{w}_0", tag=("spread", "bank0_3")[w])
             for s in range(PASSES):
@@ -314,6 +322,8 @@ def tile_moe_rag_glu_relu_kernel(
                 relu(0)
         hidden_codes(1)
         gated(0)
+        y_slots[3, 1] = last_w3.tile([P, P], F32, name="y_half3_1", align_bytes=64, offset=4 * P)[:]
+        nc.scalar.copy(y_slots[3, 1], y[3][:, 1, :])
         turn(0)
         second_product(1)
         hidden_codes(0)

@@ -19,27 +19,39 @@ MULT = mybir.AluOpType.mult
 
 P = 128
 T = 512
+HALF = T // 2
 E = 2
 H = 512
 N = 256
 PASSES = 5
+LAST = PASSES - 1
 TILES = 4
 TILE_EXPERT = (0, 1, 1, 1)
-CAST_CUTS = (((0, 96, 256), (256, 352, 512)),) + tuple(((0, c, 512),) for c in (320, 512, 512, 288))
+FIRST = (1,)
+PAIR = (2, 3)
+FINAL = (0,)
+W1, W3 = 0, 1
+PIECES = (
+    ((0, 96, HALF), (HALF, 352, T)),
+    ((0, 352, T),),
+    ((0, T, T),),
+    ((0, T, T),),
+    ((0, HALF, HALF), (HALF, T, T)),
+)
 SPARE = 192
-TILE_ORDER = (2, 3, 1)
-TURN_BANK = {2: "spare", 3: "bank0_2", 1: "bank0_1", 0: "spare"}
-Y_BANK = {2: "bank1_2", 3: "bank1_3", 1: "bank1_1", 0: "bank0_2"}
-EARLY = 3
-LATE = 3
+ROUNDED_BYTES = 8
 WARM_UPS = 4
 
 
-def interleave(ap_in, ap_out):
+def interleave(rows, grouped):
     return (
-        ap_out.rearrange("p (c i) t -> p c t i", i=4),
-        ap_in.rearrange("p t (c i) -> p c t i", i=4),
+        grouped.rearrange("p (c i) d -> p c d i", i=4),
+        rows.rearrange("p d (c i) -> p c d i", i=4),
     )
+
+
+def by_pairs(sums):
+    return sums.rearrange("p (q u v) -> p u q v", u=2, v=2)
 
 
 def tile_moe_rag_glu_relu_kernel(
@@ -48,91 +60,96 @@ def tile_moe_rag_glu_relu_kernel(
     nc = tc.nc
     with ExitStack() as ctx:
         held = ctx.enter_context(tc.tile_pool(name="held", bufs=1))
-        reused = ctx.enter_context(tc.tile_pool(name="reused", bufs=1))
-        last_w3 = ctx.enter_context(tc.tile_pool(name="last_w3", bufs=1))
+        rounded = ctx.enter_context(tc.tile_pool(name="rounded", bufs=1))
+        on_w1 = ctx.enter_context(tc.tile_pool(name="on_w1", bufs=1))
+        on_w3 = ctx.enter_context(tc.tile_pool(name="on_w3", bufs=1))
+        on_relu = ctx.enter_context(tc.tile_pool(name="on_relu", bufs=1))
         psum = ctx.enter_context(tc.psum_pool(name="psum", bufs=1))
 
         offsets = held.tile([P, T // 16], U16, name="offsets")
         x_raw = {}
         tok_codes = held.tile([P, PASSES * T + SPARE], U32, name="tok_codes", align_bytes=64)
         tok_scales = held.tile([P, PASSES * T + SPARE], U8, name="tok_scales", align_bytes=64)
-        slot_codes, slot_scales, whole = {}, {}, {}
+        slot_codes, slot_scales = {}, {}
         words = {}
         planes = [
-            [held.tile([P, PASSES, H], U8, name=f"planes{e}_{w}", align_bytes=64) for w in range(2)] for e in range(E)
+            [held.tile([P, PASSES, H], U8, name=f"planes{e}_{w}", align_bytes=64) for w in (W1, W3)] for e in range(E)
         ]
         w2_codes = held.tile([P, E, 2 * N], U8, name="w2_codes", align_bytes=64)
         w2_plane = held.tile([P, E, N], U8, name="w2_plane", align_bytes=64)
         identity = held.tile([P, P], F32, name="identity")
-        y_slots = {}
         banks = {
-            (m, w): psum.tile([P, H], F32, name=f"bank{w}_{m}", tag=f"bank{w}_{m}") for w in range(2) for m in TILE_ORDER
+            (m, w): psum.tile([P, H], F32, name=f"bank{w}_{m}", tag=f"bank{w}_{m}")
+            for w in (W1, W3)
+            for m in FIRST + PAIR
         }
-
-        w_dram = (w1_words, w3_words)
 
         def load_x(s, cols=slice(0, T)):
             if s not in x_raw:
                 x_raw[s] = held.tile([P, 4, T], F32, name=f"x_raw{s}", tag=f"x_raw{s}", align_bytes=64)
             nc.sync.dma_start(
                 out=x_raw[s][:, :, cols],
-                in_=xT[4 * P * s : 4 * P * (s + 1), cols].rearrange("(p j) w -> p j w", j=4),
+                in_=xT[4 * P * s : 4 * P * (s + 1), cols].rearrange("(p d) w -> p d w", d=4),
             )
 
-        def load_w(e, first, last, matrices=(0, 1)):
-            for w in matrices:
-                name = f"words{e}_{w}_{first}"
-                if (e, w, last) == (0, 1, PASSES):
-                    part = last_w3.tile([P, last - first, 2 * H], U8, name=name, align_bytes=64, offset=0)
-                else:
-                    part = held.tile([P, last - first, 2 * H], U8, name=name, tag=name, align_bytes=64)
-                nc.sync.dma_start(
-                    out=part[:].bitcast(I32),
-                    in_=w_dram[w][e, first:last].rearrange("s p b -> p s b").bitcast(I32),
-                )
-                for s in range(first, last):
-                    words[e, w, s] = part[:, s - first, :]
+        def load_words(e, w, first, end):
+            name = f"words{e}_{w}_{first}"
+            if (e, first) == (0, 0):
+                part = (on_w1, on_w3)[w].tile([P, end - first, 2 * H], U8, name=name, align_bytes=64, offset=0)
+            else:
+                part = held.tile([P, end - first, 2 * H], U8, name=name, tag=name, align_bytes=64)
+            nc.sync.dma_start(
+                out=part[:].bitcast(I32),
+                in_=(w1_words, w3_words)[w][e, first:end].rearrange("s p b -> p s b").bitcast(I32),
+            )
+            for s in range(first, end):
+                words[e, w, s] = part[:, s - first, :]
+
+        def load_rows(plane, by_row):
+            for r in range(4):
+                nc.sync.dma_start(out=plane[r:P:32].bitcast(I32), in_=by_row[r].bitcast(I32))
 
         def load_scales(e, w):
-            by_row = (w1_scales, w3_scales)[w][e].rearrange("s (q r) i -> r q s i", r=4)
-            for r in range(4):
-                nc.sync.dma_start(out=planes[e][w][r:P:32].bitcast(I32), in_=by_row[r].bitcast(I32))
+            load_rows(planes[e][w], (w1_scales, w3_scales)[w][e].rearrange("s (g r) i -> r g s i", r=4))
 
         gate_rows = held.tile([P, P], F32, name="gate_rows")
         nc.gpsimd.memset(gate_rows[:], 0.0)
         nc.gpsimd.memset(w2_plane[:].bitcast(I32), 0)
-        for w in range(2):
+        for w in (W1, W3):
             nc.vector.memset(planes[1][w][:].bitcast(I32), 0)
             nc.gpsimd.memset(planes[0][w][:].bitcast(I32), 0)
-        load_x(0, slice(0, 256))
-        load_x(0, slice(256, 512))
+
+        load_x(0, slice(0, HALF))
+        load_x(0, slice(HALF, T))
         nc.sync.dma_start(offsets[:], offs)
-        load_x(1)
         nc.sync.dma_start(out=gate_rows[0:TILES, :], in_=gate[0].rearrange("(m j) -> m j", j=P))
+        load_x(1)
+        load_rows(w2_plane, w2_scales.rearrange("e s (g r) i -> r g (e s) i", r=4))
         load_x(2)
-        load_w(1, 0, 1)
+        load_words(1, W1, 0, 1)
+        load_words(1, W3, 0, 1)
         load_x(3)
-        load_scales(1, 0)
-        load_scales(1, 1)
-        load_w(1, 1, EARLY, (0,))
-        load_w(1, 1, EARLY - 1, (1,))
-        load_x(4)
-        load_w(1, EARLY - 1, PASSES, (1,))
-        load_w(1, EARLY, PASSES, (0,))
+        load_scales(1, W1)
+        load_scales(1, W3)
+        load_words(1, W1, 1, 3)
+        load_x(LAST, slice(0, HALF))
+        load_words(1, W3, 1, 3)
+        load_x(LAST, slice(HALF, T))
+        load_words(1, W1, 3, PASSES)
+        load_words(1, W3, 3, PASSES)
         nc.sync.dma_start(
             out=w2_codes[:].bitcast(I32), in_=w2_words[:, 0].rearrange("e p b -> p e b").bitcast(I32)
         )
-        by_row = w2_scales.rearrange("e s (q r) i -> r q (e s) i", r=4)
-        for r in range(4):
-            nc.sync.dma_start(out=w2_plane[r:P:32].bitcast(I32), in_=by_row[r].bitcast(I32))
-        load_scales(0, 0)
-        load_w(0, 0, 5, (0,))
-        load_scales(0, 1)
-        load_w(0, 0, 3, (1,))
-        load_w(0, 3, 5, (1,))
+        load_scales(0, W1)
+        load_words(0, W1, 0, 2)
+        load_words(0, W1, 2, PASSES)
+        load_scales(0, W3)
+        load_words(0, W3, 0, 3)
+        load_words(0, W3, 3, PASSES)
 
         nc.vector.memset(tok_scales[:].bitcast(I32), 0)
         nc.vector.memset(tok_codes[:, PASSES * T :].bitcast(I32), 0)
+        nc.vector.memset(tok_codes[:, HALF:T].bitcast(I32), 0)
         make_identity(nc, identity[:])
 
         by_slot = psum.tile([P, P], F32, name="by_slot", tag="spare")
@@ -144,39 +161,48 @@ def tile_moe_rag_glu_relu_kernel(
             nc.tensor.transpose(spread[:, m, :], gate_cols[:, m : m + 1].to_broadcast([P, P]), identity[:])
 
         def first_col(s):
-            return (PASSES - 1 - s) * T
+            return (LAST - s) * T
 
-        def tokens(s):
-            if s == PASSES - 1:
-                x_bf = reused.tile([P, T, 4], BF16, name="x_bf_last", align_bytes=64, offset=0)
-            else:
-                x_bf = held.tile([P, T, 4], BF16, name="x_bf", tag=f"x_bf{s % 2}", align_bytes=64)
-            for a, cut, b in CAST_CUTS[s]:
-                if a < cut:
-                    dst, src = interleave(x_raw[s][:, :, a:cut], x_bf[:, a:cut, :])
-                    nc.scalar.activation(dst, src, COPY)
-                if cut < b:
-                    dst, src = interleave(x_raw[s][:, :, cut:b], x_bf[:, cut:b, :])
-                    nc.vector.tensor_copy(dst, src)
-                nc.vector.quantize_mx(
-                    out=tok_codes[:, first_col(s) + a : first_col(s) + b].bitcast(E4M3),
-                    scales=tok_scales[:, first_col(s) + a : first_col(s) + b],
-                    in_=x_bf[:, a:b, :].rearrange("p w j -> p (w j)"),
-                )
+        def rounded_at(s, token=0):
+            return ROUNDED_BYTES * (T * s + token)
 
-        def gather(table, found, s, first, last, tag=None, offset=None):
-            name = f"slots{table.shape[1]}_{int(table.dtype == U8)}_{s}_{first}"
-            if offset is None:
-                picked = held.tile([P, P * (last - first)], table.dtype, name=name, tag=tag or name, align_bytes=64)
+        def quantise_tokens(s, piece):
+            first, cut, end = PIECES[s][piece]
+            x_bf = rounded.tile(
+                [P, end - first, 4], BF16, name=f"x_bf{s}_{first}", align_bytes=64, offset=rounded_at(s, first)
+            )
+            dst, src = interleave(x_raw[s][:, :, first:cut], x_bf[:, 0 : cut - first, :])
+            nc.scalar.activation(dst, src, COPY)
+            if cut < end:
+                dst, src = interleave(x_raw[s][:, :, cut:end], x_bf[:, cut - first : end - first, :])
+                nc.vector.tensor_copy(dst, src)
+            cols = slice(first_col(s) + first, first_col(s) + end)
+            nc.vector.quantize_mx(
+                out=tok_codes[:, cols].bitcast(E4M3),
+                scales=tok_scales[:, cols],
+                in_=x_bf[:].rearrange("p w d -> p (w d)"),
+            )
+
+        def gather(table, found, s, first, end, pool=None, offset=None):
+            name = f"slots{int(table.dtype == U8)}_{s}_{first}"
+            shape = [P, P * (end - first)]
+            if pool is None:
+                picked = held.tile(shape, table.dtype, name=name, tag=name, align_bytes=64)
             else:
-                picked = reused.tile([P, P * (last - first)], table.dtype, name=name, align_bytes=64, offset=offset)
-            cols = slice(first_col(s), first_col(s) + T + SPARE)
-            nc.vector.tensor_copy(picked[:], table[:, cols].indirect(offsets[:, 8 * first : 8 * last]))
-            whole[s, table.dtype == U8] = picked[:]
-            for m in range(first, last):
+                picked = pool.tile(shape, table.dtype, name=name, align_bytes=64, offset=offset)
+            window = table[:, first_col(s) : first_col(s) + T + SPARE]
+            nc.vector.tensor_copy(picked[:], window.indirect(offsets[:, 8 * first : 8 * end]))
+            for m in range(first, end):
                 found[s, m] = picked[:, P * (m - first) : P * (m - first + 1)]
+            return picked
 
-        def multiply(s, m, w, order=tuple(range(PASSES))):
+        def gather_words(s, first, end, pool=None, offset=None):
+            gather(tok_codes[:], slot_codes, s, first, end, pool, offset)
+
+        def gather_scales(s, first, end, pool=None, offset=None):
+            return gather(tok_scales[:], slot_scales, s, first, end, pool, offset)
+
+        def multiply(s, m, w):
             e = TILE_EXPERT[m]
             nc.tensor.matmul_mx(
                 out=banks[m, w][:],
@@ -184,156 +210,150 @@ def tile_moe_rag_glu_relu_kernel(
                 lhsT_scale=slot_scales[s, m],
                 rhs=words[e, w, s].bitcast(E2M1),
                 rhs_scale=planes[e][w][:, s, :],
-                start=(s == order[0]),
-                stop=(s == order[-1]),
+                start=(s == 0),
+                stop=(s == LAST),
             )
 
-        tokens(0)
-        gather(tok_scales[:], slot_scales, 0, 0, TILES)
-        gather(tok_codes[:], slot_codes, 0, 0, TILES)
-        for s in range(1, LATE):
-            tokens(s)
-            gather(tok_scales[:], slot_scales, s, 0, TILES)
-            gather(tok_codes[:], slot_codes, s, 0, TILES)
-        tokens(LATE)
-        gather(tok_scales[:], slot_scales, LATE, 1, TILES)
-        gather(tok_codes[:], slot_codes, LATE, 1, TILES)
-        tokens(LATE + 1)
-        gates = reused.tile([P, T], F32, name="gates", align_bytes=64, offset=0)
-        nc.scalar.copy(gates[:], spread[:].rearrange("p m j -> p (m j)"))
-        for first, last in ((2, 3), (3, 4), (1, 2)):
-            gather(tok_scales[:], slot_scales, PASSES - 1, first, last)
-            gather(tok_codes[:], slot_codes, PASSES - 1, first, last)
-
-        for s in range(LATE, PASSES):
-            gather(tok_scales[:], slot_scales, s, 0, 1, offset=4 * T + P * s)
-
-        def keep_warm(count, tag):
-            warm = psum.tile([P, H], F32, name="warm", tag=tag)
-            for n in range(count):
-                nc.tensor.matmul_mx(
-                    out=warm[:],
-                    lhsT=slot_codes[0, n % TILES].bitcast(E4M3),
-                    lhsT_scale=slot_scales[0, n % TILES],
-                    rhs=words[1, 0, 0].bitcast(E2M1),
-                    rhs_scale=whole[1, True],
-                    start=True,
-                    stop=True,
-                )
-
-        keep_warm(WARM_UPS, "spare")
+        all_scales = {}
+        quantise_tokens(0, 0)
         for s in range(PASSES):
-            for m in TILE_ORDER:
-                for w in range(2):
+            quantise_tokens(s, 1 if s == 0 else 0)
+            if s > 0:
+                gather_words(s - 1, 0, 1, rounded, rounded_at(s))
+            if s == LAST - 1:
+                gates = rounded.tile([P, T], F32, name="gates", align_bytes=64, offset=rounded_at(s, HALF))
+                nc.scalar.copy(gates[:], spread[:].rearrange("p m j -> p (m j)"))
+            if s < LAST:
+                all_scales[s] = gather_scales(s, 0, TILES)
+                gather_words(s, 1, TILES)
+        gather_scales(LAST, 1, 2)
+        gather_words(LAST, 1, 2)
+        quantise_tokens(LAST, 1)
+        for m in PAIR:
+            gather_scales(LAST, m, m + 1)
+            gather_words(LAST, m, m + 1)
+
+        warm = psum.tile([P, H], F32, name="warm", tag="spare")
+        for n in range(WARM_UPS):
+            m = (FIRST + PAIR)[n % 3]
+            nc.tensor.matmul_mx(
+                out=warm[:],
+                lhsT=slot_codes[0, m].bitcast(E4M3),
+                lhsT_scale=slot_scales[0, m],
+                rhs=words[1, W1, 0].bitcast(E2M1),
+                rhs_scale=all_scales[1][:],
+                start=True,
+                stop=True,
+            )
+
+        for s in range(PASSES):
+            for m in FIRST + PAIR:
+                for w in (W1, W3):
                     multiply(s, m, w)
 
-        h, h_in, turned, h_codes, h_scales, y, a_pos = {}, {}, {}, {}, {}, {}, {}
+        h, a_pos, y_slots = {}, {}, {}
+        WHOLE, HALVES = (slice(0, 2),), (slice(0, 1), slice(1, 2))
 
-        def relu(m):
-            a_pos[m] = held.tile([P, H], F32, name=f"a_pos{m}", tag=f"a_pos{m}", align_bytes=64)
-            a_values = a_pos[m][:].rearrange("p (u q v) -> p u q v", u=2, v=2)
-            a_sums = banks[m, 0][:].rearrange("p (q u v) -> p u q v", u=2, v=2)
-            for u in (slice(0, 1), slice(1, 2)) if m == 2 else (slice(0, 2),):
-                nc.scalar.activation(a_values[:, u], a_sums[:, u], RELU)
-
-        def gated(m):
-            h[m] = held.tile([P, 2, P, 2], BF16, name=f"h{m}", tag=f"h{m}", align_bytes=64)
-            b_sums = banks[m, 1][:].rearrange("p (q u v) -> p u q v", u=2, v=2)
-            a_values = a_pos[m][:].rearrange("p (u q v) -> p u q v", u=2, v=2)
-            for u in (slice(0, 1), slice(1, 2)) if m in (0, 2) else (slice(0, 2),):
-                nc.vector.tensor_tensor(h[m][:, u], b_sums[:, u], a_values[:, u], MULT)
-
-        def turn(m):
-            turned[m] = psum.tile([P, 2, P], F32, name=f"turned{m}", tag=TURN_BANK[m])
-            pairs = h[m][:].rearrange("p u q v -> p (u q v)").bitcast(F32)
-            for u in range(2):
-                nc.tensor.transpose(turned[m][:, u, :], pairs[:, P * u : P * (u + 1)], identity[:])
-            h_in[m] = held.tile([P, 4 * P], BF16, name=f"h_in{m}", tag=f"h_in{m}", align_bytes=64)
-            nc.scalar.copy(
-                h_in[m][:].bitcast(F32).rearrange("p (c u) -> p c u", u=2),
-                turned[m][:].rearrange("p u c -> p c u"),
-            )
-
-        def hidden_codes(m):
-            if m == 1:
-                h_codes[m] = last_w3.tile([P, P], U32, name="h_codes1", align_bytes=64, offset=0)
+        def relu(m, parts=WHOLE, pool=None):
+            if pool is None:
+                a_pos[m] = held.tile([P, H], F32, name=f"a_pos{m}", tag=f"a_pos{m}", align_bytes=64)
             else:
-                h_codes[m] = held.tile([P, P], U32, name=f"h_codes{m}", align_bytes=64)
-            h_scales[m] = held.tile([P, P], U8, name=f"h_scales{m}", align_bytes=64)
-            nc.vector.quantize_mx(out=h_codes[m][:].bitcast(E4M3), scales=h_scales[m][:], in_=h_in[m][:])
+                a_pos[m] = pool.tile([P, H], F32, name=f"a_pos{m}", align_bytes=64, offset=0)
+            a_values = a_pos[m][:].rearrange("p (u q v) -> p u q v", u=2, v=2)
+            for u in parts:
+                nc.scalar.activation(a_values[:, u], by_pairs(banks[m, W1][:])[:, u], RELU)
 
-        def second_product(m):
-            e = TILE_EXPERT[m]
-            y[m] = psum.tile([P, 2, P], F32, name=f"y{m}", tag=Y_BANK[m])
-            for t in range(2):
+        def gated(m, tag, parts=WHOLE):
+            h[m] = held.tile([P, 2, P, 2], BF16, name=f"h{m}", tag=tag, align_bytes=64)
+            a_values = a_pos[m][:].rearrange("p (u q v) -> p u q v", u=2, v=2)
+            for u in parts:
+                nc.vector.tensor_tensor(h[m][:, u], by_pairs(banks[m, W3][:])[:, u], a_values[:, u], MULT)
+
+        def turn(tiles, bank):
+            turned = psum.tile([P, len(tiles), 2, P], F32, name=f"turned{tiles[0]}", tag=bank)
+            for j, m in enumerate(tiles):
+                pairs = h[m][:].rearrange("p u q v -> p (u q v)").bitcast(F32)
+                for u in range(2):
+                    nc.tensor.transpose(turned[:, j, u, :], pairs[:, P * u : P * (u + 1)], identity[:])
+            name = f"h_in{tiles[0]}"
+            h_in = held.tile([P, 4 * P * len(tiles)], BF16, name=name, tag=name, align_bytes=64)
+            nc.scalar.copy(
+                h_in[:].bitcast(F32).rearrange("p (j c u) -> p j c u", u=2, c=P),
+                turned[:].rearrange("p j u c -> p j c u"),
+            )
+            return h_in
+
+        def quantise_hidden(h_in, tiles, pool=None):
+            shape = [P, P * len(tiles)]
+            if pool is None:
+                codes = held.tile(shape, U32, name=f"h_codes{tiles[0]}", align_bytes=64)
+            else:
+                codes = pool.tile(shape, U32, name=f"h_codes{tiles[0]}", align_bytes=64, offset=0)
+            scales = held.tile(shape, U8, name=f"h_scales{tiles[0]}", align_bytes=64)
+            nc.vector.quantize_mx(out=codes[:].bitcast(E4M3), scales=scales[:], in_=h_in[:])
+            return codes, scales
+
+        def second_product(hidden, tiles, bank, row_blocks=(0, 1)):
+            codes, scales = hidden
+            e = TILE_EXPERT[tiles[0]]
+            width = P * len(tiles)
+            y = psum.tile([P, len(row_blocks), width], F32, name=f"y{tiles[0]}_{row_blocks[0]}", tag=bank)
+            for j, t in enumerate(row_blocks):
                 nc.tensor.matmul_mx(
-                    out=y[m][:, t, :],
+                    out=y[:, j, :],
                     lhsT=w2_codes[:, e, 2 * P * t : 2 * P * (t + 1)].bitcast(E2M1),
                     lhsT_scale=w2_plane[:, e, P * t : P * (t + 1)],
-                    rhs=h_codes[m][:].bitcast(E4M3),
-                    rhs_scale=h_scales[m][:],
+                    rhs=codes[:].bitcast(E4M3),
+                    rhs_scale=scales[:],
                     start=True,
                     stop=True,
                 )
-
-        def unload(m, tag=None):
-            both = held.tile([P, 2, P], F32, name=f"y_slots{m}", tag=tag or f"y_slots{m}", align_bytes=64)
-            nc.scalar.copy(both[:], y[m][:])
-            for t in range(2):
-                y_slots[m, t] = both[:, t, :]
-
-        def unload_half(m, t, tag):
-            half = held.tile([P, P], F32, name=f"y_half{m}_{t}", tag=tag, align_bytes=64)
-            nc.scalar.copy(half[:], y[m][:, t, :])
-            y_slots[m, t] = half[:]
+            for j, t in enumerate(row_blocks):
+                y_slots[tiles, t] = held.tile([P, width], F32, name=f"y_slots{tiles[0]}_{t}", align_bytes=64)
+                nc.scalar.copy(y_slots[tiles, t][:], y[:, j, :])
 
         y_tokens = [held.tile([P, T], F32, name=f"y_tokens{t}") for t in range(2)]
 
-        def scatter(t, m):
+        def scatter(tiles, t):
+            first, end = tiles[0], tiles[-1] + 1
             nc.vector.tensor_tensor(
-                y_tokens[t][:].indirect(offsets[:, 8 * m : 8 * (m + 1)]),
-                y_slots[m, t],
-                gates[:, P * m : P * (m + 1)],
+                y_tokens[t][:].indirect(offsets[:, 8 * first : 8 * end]),
+                y_slots[tiles, t][:],
+                gates[:, P * first : P * end],
                 MULT,
             )
 
-        for m in TILE_ORDER:
-            relu(m)
-        for tag in ("bank0_1", "bank1_1"):
-            if tag == "bank1_1":
-                for m in TILE_ORDER:
-                    gated(m)
-            keep_warm(1, tag)
-        for m in TILE_ORDER[:2]:
-            turn(m)
-            hidden_codes(m)
-        turn(1)
-        for s, m in zip(range(LATE, PASSES), (3, 1)):
-            gather(tok_codes[:], slot_codes, s, 0, 1, f"a_pos{m}")
-        for m in TILE_ORDER[:2]:
-            second_product(m)
-        unload(2)
-        unload_half(3, 0, "y_half3")
-        for w in range(2):
-            banks[0, w] = psum.tile([P, H], F32, name=f"bank{w}_0", tag=("spread", "bank0_3")[w])
-            for s in range(PASSES):
-                multiply(s, 0, w)
-            if w == 0:
-                relu(0)
-        hidden_codes(1)
-        gated(0)
-        y_slots[3, 1] = last_w3.tile([P, P], F32, name="y_half3_1", align_bytes=64, offset=4 * P)[:]
-        nc.scalar.copy(y_slots[3, 1], y[3][:, 1, :])
-        turn(0)
-        second_product(1)
-        hidden_codes(0)
-        second_product(0)
-        unload_half(1, 0, "y_half1")
-        unload_half(1, 1, "h0")
+        relu(1, HALVES, on_relu)
+        relu(2)
+        relu(3)
+        gated(1, "h1", HALVES)
+        turned_first = turn(FIRST, "spare")
+        gather_scales(LAST, 0, 1, on_relu, 4 * P)
+        gather_words(LAST, 0, 1, on_relu, 0)
+        gated(2, "h2")
+        banks[0, W1] = psum.tile([P, H], F32, name="bank0_0", tag="bank1_1")
+        for s in range(PASSES):
+            multiply(s, 0, W1)
+        hidden_first = quantise_hidden(turned_first, FIRST, on_w1)
+        second_product(hidden_first, FIRST, "spread")
+        relu(0, WHOLE, on_w1)
+        gated(3, "h_in1")
+        turned_pair = turn(PAIR, "bank1_3")
+        banks[0, W3] = psum.tile([P, H], F32, name="bank1_0", tag="spread")
+        for s in range(PASSES):
+            multiply(s, 0, W3)
+        scatter(FIRST, 0)
+        hidden_pair = quantise_hidden(turned_pair, PAIR, on_w3)
+        scatter(FIRST, 1)
+        second_product(hidden_pair, PAIR, "bank0_3", (0,))
+        gated(0, "h0", HALVES)
+        turned_final = turn(FINAL, "spare")
+        second_product(hidden_pair, PAIR, "spare", (1,))
+        scatter(PAIR, 0)
+        hidden_final = quantise_hidden(turned_final, FINAL)
+        second_product(hidden_final, FINAL, "bank1_2")
+        scatter(PAIR, 1)
         for t in range(2):
-            unload_half(0, t, f"y_half0_{t}")
-        for m in TILE_ORDER + (0,):
-            for t in range(2):
-                scatter(t, m)
+            scatter(FINAL, t)
         for t in range(2):
             nc.sync.dma_start(out=out[P * t : P * (t + 1), :], in_=y_tokens[t][:])

@@ -41,6 +41,24 @@ PIECES = (
 SPARE = 192
 ROUNDED_BYTES = 8
 WARM_UPS = 4
+SHARED = {
+    "a_pos1": ("on_relu1", 0),
+    "slots0_4_0": ("on_relu1", 0),
+    "slots1_4_0": ("on_relu1", 512),
+    "words0_0_0": ("on_w1", 0),
+    "h_codes1": ("on_w1", 0),
+    "a_pos0": ("on_w1", 0),
+    "h_in1": ("on_turned1", 0),
+    "h3": ("on_turned1", 0),
+    "y_tokens0": ("on_turned1", 0),
+    "a_pos3": ("on_relu3", 0),
+    "y_slots1_0_0": ("on_relu3", 0),
+    "words0_1_0": ("on_w3", 0),
+    "h_codes_pair": ("on_w3", 0),
+    "h0": ("on_h0", 0),
+    "y_slots3_1_0": ("on_h0", 0),
+    "y_slots3_0_0": ("on_h0", 512),
+}
 
 
 def interleave(rows, grouped):
@@ -61,9 +79,14 @@ def tile_moe_rag_glu_relu_kernel(
     with ExitStack() as ctx:
         held = ctx.enter_context(tc.tile_pool(name="held", bufs=1))
         rounded = ctx.enter_context(tc.tile_pool(name="rounded", bufs=1))
-        on_w1 = ctx.enter_context(tc.tile_pool(name="on_w1", bufs=1))
-        on_w3 = ctx.enter_context(tc.tile_pool(name="on_w3", bufs=1))
-        on_relu = ctx.enter_context(tc.tile_pool(name="on_relu", bufs=1))
+        places = {name: ctx.enter_context(tc.tile_pool(name=name, bufs=1)) for name in sorted({p for p, o in SHARED.values()})}
+
+        def sbuf(shape, dtype, name):
+            if name in SHARED:
+                place, offset = SHARED[name]
+                return places[place].tile(shape, dtype, name=name, align_bytes=64, offset=offset)
+            return held.tile(shape, dtype, name=name, align_bytes=64)
+
         psum = ctx.enter_context(tc.psum_pool(name="psum", bufs=1))
 
         offsets = held.tile([P, T // 16], U16, name="offsets")
@@ -94,10 +117,7 @@ def tile_moe_rag_glu_relu_kernel(
 
         def load_words(e, w, first, end):
             name = f"words{e}_{w}_{first}"
-            if (e, first) == (0, 0):
-                part = (on_w1, on_w3)[w].tile([P, end - first, 2 * H], U8, name=name, align_bytes=64, offset=0)
-            else:
-                part = held.tile([P, end - first, 2 * H], U8, name=name, tag=name, align_bytes=64)
+            part = sbuf([P, end - first, 2 * H], U8, name)
             nc.sync.dma_start(
                 out=part[:].bitcast(I32),
                 in_=(w1_words, w3_words)[w][e, first:end].rearrange("s p b -> p s b").bitcast(I32),
@@ -187,7 +207,7 @@ def tile_moe_rag_glu_relu_kernel(
             name = f"slots{int(table.dtype == U8)}_{s}_{first}"
             shape = [P, P * (end - first)]
             if pool is None:
-                picked = held.tile(shape, table.dtype, name=name, tag=name, align_bytes=64)
+                picked = sbuf(shape, table.dtype, name)
             else:
                 picked = pool.tile(shape, table.dtype, name=name, align_bytes=64, offset=offset)
             window = table[:, first_col(s) : first_col(s) + T + SPARE]
@@ -226,13 +246,75 @@ def tile_moe_rag_glu_relu_kernel(
             if s < LAST:
                 all_scales[s] = gather_scales(s, 0, TILES)
                 gather_words(s, 1, TILES)
+        h, a_pos, h_in, hidden, sums, y_slots = {}, {}, {}, {}, {}, {}
+        y_tokens = [sbuf([P, T], F32, f"y_tokens{t}") for t in range(2)]
+        WHOLE, HALVES = (slice(0, 2),), (slice(0, 1), slice(1, 2))
+
+        def relu(m, parts=WHOLE):
+            a_pos[m] = sbuf([P, H], F32, f"a_pos{m}")
+            a_values = a_pos[m][:].rearrange("p (u q v) -> p u q v", u=2, v=2)
+            for u in parts:
+                nc.scalar.activation(a_values[:, u], by_pairs(banks[m, W1][:])[:, u], RELU)
+
+        def gated(m, parts=WHOLE):
+            h[m] = sbuf([P, 2, P, 2], BF16, f"h{m}")
+            a_values = a_pos[m][:].rearrange("p (u q v) -> p u q v", u=2, v=2)
+            for u in parts:
+                nc.vector.tensor_tensor(h[m][:, u], by_pairs(banks[m, W3][:])[:, u], a_values[:, u], MULT)
+
+        def turn(m, bank):
+            turned = psum.tile([P, 2, P], F32, name=f"turned{m}", tag=bank)
+            pairs = h[m][:].rearrange("p u q v -> p (u q v)").bitcast(F32)
+            for u in range(2):
+                nc.tensor.transpose(turned[:, u, :], pairs[:, P * u : P * (u + 1)], identity[:])
+            h_in[m] = sbuf([P, 4 * P], BF16, f"h_in{m}")
+            nc.scalar.copy(
+                h_in[m][:].bitcast(F32).rearrange("p (c u) -> p c u", u=2),
+                turned[:].rearrange("p u c -> p c u"),
+            )
+
+        def quantise_hidden(m):
+            codes = sbuf([P, P], U32, f"h_codes{m}")
+            scales = sbuf([P, P], U8, f"h_scales{m}")
+            nc.vector.quantize_mx(out=codes[:].bitcast(E4M3), scales=scales[:], in_=h_in[m][:])
+            hidden[m] = codes, scales
+
+        def second_product(m, bank_tags):
+            codes, scales = hidden[m]
+            e = TILE_EXPERT[m]
+            for t, tag in enumerate(bank_tags):
+                sums[m, t] = psum.tile([P, P], F32, name=f"y{m}_{t}", tag=tag)
+                nc.tensor.matmul_mx(
+                    out=sums[m, t][:],
+                    lhsT=w2_codes[:, e, 2 * P * t : 2 * P * (t + 1)].bitcast(E2M1),
+                    lhsT_scale=w2_plane[:, e, P * t : P * (t + 1)],
+                    rhs=codes[:].bitcast(E4M3),
+                    rhs_scale=scales[:],
+                    start=True,
+                    stop=True,
+                )
+
+        def leave_bank(m, t, by_vector, first=0, end=P):
+            y_slots[m, t, first] = sbuf([P, end - first], F32, f"y_slots{m}_{t}_{first}")
+            if by_vector:
+                nc.scalar.copy(y_slots[m, t, first][:], sums[m, t][:, first:end])
+            else:
+                nc.vector.tensor_tensor(
+                    y_slots[m, t, first][:], sums[m, t][:, first:end], gates[:, P * m + first : P * m + end], MULT
+                )
+
+        def scatter(m, t, by_vector, first=0, end=P):
+            window = y_tokens[t][:].indirect(offsets[:, (P * m + first) // 16 : (P * m + end) // 16])
+            if by_vector:
+                nc.vector.tensor_tensor(window, y_slots[m, t, first][:], gates[:, P * m + first : P * m + end], MULT)
+            else:
+                nc.scalar.activation(window, y_slots[m, t, first][:], COPY)
+
+        def new_bank(m, w, tag):
+            banks[m, w] = psum.tile([P, H], F32, name=f"bank{w}_{m}", tag=tag)
+
         gather_scales(LAST, 1, 2)
         gather_words(LAST, 1, 2)
-        quantise_tokens(LAST, 1)
-        for m in PAIR:
-            gather_scales(LAST, m, m + 1)
-            gather_words(LAST, m, m + 1)
-
         warm = psum.tile([P, H], F32, name="warm", tag="spare")
         for n in range(WARM_UPS):
             m = (FIRST + PAIR)[n % 3]
@@ -246,114 +328,98 @@ def tile_moe_rag_glu_relu_kernel(
                 stop=True,
             )
 
-        for s in range(PASSES):
+
+        for s in range(LAST):
             for m in FIRST + PAIR:
                 for w in (W1, W3):
                     multiply(s, m, w)
 
-        h, a_pos, y_slots = {}, {}, {}
-        WHOLE, HALVES = (slice(0, 2),), (slice(0, 1), slice(1, 2))
+        def last_pass(m):
+            for w in (W1, W3):
+                multiply(LAST, m, w)
 
-        def relu(m, parts=WHOLE, pool=None):
-            if pool is None:
-                a_pos[m] = held.tile([P, H], F32, name=f"a_pos{m}", tag=f"a_pos{m}", align_bytes=64)
-            else:
-                a_pos[m] = pool.tile([P, H], F32, name=f"a_pos{m}", align_bytes=64, offset=0)
-            a_values = a_pos[m][:].rearrange("p (u q v) -> p u q v", u=2, v=2)
-            for u in parts:
-                nc.scalar.activation(a_values[:, u], by_pairs(banks[m, W1][:])[:, u], RELU)
-
-        def gated(m, tag, parts=WHOLE):
-            h[m] = held.tile([P, 2, P, 2], BF16, name=f"h{m}", tag=tag, align_bytes=64)
-            a_values = a_pos[m][:].rearrange("p (u q v) -> p u q v", u=2, v=2)
-            for u in parts:
-                nc.vector.tensor_tensor(h[m][:, u], by_pairs(banks[m, W3][:])[:, u], a_values[:, u], MULT)
-
-        def turn(tiles, bank):
-            turned = psum.tile([P, len(tiles), 2, P], F32, name=f"turned{tiles[0]}", tag=bank)
-            for j, m in enumerate(tiles):
+        def turn_pair(bank):
+            turned = psum.tile([P, 2, 2, P], F32, name="turned_pair", tag=bank)
+            for j, m in enumerate(PAIR):
                 pairs = h[m][:].rearrange("p u q v -> p (u q v)").bitcast(F32)
                 for u in range(2):
                     nc.tensor.transpose(turned[:, j, u, :], pairs[:, P * u : P * (u + 1)], identity[:])
-            name = f"h_in{tiles[0]}"
-            h_in = held.tile([P, 4 * P * len(tiles)], BF16, name=name, tag=name, align_bytes=64)
+            h_in[PAIR] = sbuf([P, 8 * P], BF16, "h_in_pair")
             nc.scalar.copy(
-                h_in[:].bitcast(F32).rearrange("p (j c u) -> p j c u", u=2, c=P),
+                h_in[PAIR][:].bitcast(F32).rearrange("p (j c u) -> p j c u", u=2, c=P),
                 turned[:].rearrange("p j u c -> p j c u"),
             )
-            return h_in
 
-        def quantise_hidden(h_in, tiles, pool=None):
-            shape = [P, P * len(tiles)]
-            if pool is None:
-                codes = held.tile(shape, U32, name=f"h_codes{tiles[0]}", align_bytes=64)
-            else:
-                codes = pool.tile(shape, U32, name=f"h_codes{tiles[0]}", align_bytes=64, offset=0)
-            scales = held.tile(shape, U8, name=f"h_scales{tiles[0]}", align_bytes=64)
-            nc.vector.quantize_mx(out=codes[:].bitcast(E4M3), scales=scales[:], in_=h_in[:])
-            return codes, scales
-
-        def second_product(hidden, tiles, bank, row_blocks=(0, 1)):
-            codes, scales = hidden
-            e = TILE_EXPERT[tiles[0]]
-            width = P * len(tiles)
-            y = psum.tile([P, len(row_blocks), width], F32, name=f"y{tiles[0]}_{row_blocks[0]}", tag=bank)
-            for j, t in enumerate(row_blocks):
+        def pair_product(bank_tags):
+            codes = sbuf([P, 2 * P], U32, "h_codes_pair")
+            scales = sbuf([P, 2 * P], U8, "h_scales_pair")
+            nc.vector.quantize_mx(out=codes[:].bitcast(E4M3), scales=scales[:], in_=h_in[PAIR][:])
+            for t, tag in enumerate(bank_tags):
+                both = psum.tile([P, 2 * P], F32, name=f"y_pair{t}", tag=tag)
                 nc.tensor.matmul_mx(
-                    out=y[:, j, :],
-                    lhsT=w2_codes[:, e, 2 * P * t : 2 * P * (t + 1)].bitcast(E2M1),
-                    lhsT_scale=w2_plane[:, e, P * t : P * (t + 1)],
+                    out=both[:],
+                    lhsT=w2_codes[:, 1, 2 * P * t : 2 * P * (t + 1)].bitcast(E2M1),
+                    lhsT_scale=w2_plane[:, 1, P * t : P * (t + 1)],
                     rhs=codes[:].bitcast(E4M3),
                     rhs_scale=scales[:],
                     start=True,
                     stop=True,
                 )
-            for j, t in enumerate(row_blocks):
-                y_slots[tiles, t] = held.tile([P, width], F32, name=f"y_slots{tiles[0]}_{t}", align_bytes=64)
-                nc.scalar.copy(y_slots[tiles, t][:], y[:, j, :])
+                for j, m in enumerate(PAIR):
+                    sums[m, t] = both[:, P * j : P * (j + 1)]
 
-        y_tokens = [held.tile([P, T], F32, name=f"y_tokens{t}") for t in range(2)]
+        def gated_part(m, u):
+            if m not in h:
+                h[m] = sbuf([P, 2, P, 2], BF16, f"h{m}")
+            a_values = a_pos[m][:].rearrange("p (u q v) -> p u q v", u=2, v=2)
+            nc.vector.tensor_tensor(h[m][:, u], by_pairs(banks[m, W3][:])[:, u], a_values[:, u], MULT)
 
-        def scatter(tiles, t):
-            first, end = tiles[0], tiles[-1] + 1
-            nc.vector.tensor_tensor(
-                y_tokens[t][:].indirect(offsets[:, 8 * first : 8 * end]),
-                y_slots[tiles, t][:],
-                gates[:, P * first : P * end],
-                MULT,
-            )
-
-        relu(1, HALVES, on_relu)
+        last_pass(1)
+        quantise_tokens(LAST, 1)
+        for m in PAIR:
+            gather_scales(LAST, m, m + 1)
+            gather_words(LAST, m, m + 1)
+            last_pass(m)
+        relu(1, HALVES)
         relu(2)
         relu(3)
-        gated(1, "h1", HALVES)
-        turned_first = turn(FIRST, "spare")
-        gather_scales(LAST, 0, 1, on_relu, 4 * P)
-        gather_words(LAST, 0, 1, on_relu, 0)
-        gated(2, "h2")
-        banks[0, W1] = psum.tile([P, H], F32, name="bank0_0", tag="bank1_1")
+        gated(1, HALVES)
+        turn(1, "spare")
+        gather_scales(LAST, 0, 1)
+        gather_words(LAST, 0, 1)
+        gated(2)
+        new_bank(0, W1, "bank1_1")
         for s in range(PASSES):
             multiply(s, 0, W1)
-        hidden_first = quantise_hidden(turned_first, FIRST, on_w1)
-        second_product(hidden_first, FIRST, "spread")
-        relu(0, WHOLE, on_w1)
-        gated(3, "h_in1")
-        turned_pair = turn(PAIR, "bank1_3")
-        banks[0, W3] = psum.tile([P, H], F32, name="bank1_0", tag="spread")
+        quantise_hidden(1)
+        second_product(1, ("spread", "bank0_1"))
+        gated(3)
+        turn_pair("bank1_3")
+        leave_bank(1, 0, False)
+        leave_bank(1, 1, True)
+        relu(0)
+        new_bank(0, W3, "spread")
         for s in range(PASSES):
             multiply(s, 0, W3)
-        scatter(FIRST, 0)
-        hidden_pair = quantise_hidden(turned_pair, PAIR, on_w3)
-        scatter(FIRST, 1)
-        second_product(hidden_pair, PAIR, "bank0_3", (0,))
-        gated(0, "h0", HALVES)
-        turned_final = turn(FINAL, "spare")
-        second_product(hidden_pair, PAIR, "spare", (1,))
-        scatter(PAIR, 0)
-        hidden_final = quantise_hidden(turned_final, FINAL)
-        second_product(hidden_final, FINAL, "bank1_2")
-        scatter(PAIR, 1)
-        for t in range(2):
-            scatter(FINAL, t)
-        for t in range(2):
-            nc.sync.dma_start(out=out[P * t : P * (t + 1), :], in_=y_tokens[t][:])
+        scatter(1, 1, True)
+        scatter(1, 0, False)
+        pair_product(("bank0_3", "bank0_2"))
+        gated_part(0, HALVES[0])
+        leave_bank(2, 0, False)
+        leave_bank(2, 1, True)
+        gated_part(0, HALVES[1])
+        scatter(2, 0, False)
+        turn(0, "spare")
+        scatter(2, 1, True)
+        leave_bank(3, 0, False)
+        leave_bank(3, 1, True)
+        quantise_hidden(0)
+        second_product(0, ("bank1_2", "bank0_1"))
+        scatter(3, 0, False)
+        scatter(3, 1, True)
+        leave_bank(0, 0, False)
+        leave_bank(0, 1, True)
+        scatter(0, 0, False)
+        scatter(0, 1, True)
+        nc.sync.dma_start(out=out[P:, :], in_=y_tokens[1][:])
+        nc.scalar.dma_start(out=out[:P, :], in_=y_tokens[0][:])

@@ -42,22 +42,17 @@ SPARE = 192
 ROUNDED_BYTES = 8
 WARM_UPS = 4
 SHARED = {
-    "a_pos1": ("on_relu1", 0),
-    "slots0_4_0": ("on_relu1", 0),
-    "slots1_4_0": ("on_relu1", 512),
     "words0_0_0": ("on_w1", 0),
-    "h_codes1": ("on_w1", 0),
-    "a_pos0": ("on_w1", 0),
-    "h_in1": ("on_turned1", 0),
-    "h3": ("on_turned1", 0),
-    "y_tokens0": ("on_turned1", 0),
-    "a_pos3": ("on_relu3", 0),
-    "y_slots1_0_0": ("on_relu3", 0),
-    "words0_1_0": ("on_w3", 0),
-    "h_codes_pair": ("on_w3", 0),
+    "h3": ("on_w1", 0),
     "h0": ("on_h0", 0),
-    "y_slots3_1_0": ("on_h0", 0),
-    "y_slots3_0_0": ("on_h0", 512),
+    "y_slots2_1_0": ("on_h0", 0),
+    "y_slots2_0_0": ("on_h0", 512),
+    "h_codes0": ("on_codes0", 0),
+    "y_slots3_1_0": ("on_codes0", 0),
+    "h_in0": ("on_turned0", 0),
+    "y_slots3_0_0": ("on_turned0", 0),
+    "words0_1_0": ("on_w3", 0),
+    "h_codes_all": ("on_w3", 0),
 }
 
 
@@ -338,87 +333,83 @@ def tile_moe_rag_glu_relu_kernel(
             for w in (W1, W3):
                 multiply(LAST, m, w)
 
-        def turn_pair(bank):
-            turned = psum.tile([P, 2, 2, P], F32, name="turned_pair", tag=bank)
-            for j, m in enumerate(PAIR):
+        EXPERT1 = FIRST + PAIR
+        h_all = sbuf([P, 3, 4 * P], BF16, "h_all")
+
+        def turn_some(tiles, bank, copy):
+            turned = psum.tile([P, len(tiles), 2, P], F32, name=f"turned{tiles[0]}", tag=bank)
+            for j, m in enumerate(tiles):
                 pairs = h[m][:].rearrange("p u q v -> p (u q v)").bitcast(F32)
                 for u in range(2):
                     nc.tensor.transpose(turned[:, j, u, :], pairs[:, P * u : P * (u + 1)], identity[:])
-            h_in[PAIR] = sbuf([P, 8 * P], BF16, "h_in_pair")
-            nc.scalar.copy(
-                h_in[PAIR][:].bitcast(F32).rearrange("p (j c u) -> p j c u", u=2, c=P),
+            part = h_all[:, tiles[0] - 1 : tiles[-1], :].rearrange("p j c -> p (j c)")
+            copy(
+                part.bitcast(F32).rearrange("p (j c u) -> p j c u", u=2, c=P),
                 turned[:].rearrange("p j u c -> p j c u"),
             )
 
-        def pair_product(bank_tags):
-            codes = sbuf([P, 2 * P], U32, "h_codes_pair")
-            scales = sbuf([P, 2 * P], U8, "h_scales_pair")
-            nc.vector.quantize_mx(out=codes[:].bitcast(E4M3), scales=scales[:], in_=h_in[PAIR][:])
+        def expert1_product(bank_tags):
+            codes = sbuf([P, 3 * P], U32, "h_codes_all")
+            scales = sbuf([P, 3 * P], U8, "h_scales_all")
+            nc.vector.quantize_mx(
+                out=codes[:].bitcast(E4M3), scales=scales[:], in_=h_all[:].rearrange("p j c -> p (j c)")
+            )
             for t, tag in enumerate(bank_tags):
-                both = psum.tile([P, 2 * P], F32, name=f"y_pair{t}", tag=tag)
-                nc.tensor.matmul_mx(
-                    out=both[:],
-                    lhsT=w2_codes[:, 1, 2 * P * t : 2 * P * (t + 1)].bitcast(E2M1),
-                    lhsT_scale=w2_plane[:, 1, P * t : P * (t + 1)],
-                    rhs=codes[:].bitcast(E4M3),
-                    rhs_scale=scales[:],
-                    start=True,
-                    stop=True,
-                )
-                for j, m in enumerate(PAIR):
-                    sums[m, t] = both[:, P * j : P * (j + 1)]
-
-        def gated_part(m, u):
-            if m not in h:
-                h[m] = sbuf([P, 2, P, 2], BF16, f"h{m}")
-            a_values = a_pos[m][:].rearrange("p (u q v) -> p u q v", u=2, v=2)
-            nc.vector.tensor_tensor(h[m][:, u], by_pairs(banks[m, W3][:])[:, u], a_values[:, u], MULT)
+                wide = psum.tile([P, 3 * P], F32, name=f"y_all{t}", tag=tag)
+                for cols in (slice(0, 2 * P), slice(2 * P, 3 * P)):
+                    nc.tensor.matmul_mx(
+                        out=wide[:, cols],
+                        lhsT=w2_codes[:, 1, 2 * P * t : 2 * P * (t + 1)].bitcast(E2M1),
+                        lhsT_scale=w2_plane[:, 1, P * t : P * (t + 1)],
+                        rhs=codes[:, cols].bitcast(E4M3),
+                        rhs_scale=scales[:, cols],
+                        start=True,
+                        stop=True,
+                    )
+                for j, m in enumerate(EXPERT1):
+                    sums[m, t] = wide[:, P * j : P * (j + 1)]
 
         last_pass(1)
         quantise_tokens(LAST, 1)
-        for m in PAIR:
+        for m in PAIR + FINAL:
             gather_scales(LAST, m, m + 1)
             gather_words(LAST, m, m + 1)
+        for m in PAIR:
             last_pass(m)
         relu(1, HALVES)
         relu(2)
         relu(3)
-        gated(1, HALVES)
-        turn(1, "spare")
-        gather_scales(LAST, 0, 1)
-        gather_words(LAST, 0, 1)
-        gated(2)
-        new_bank(0, W1, "bank1_1")
+        new_bank(0, W1, "spread")
         for s in range(PASSES):
             multiply(s, 0, W1)
-        quantise_hidden(1)
-        second_product(1, ("spread", "bank0_1"))
+        gated(1)
+        gated(2)
         gated(3)
-        turn_pair("bank1_3")
-        leave_bank(1, 0, False)
-        leave_bank(1, 1, True)
+        turn_some((1, 2), "bank1_3", nc.scalar.copy)
+        turn_some((3,), "bank0_2", nc.vector.tensor_copy)
         relu(0)
-        new_bank(0, W3, "spread")
+        new_bank(0, W3, "spare")
         for s in range(PASSES):
             multiply(s, 0, W3)
-        scatter(1, 1, True)
+        expert1_product(("bank0_1", "bank1_1"))
+        gated(0, HALVES)
+        leave_bank(1, 0, False)
+        leave_bank(1, 1, True)
         scatter(1, 0, False)
-        pair_product(("bank0_3", "bank0_2"))
-        gated_part(0, HALVES[0])
+        turn(0, "bank0_3")
         leave_bank(2, 0, False)
-        leave_bank(2, 1, True)
-        gated_part(0, HALVES[1])
-        scatter(2, 0, False)
-        turn(0, "spare")
-        scatter(2, 1, True)
         leave_bank(3, 0, False)
-        leave_bank(3, 1, True)
+        scatter(1, 1, True)
+        leave_bank(2, 1, True)
         quantise_hidden(0)
-        second_product(0, ("bank1_2", "bank0_1"))
+        second_product(0, ("bank1_2", "spread"))
+        scatter(2, 0, False)
+        scatter(2, 1, True)
         scatter(3, 0, False)
-        scatter(3, 1, True)
         leave_bank(0, 0, False)
+        leave_bank(3, 1, True)
         leave_bank(0, 1, True)
+        scatter(3, 1, True)
         scatter(0, 0, False)
         scatter(0, 1, True)
         nc.sync.dma_start(out=out[P:, :], in_=y_tokens[1][:])

@@ -43,16 +43,13 @@ ROUNDED_BYTES = 8
 WARM_UPS = 4
 SHARED = {
     "words0_0_0": ("on_w1", 0),
-    "h3": ("on_w1", 0),
-    "h0": ("on_h0", 0),
-    "y_slots2_1_0": ("on_h0", 0),
-    "y_slots2_0_0": ("on_h0", 512),
-    "h_codes0": ("on_codes0", 0),
-    "y_slots3_1_0": ("on_codes0", 0),
+    "h1": ("on_w1", 0),
+    "words0_1_0": ("on_w3", 512),
+    "h3": ("on_w3", 1024),
+    "h_codes1": ("on_w3", 512),
     "h_in0": ("on_turned0", 0),
-    "y_slots3_0_0": ("on_turned0", 0),
-    "words0_1_0": ("on_w3", 0),
-    "h_codes_all": ("on_w3", 0),
+    "y_slots2_0_0": ("on_turned0", 0),
+    "y_slots2_1_0": ("on_turned0", 512),
 }
 
 
@@ -152,15 +149,16 @@ def tile_moe_rag_glu_relu_kernel(
         load_x(LAST, slice(HALF, T))
         load_words(1, W1, 3, PASSES)
         load_words(1, W3, 3, PASSES)
-        nc.sync.dma_start(
-            out=w2_codes[:].bitcast(I32), in_=w2_words[:, 0].rearrange("e p b -> p e b").bitcast(I32)
-        )
         load_scales(0, W1)
         load_words(0, W1, 0, 2)
         load_words(0, W1, 2, PASSES)
         load_scales(0, W3)
-        load_words(0, W3, 0, 3)
+        load_words(0, W3, 1, 3)
+        load_words(0, W3, 0, 1)
         load_words(0, W3, 3, PASSES)
+        nc.sync.dma_start(
+            out=w2_codes[:].bitcast(I32), in_=w2_words[:, 0].rearrange("e p b -> p e b").bitcast(I32)
+        )
 
         nc.vector.memset(tok_scales[:].bitcast(I32), 0)
         nc.vector.memset(tok_codes[:, PASSES * T :].bitcast(I32), 0)
@@ -333,42 +331,6 @@ def tile_moe_rag_glu_relu_kernel(
             for w in (W1, W3):
                 multiply(LAST, m, w)
 
-        EXPERT1 = FIRST + PAIR
-        h_all = sbuf([P, 3, 4 * P], BF16, "h_all")
-
-        def turn_some(tiles, bank, copy):
-            turned = psum.tile([P, len(tiles), 2, P], F32, name=f"turned{tiles[0]}", tag=bank)
-            for j, m in enumerate(tiles):
-                pairs = h[m][:].rearrange("p u q v -> p (u q v)").bitcast(F32)
-                for u in range(2):
-                    nc.tensor.transpose(turned[:, j, u, :], pairs[:, P * u : P * (u + 1)], identity[:])
-            part = h_all[:, tiles[0] - 1 : tiles[-1], :].rearrange("p j c -> p (j c)")
-            copy(
-                part.bitcast(F32).rearrange("p (j c u) -> p j c u", u=2, c=P),
-                turned[:].rearrange("p j u c -> p j c u"),
-            )
-
-        def expert1_product(bank_tags):
-            codes = sbuf([P, 3 * P], U32, "h_codes_all")
-            scales = sbuf([P, 3 * P], U8, "h_scales_all")
-            nc.vector.quantize_mx(
-                out=codes[:].bitcast(E4M3), scales=scales[:], in_=h_all[:].rearrange("p j c -> p (j c)")
-            )
-            for t, tag in enumerate(bank_tags):
-                wide = psum.tile([P, 3 * P], F32, name=f"y_all{t}", tag=tag)
-                for cols in (slice(0, 2 * P), slice(2 * P, 3 * P)):
-                    nc.tensor.matmul_mx(
-                        out=wide[:, cols],
-                        lhsT=w2_codes[:, 1, 2 * P * t : 2 * P * (t + 1)].bitcast(E2M1),
-                        lhsT_scale=w2_plane[:, 1, P * t : P * (t + 1)],
-                        rhs=codes[:, cols].bitcast(E4M3),
-                        rhs_scale=scales[:, cols],
-                        start=True,
-                        stop=True,
-                    )
-                for j, m in enumerate(EXPERT1):
-                    sums[m, t] = wide[:, P * j : P * (j + 1)]
-
         last_pass(1)
         quantise_tokens(LAST, 1)
         for m in PAIR + FINAL:
@@ -376,39 +338,45 @@ def tile_moe_rag_glu_relu_kernel(
             gather_words(LAST, m, m + 1)
         for m in PAIR:
             last_pass(m)
-        relu(1, HALVES)
+        relu(1)
         relu(2)
         relu(3)
         new_bank(0, W1, "spread")
         for s in range(PASSES):
             multiply(s, 0, W1)
-        gated(1)
-        gated(2)
-        gated(3)
-        turn_some((1, 2), "bank1_3", nc.scalar.copy)
-        turn_some((3,), "bank0_2", nc.vector.tensor_copy)
         relu(0)
-        new_bank(0, W3, "spare")
+        gated(1)
+        turn(1, "spare")
+        gated(2)
+        new_bank(0, W3, "bank1_1")
         for s in range(PASSES):
             multiply(s, 0, W3)
-        expert1_product(("bank0_1", "bank1_1"))
+        gated(3)
+        turn(2, "bank1_3")
+        turn(3, "bank0_2")
+        quantise_hidden(1)
+        second_product(1, ("bank0_1", "bank1_2"))
         gated(0, HALVES)
         leave_bank(1, 0, False)
+        quantise_hidden(2)
+        second_product(2, ("bank0_3", "spread"))
         leave_bank(1, 1, True)
         scatter(1, 0, False)
-        turn(0, "bank0_3")
-        leave_bank(2, 0, False)
-        leave_bank(3, 0, False)
+        quantise_hidden(3)
+        turn(0, "spare")
+        second_product(3, ("bank1_3", "bank0_2"))
         scatter(1, 1, True)
-        leave_bank(2, 1, True)
         quantise_hidden(0)
-        second_product(0, ("bank1_2", "spread"))
+        second_product(0, ("bank1_1", "spare"))
+        leave_bank(2, 0, False)
+        leave_bank(2, 1, True)
         scatter(2, 0, False)
         scatter(2, 1, True)
-        scatter(3, 0, False)
-        leave_bank(0, 0, False)
+        leave_bank(3, 0, False)
         leave_bank(3, 1, True)
+        leave_bank(0, 0, False)
         leave_bank(0, 1, True)
+        scatter(3, 0, False)
         scatter(3, 1, True)
         scatter(0, 0, False)
         scatter(0, 1, True)

@@ -32,7 +32,7 @@ PAIR = (2, 3)
 FINAL = (0,)
 W1, W3 = 0, 1
 PIECES = (
-    ((0, 96, HALF), (HALF, 352, T)),
+    ((0, 192, T),),
     ((0, 352, T),),
     ((0, T, T),),
     ((0, T, T),),
@@ -131,8 +131,10 @@ def tile_moe_rag_glu_relu_kernel(
             nc.vector.memset(planes[1][w][:].bitcast(I32), 0)
             nc.gpsimd.memset(planes[0][w][:].bitcast(I32), 0)
 
-        load_x(0, slice(0, HALF))
-        load_x(0, slice(HALF, T))
+        first_rows = xT[: 4 * P, :].rearrange("(p d) w -> p d w", d=4)
+        x_pairs = [held.tile([P, 2, T], F32, name=f"x_pairs{u}", align_bytes=64) for u in range(2)]
+        for u in range(2):
+            nc.sync.dma_start(out=x_pairs[u][:], in_=first_rows[:, 2 * u : 2 * u + 2, :])
         nc.sync.dma_start(offsets[:], offs)
         nc.sync.dma_start(out=gate_rows[0:TILES, :], in_=gate[0].rearrange("(m j) -> m j", j=P))
         load_x(1)
@@ -184,10 +186,15 @@ def tile_moe_rag_glu_relu_kernel(
             x_bf = rounded.tile(
                 [P, end - first, 4], BF16, name=f"x_bf{s}_{first}", align_bytes=64, offset=rounded_at(s, first)
             )
-            dst, src = interleave(x_raw[s][:, :, first:cut], x_bf[:, 0 : cut - first, :])
+            if s == 0:
+                nc.vector.tensor_copy(*interleave(x_pairs[0][:], x_bf[:, :, 0:2]))
+                rows, place = x_pairs[1], x_bf[:, :, 2:4]
+            else:
+                rows, place = x_raw[s], x_bf[:]
+            dst, src = interleave(rows[:, :, first:cut], place[:, 0 : cut - first, :])
             nc.scalar.activation(dst, src, COPY)
             if cut < end:
-                dst, src = interleave(x_raw[s][:, :, cut:end], x_bf[:, cut - first : end - first, :])
+                dst, src = interleave(rows[:, :, cut:end], place[:, cut - first : end - first, :])
                 nc.vector.tensor_copy(dst, src)
             cols = slice(first_col(s) + first, first_col(s) + end)
             nc.vector.quantize_mx(
@@ -228,9 +235,8 @@ def tile_moe_rag_glu_relu_kernel(
             )
 
         all_scales = {}
-        quantise_tokens(0, 0)
         for s in range(PASSES):
-            quantise_tokens(s, 1 if s == 0 else 0)
+            quantise_tokens(s, 0)
             if s > 0:
                 gather_words(s - 1, 0, 1, rounded, rounded_at(s))
             if s == LAST - 1:

@@ -47,9 +47,6 @@ SHARED = {
     "words0_1_0": ("on_w3", 512),
     "h3": ("on_w3", 1024),
     "h_codes1": ("on_w3", 512),
-    "h_in0": ("on_turned0", 0),
-    "y_slots2_0_0": ("on_turned0", 0),
-    "y_slots2_1_0": ("on_turned0", 512),
 }
 
 
@@ -363,28 +360,16 @@ def tile_moe_rag_glu_relu_kernel(
         quantise_hidden(1)
         second_product(1, ("bank0_1", "bank1_2"))
         gated(0, HALVES)
-        leave_bank(1, 0, False)
-        quantise_hidden(2)
-        second_product(2, ("bank0_3", "spread"))
-        leave_bank(1, 1, True)
-        scatter(1, 0, False)
-        quantise_hidden(3)
         turn(0, "spare")
-        second_product(3, ("bank1_3", "bank0_2"))
-        scatter(1, 1, True)
-        quantise_hidden(0)
-        second_product(0, ("bank1_1", "spare"))
-        leave_bank(2, 0, False)
-        leave_bank(2, 1, True)
-        scatter(2, 0, False)
-        scatter(2, 1, True)
-        leave_bank(3, 0, False)
-        leave_bank(3, 1, True)
-        leave_bank(0, 0, False)
-        leave_bank(0, 1, True)
-        scatter(3, 0, False)
-        scatter(3, 1, True)
-        scatter(0, 0, False)
-        scatter(0, 1, True)
+        banks_of = {2: ("bank0_3", "spread"), 3: ("bank1_3", "bank0_2"), 0: ("bank1_1", "spare")}
+        for m in PAIR + FINAL:
+            quantise_hidden(m)
+            second_product(m, banks_of[m])
+        for m in FIRST + PAIR + FINAL:
+            leave_bank(m, 0, False)
+            leave_bank(m, 1, True)
+        for m in FIRST + PAIR + FINAL:
+            scatter(m, 0, False)
+            scatter(m, 1, True)
         nc.sync.dma_start(out=out[P:, :], in_=y_tokens[1][:])
         nc.scalar.dma_start(out=out[:P, :], in_=y_tokens[0][:])

@@ -33,7 +33,7 @@ FINAL = (0,)
 W1, W3 = 0, 1
 PIECES = (
     ((0, 192, T),),
-    ((0, 352, T),),
+    ((0, 416, T),),
     ((0, T, T),),
     ((0, T, T),),
     ((0, HALF, HALF), (HALF, T, T)),
@@ -135,8 +135,8 @@ def tile_moe_rag_glu_relu_kernel(
         nc.sync.dma_start(offsets[:], offs)
         nc.sync.dma_start(out=gate_rows[0:TILES, :], in_=gate[0].rearrange("(m j) -> m j", j=P))
         load_x(1)
-        load_rows(w2_plane, w2_scales.rearrange("e s (g r) i -> r g (e s) i", r=4))
         load_x(2)
+        load_rows(w2_plane, w2_scales.rearrange("e s (g r) i -> r g (e s) i", r=4))
         load_words(1, W1, 0, 1)
         load_words(1, W3, 0, 1)
         load_x(3)
@@ -313,13 +313,12 @@ def tile_moe_rag_glu_relu_kernel(
         gather_words(LAST, 1, 2)
         warm = psum.tile([P, H], F32, name="warm", tag="spare")
         for n in range(WARM_UPS):
-            m = (FIRST + PAIR)[n % 3]
             nc.tensor.matmul_mx(
                 out=warm[:],
-                lhsT=slot_codes[0, m].bitcast(E4M3),
-                lhsT_scale=slot_scales[0, m],
+                lhsT=slot_codes[0, 0].bitcast(E4M3),
+                lhsT_scale=slot_scales[0, 0],
                 rhs=words[1, W1, 0].bitcast(E2M1),
-                rhs_scale=all_scales[1][:],
+                rhs_scale=all_scales[0][:],
                 start=True,
                 stop=True,
             )
@@ -367,9 +366,13 @@ def tile_moe_rag_glu_relu_kernel(
             second_product(m, banks_of[m])
         for m in FIRST + PAIR + FINAL:
             leave_bank(m, 0, False)
-            leave_bank(m, 1, True)
+            leave_bank(m, 1, m not in FINAL)
         for m in FIRST + PAIR + FINAL:
             scatter(m, 0, False)
-            scatter(m, 1, True)
+            if m in FINAL:
+                window = y_tokens[1][:].indirect(offsets[:, 8 * m : 8 * (m + 1)])
+                nc.vector.tensor_copy(window, y_slots[m, 1, 0][:])
+            else:
+                scatter(m, 1, True)
         nc.sync.dma_start(out=out[P:, :], in_=y_tokens[1][:])
         nc.scalar.dma_start(out=out[:P, :], in_=y_tokens[0][:])

@@ -73,23 +73,23 @@ def tile_moe_rag_glu_relu_kernel(
         def sbuf(shape, dtype, name):
             if name in SHARED:
                 place, offset = SHARED[name]
-                return places[place].tile(shape, dtype, name=name, align_bytes=64, offset=offset)
-            return held.tile(shape, dtype, name=name, align_bytes=64)
+                return places[place].tile(shape, dtype, name=name, align_bytes=256, offset=offset)
+            return held.tile(shape, dtype, name=name, align_bytes=256)
 
         psum = ctx.enter_context(tc.psum_pool(name="psum", bufs=1))
 
         offsets = held.tile([P, T // 16], U16, name="offsets")
         x_raw = {}
-        tok_codes = held.tile([P, PASSES * T + SPARE], U32, name="tok_codes", align_bytes=64)
-        tok_scales = held.tile([P, PASSES * T + SPARE], U8, name="tok_scales", align_bytes=64)
+        tok_codes = held.tile([P, PASSES * T + SPARE], U32, name="tok_codes", align_bytes=256)
+        tok_scales = held.tile([P, PASSES * T + SPARE], U8, name="tok_scales", align_bytes=256)
         slot_codes, slot_scales = {}, {}
         words = {}
         planes = [
-            [held.tile([P, PASSES, H], U8, name=f"planes{e}_{w}", align_bytes=64) for w in (W1, W3)] for e in range(E)
+            [held.tile([P, PASSES, H], U8, name=f"planes{e}_{w}", align_bytes=256) for w in (W1, W3)] for e in range(E)
         ]
-        w2_codes = held.tile([P, E, 2 * N], U8, name="w2_codes", align_bytes=64)
-        w2_plane = held.tile([P, E, N], U8, name="w2_plane", align_bytes=64)
-        identity = held.tile([P, P], F32, name="identity")
+        w2_codes = held.tile([P, E, 2 * N], U8, name="w2_codes", align_bytes=256)
+        w2_plane = held.tile([P, E, N], U8, name="w2_plane", align_bytes=256)
+        identity = held.tile([P, P], F32, name="identity", align_bytes=256)
         banks = {
             (m, w): psum.tile([P, H], F32, name=f"bank{w}_{m}", tag=f"bank{w}_{m}")
             for w in (W1, W3)
@@ -98,7 +98,7 @@ def tile_moe_rag_glu_relu_kernel(
 
         def load_x(s, cols=slice(0, T)):
             if s not in x_raw:
-                x_raw[s] = held.tile([P, 4, T], F32, name=f"x_raw{s}", tag=f"x_raw{s}", align_bytes=64)
+                x_raw[s] = held.tile([P, 4, T], F32, name=f"x_raw{s}", tag=f"x_raw{s}", align_bytes=256)
             nc.sync.dma_start(
                 out=x_raw[s][:, :, cols],
                 in_=xT[4 * P * s : 4 * P * (s + 1), cols].rearrange("(p d) w -> p d w", d=4),
@@ -121,7 +121,7 @@ def tile_moe_rag_glu_relu_kernel(
         def load_scales(e, w):
             load_rows(planes[e][w], (w1_scales, w3_scales)[w][e].rearrange("s (g r) i -> r g s i", r=4))
 
-        gate_rows = held.tile([P, P], F32, name="gate_rows")
+        gate_rows = held.tile([P, P], F32, name="gate_rows", align_bytes=256)
         nc.gpsimd.memset(gate_rows[:], 0.0)
         nc.gpsimd.memset(w2_plane[:].bitcast(I32), 0)
         for w in (W1, W3):
@@ -129,7 +129,7 @@ def tile_moe_rag_glu_relu_kernel(
             nc.gpsimd.memset(planes[0][w][:].bitcast(I32), 0)
 
         first_rows = xT[: 4 * P, :].rearrange("(p d) w -> p d w", d=4)
-        x_pairs = [held.tile([P, 2, T], F32, name=f"x_pairs{u}", align_bytes=64) for u in range(2)]
+        x_pairs = [held.tile([P, 2, T], F32, name=f"x_pairs{u}", align_bytes=256) for u in range(2)]
         for u in range(2):
             nc.sync.dma_start(out=x_pairs[u][:], in_=first_rows[:, 2 * u : 2 * u + 2, :])
         nc.sync.dma_start(offsets[:], offs)
@@ -181,7 +181,7 @@ def tile_moe_rag_glu_relu_kernel(
         def quantise_tokens(s, piece):
             first, cut, end = PIECES[s][piece]
             x_bf = rounded.tile(
-                [P, end - first, 4], BF16, name=f"x_bf{s}_{first}", align_bytes=64, offset=rounded_at(s, first)
+                [P, end - first, 4], BF16, name=f"x_bf{s}_{first}", align_bytes=256, offset=rounded_at(s, first)
             )
             if s == 0:
                 nc.vector.tensor_copy(*interleave(x_pairs[0][:], x_bf[:, :, 0:2]))
@@ -206,7 +206,7 @@ def tile_moe_rag_glu_relu_kernel(
             if pool is None:
                 picked = sbuf(shape, table.dtype, name)
             else:
-                picked = pool.tile(shape, table.dtype, name=name, align_bytes=64, offset=offset)
+                picked = pool.tile(shape, table.dtype, name=name, align_bytes=256, offset=offset)
             window = table[:, first_col(s) : first_col(s) + T + SPARE]
             nc.vector.tensor_copy(picked[:], window.indirect(offsets[:, 8 * first : 8 * end]))
             for m in range(first, end):
@@ -237,7 +237,7 @@ def tile_moe_rag_glu_relu_kernel(
             if s > 0:
                 gather_words(s - 1, 0, 1, rounded, rounded_at(s))
             if s == LAST - 1:
-                gates = rounded.tile([P, T], F32, name="gates", align_bytes=64, offset=rounded_at(s, HALF))
+                gates = rounded.tile([P, T], F32, name="gates", align_bytes=256, offset=rounded_at(s, HALF))
                 nc.scalar.copy(gates[:], spread[:].rearrange("p m j -> p (m j)"))
             if s < LAST:
                 all_scales[s] = gather_scales(s, 0, TILES)

@@ -36,17 +36,21 @@ PIECES = (
     ((0, 416, T),),
     ((0, T, T),),
     ((0, T, T),),
-    ((0, HALF, HALF), (HALF, T, T)),
+    ((0, HALF, HALF), (HALF, 416, T)),
 )
 SPARE = 192
 ROUNDED_BYTES = 8
 WARM_UPS = 4
 SHARED = {
-    "words0_0_0": ("on_w1", 0),
-    "h1": ("on_w1", 0),
+    "tok_codes": ("on_codes", 0),
+    "h2": ("on_codes", 0),
+    "a_pos1": ("on_relu1", 0),
+    "slots1_4_0": ("on_relu1", 0),
+    "slots0_4_0": ("on_relu1", 256),
+    "slots1_2_0": ("on_relu1", 768),
+    "slots1_3_0": ("on_relu1", 1024),
     "words0_1_0": ("on_w3", 512),
     "h3": ("on_w3", 1024),
-    "h_codes1": ("on_w3", 512),
 }
 
 
@@ -80,7 +84,7 @@ def tile_moe_rag_glu_relu_kernel(
 
         offsets = held.tile([P, T // 16], U16, name="offsets")
         x_raw = {}
-        tok_codes = held.tile([P, PASSES * T + SPARE], U32, name="tok_codes", align_bytes=256)
+        tok_codes = sbuf([P, PASSES * T + SPARE], U32, "tok_codes")
         tok_scales = held.tile([P, PASSES * T + SPARE], U8, name="tok_scales", align_bytes=256)
         slot_codes, slot_scales = {}, {}
         words = {}
@@ -146,11 +150,11 @@ def tile_moe_rag_glu_relu_kernel(
         load_x(LAST, slice(0, HALF))
         load_words(1, W3, 1, 3)
         load_x(LAST, slice(HALF, T))
-        load_words(1, W1, 3, PASSES)
-        load_words(1, W3, 3, PASSES)
+        for s in (LAST - 1, LAST):
+            load_words(1, W1, s, s + 1)
+            load_words(1, W3, s, s + 1)
         load_scales(0, W1)
-        load_words(0, W1, 0, 2)
-        load_words(0, W1, 2, PASSES)
+        load_words(0, W1, 0, PASSES)
         load_scales(0, W3)
         load_words(0, W3, 1, 3)
         load_words(0, W3, 0, 1)
@@ -240,7 +244,7 @@ def tile_moe_rag_glu_relu_kernel(
                 gates = rounded.tile([P, T], F32, name="gates", align_bytes=256, offset=rounded_at(s, HALF))
                 nc.scalar.copy(gates[:], spread[:].rearrange("p m j -> p (m j)"))
             if s < LAST:
-                all_scales[s] = gather_scales(s, 0, TILES)
+                all_scales[s] = gather_scales(s, int(s >= 2), TILES)
                 gather_words(s, 1, TILES)
         h, a_pos, h_in, hidden, sums, y_slots = {}, {}, {}, {}, {}, {}
         y_tokens = [sbuf([P, T], F32, f"y_tokens{t}") for t in range(2)]
@@ -335,7 +339,7 @@ def tile_moe_rag_glu_relu_kernel(
 
         last_pass(1)
         quantise_tokens(LAST, 1)
-        for m in PAIR + FINAL:
+        for m in PAIR:
             gather_scales(LAST, m, m + 1)
             gather_words(LAST, m, m + 1)
         for m in PAIR:
@@ -343,12 +347,15 @@ def tile_moe_rag_glu_relu_kernel(
         relu(1)
         relu(2)
         relu(3)
+        gated(1)
+        for s in range(2, PASSES):
+            gather_scales(s, 0, 1)
+        gather_words(LAST, 0, 1)
+        turn(1, "spare")
         new_bank(0, W1, "spread")
         for s in range(PASSES):
             multiply(s, 0, W1)
         relu(0)
-        gated(1)
-        turn(1, "spare")
         gated(2)
         new_bank(0, W3, "bank1_1")
         for s in range(PASSES):

@@ -140,14 +140,14 @@ def tile_moe_rag_glu_relu_kernel(
         nc.sync.dma_start(out=gate_rows[0:TILES, :], in_=gate[0].rearrange("(m j) -> m j", j=P))
         load_x(1)
         load_x(2)
-        load_rows(w2_plane, w2_scales.rearrange("e s (g r) i -> r g (e s) i", r=4))
         load_words(1, W1, 0, 1)
-        load_words(1, W3, 0, 1)
         load_x(3)
         load_scales(1, W1)
         load_scales(1, W3)
+        load_words(1, W3, 0, 1)
         load_words(1, W1, 1, 3)
         load_x(LAST, slice(0, HALF))
+        load_rows(w2_plane, w2_scales.rearrange("e s (g r) i -> r g (e s) i", r=4))
         load_words(1, W3, 1, 3)
         load_x(LAST, slice(HALF, T))
         for s in (LAST - 1, LAST):

@@ -44,6 +44,16 @@ WARM_UPS = 4
 SHARED = {
     "tok_codes": ("on_codes", 0),
     "h2": ("on_codes", 0),
+    "x_raw1_0": ("on_x1", 0),
+    "slots0_0_0": ("on_x1", 0),
+    "x_raw2_0": ("on_x2", 0),
+    "slots0_1_0": ("on_x2", 0),
+    "x_raw3_0": ("on_x3", 0),
+    "slots0_2_0": ("on_x3", 0),
+    "x_raw4_0": ("on_x4", 0),
+    "slots0_3_0": ("on_x4", 0),
+    "x_raw4_256": ("on_x5", 0),
+    "slots1_1_0": ("on_x5", 0),
     "a_pos1": ("on_relu1", 0),
     "slots1_4_0": ("on_relu1", 0),
     "slots0_4_0": ("on_relu1", 256),
@@ -100,12 +110,11 @@ def tile_moe_rag_glu_relu_kernel(
             for m in FIRST + PAIR
         }
 
-        def load_x(s, cols=slice(0, T)):
-            if s not in x_raw:
-                x_raw[s] = held.tile([P, 4, T], F32, name=f"x_raw{s}", tag=f"x_raw{s}", align_bytes=256)
+        def load_x(s, first=0, end=T):
+            x_raw[s, first] = sbuf([P, 4, end - first], F32, f"x_raw{s}_{first}")
             nc.sync.dma_start(
-                out=x_raw[s][:, :, cols],
-                in_=xT[4 * P * s : 4 * P * (s + 1), cols].rearrange("(p d) w -> p d w", d=4),
+                out=x_raw[s, first][:],
+                in_=xT[4 * P * s : 4 * P * (s + 1), first:end].rearrange("(p d) w -> p d w", d=4),
             )
 
         def load_words(e, w, first, end):
@@ -144,12 +153,12 @@ def tile_moe_rag_glu_relu_kernel(
         load_x(3)
         load_scales(1, W1)
         load_scales(1, W3)
-        load_words(1, W3, 0, 1)
         load_words(1, W1, 1, 3)
-        load_x(LAST, slice(0, HALF))
+        load_x(LAST, 0, HALF)
+        load_words(1, W3, 0, 1)
         load_rows(w2_plane, w2_scales.rearrange("e s (g r) i -> r g (e s) i", r=4))
         load_words(1, W3, 1, 3)
-        load_x(LAST, slice(HALF, T))
+        load_x(LAST, HALF, T)
         for s in (LAST - 1, LAST):
             load_words(1, W1, s, s + 1)
             load_words(1, W3, s, s + 1)
@@ -191,11 +200,11 @@ def tile_moe_rag_glu_relu_kernel(
                 nc.vector.tensor_copy(*interleave(x_pairs[0][:], x_bf[:, :, 0:2]))
                 rows, place = x_pairs[1], x_bf[:, :, 2:4]
             else:
-                rows, place = x_raw[s], x_bf[:]
-            dst, src = interleave(rows[:, :, first:cut], place[:, 0 : cut - first, :])
+                rows, place = x_raw[s, first], x_bf[:]
+            dst, src = interleave(rows[:, :, 0 : cut - first], place[:, 0 : cut - first, :])
             nc.scalar.activation(dst, src, COPY)
             if cut < end:
-                dst, src = interleave(rows[:, :, cut:end], place[:, cut - first : end - first, :])
+                dst, src = interleave(rows[:, :, cut - first : end - first], place[:, cut - first : end - first, :])
                 nc.vector.tensor_copy(dst, src)
             cols = slice(first_col(s) + first, first_col(s) + end)
             nc.vector.quantize_mx(
@@ -239,12 +248,12 @@ def tile_moe_rag_glu_relu_kernel(
         for s in range(PASSES):
             quantise_tokens(s, 0)
             if s > 0:
-                gather_words(s - 1, 0, 1, rounded, rounded_at(s))
+                gather_words(s - 1, 0, 1)
             if s == LAST - 1:
                 gates = rounded.tile([P, T], F32, name="gates", align_bytes=256, offset=rounded_at(s, HALF))
                 nc.scalar.copy(gates[:], spread[:].rearrange("p m j -> p (m j)"))
             if s < LAST:
-                all_scales[s] = gather_scales(s, int(s >= 2), TILES)
+                all_scales[s] = gather_scales(s, int(s >= 1), TILES)
                 gather_words(s, 1, TILES)
         h, a_pos, h_in, hidden, sums, y_slots = {}, {}, {}, {}, {}, {}
         y_tokens = [sbuf([P, T], F32, f"y_tokens{t}") for t in range(2)]
@@ -339,6 +348,7 @@ def tile_moe_rag_glu_relu_kernel(
 
         last_pass(1)
         quantise_tokens(LAST, 1)
+        gather_scales(1, 0, 1)
         for m in PAIR:
             gather_scales(LAST, m, m + 1)
             gather_words(LAST, m, m + 1)

from contextlib import ExitStack

import concourse.mybir as mybir
from concourse.masks import make_identity

FLOPS = 2818572288

F32 = mybir.dt.float32
BF16 = mybir.dt.bfloat16
I32 = mybir.dt.int32
U32 = mybir.dt.uint32
U16 = mybir.dt.uint16
U8 = mybir.dt.uint8
E4M3 = mybir.dt.float8_e4m3fn_x4
E2M1 = mybir.dt.float4_e2m1fn_x4
COPY = mybir.ActivationFunctionType.Copy
RELU = mybir.ActivationFunctionType.Relu
MULT = mybir.AluOpType.mult

P = 128
T = 512
HALF = T // 2
E = 2
H = 512
N = 256
PASSES = 5
LAST = PASSES - 1
TILES = 4
TILE_EXPERT = (0, 1, 1, 1)
FIRST = (1,)
PAIR = (2, 3)
FINAL = (0,)
W1, W3 = 0, 1
PIECES = (
    ((0, 192, T),),
    ((0, 416, T),),
    ((0, T, T),),
    ((0, T, T),),
    ((0, HALF, HALF), (HALF, 416, T)),
)
SPARE = 192
ROUNDED_BYTES = 8
WARM_UPS = 4
SHARED = {
    "tok_codes": ("on_codes", 0),
    "h2": ("on_codes", 0),
    "x_raw1_0": ("on_x1", 0),
    "slots0_0_0": ("on_x1", 0),
    "x_raw2_0": ("on_x2", 0),
    "slots0_1_0": ("on_x2", 0),
    "x_raw3_0": ("on_x3", 0),
    "slots0_2_0": ("on_x3", 0),
    "x_raw4_0": ("on_x4", 0),
    "slots0_3_0": ("on_x4", 0),
    "x_raw4_256": ("on_x5", 0),
    "slots1_1_0": ("on_x5", 0),
    "a_pos1": ("on_relu1", 0),
    "slots1_4_0": ("on_relu1", 0),
    "slots0_4_0": ("on_relu1", 256),
    "slots1_2_0": ("on_relu1", 768),
    "slots1_3_0": ("on_relu1", 1024),
    "words0_1_0": ("on_w3", 512),
    "h3": ("on_w3", 1024),
}


def interleave(rows, grouped):
    return (
        grouped.rearrange("p (c i) d -> p c d i", i=4),
        rows.rearrange("p d (c i) -> p c d i", i=4),
    )


def by_pairs(sums):
    return sums.rearrange("p (q u v) -> p u q v", u=2, v=2)


def tile_moe_rag_glu_relu_kernel(
    tc, xT, w1_words, w1_scales, w3_words, w3_scales, w2_words, w2_scales, gate, offs, out
):
    nc = tc.nc
    with ExitStack() as ctx:
        held = ctx.enter_context(tc.tile_pool(name="held", bufs=1))
        rounded = ctx.enter_context(tc.tile_pool(name="rounded", bufs=1))
        places = {name: ctx.enter_context(tc.tile_pool(name=name, bufs=1)) for name in sorted({p for p, o in SHARED.values()})}

        def sbuf(shape, dtype, name):
            if name in SHARED:
                place, offset = SHARED[name]
                return places[place].tile(shape, dtype, name=name, align_bytes=256, offset=offset)
            return held.tile(shape, dtype, name=name, align_bytes=256)

        psum = ctx.enter_context(tc.psum_pool(name="psum", bufs=1))

        offsets = held.tile([P, T // 16], U16, name="offsets")
        x_raw = {}
        tok_codes = sbuf([P, PASSES * T + SPARE], U32, "tok_codes")
        tok_scales = held.tile([P, PASSES * T + SPARE], U8, name="tok_scales", align_bytes=256)
        slot_codes, slot_scales = {}, {}
        words = {}
        planes = [
            [held.tile([P, PASSES, H], U8, name=f"planes{e}_{w}", align_bytes=256) for w in (W1, W3)] for e in range(E)
        ]
        w2_codes = held.tile([P, E, 2 * N], U8, name="w2_codes", align_bytes=256)
        w2_plane = held.tile([P, E, N], U8, name="w2_plane", align_bytes=256)
        identity = held.tile([P, P], F32, name="identity", align_bytes=256)
        banks = {
            (m, w): psum.tile([P, H], F32, name=f"bank{w}_{m}", tag=f"bank{w}_{m}")
            for w in (W1, W3)
            for m in FIRST + PAIR
        }

        def load_x(s, first=0, end=T):
            x_raw[s, first] = sbuf([P, 4, end - first], F32, f"x_raw{s}_{first}")
            nc.sync.dma_start(
                out=x_raw[s, first][:],
                in_=xT[4 * P * s : 4 * P * (s + 1), first:end].rearrange("(p d) w -> p d w", d=4),
            )

        def load_words(e, w, first, end):
            name = f"words{e}_{w}_{first}"
            part = sbuf([P, end - first, 2 * H], U8, name)
            nc.sync.dma_start(
                out=part[:].bitcast(I32),
                in_=(w1_words, w3_words)[w][e, first:end].rearrange("s p b -> p s b").bitcast(I32),
            )
            for s in range(first, end):
                words[e, w, s] = part[:, s - first, :]

        def load_rows(plane, by_row):
            for r in range(4):
                nc.sync.dma_start(out=plane[r:P:32].bitcast(I32), in_=by_row[r].bitcast(I32))

        def load_scales(e, w):
            load_rows(planes[e][w], (w1_scales, w3_scales)[w][e].rearrange("s (g r) i -> r g s i", r=4))

        gate_rows = held.tile([P, P], F32, name="gate_rows", align_bytes=256)
        nc.gpsimd.memset(gate_rows[:], 0.0)
        nc.gpsimd.memset(w2_plane[:].bitcast(I32), 0)
        for w in (W1, W3):
            nc.vector.memset(planes[1][w][:].bitcast(I32), 0)
            nc.gpsimd.memset(planes[0][w][:].bitcast(I32), 0)

        first_rows = xT[: 4 * P, :].rearrange("(p d) w -> p d w", d=4)
        x_pairs = [held.tile([P, 2, T], F32, name=f"x_pairs{u}", align_bytes=256) for u in range(2)]
        for u in range(2):
            nc.sync.dma_start(out=x_pairs[u][:], in_=first_rows[:, 2 * u : 2 * u + 2, :])
        nc.sync.dma_start(offsets[:], offs)
        nc.sync.dma_start(out=gate_rows[0:TILES, :], in_=gate[0].rearrange("(m j) -> m j", j=P))
        load_x(1)
        load_x(2)
        load_words(1, W1, 0, 1)
        load_x(3)
        load_scales(1, W1)
        load_scales(1, W3)
        load_words(1, W1, 1, 3)
        load_x(LAST, 0, HALF)
        load_words(1, W3, 0, 1)
        load_rows(w2_plane, w2_scales.rearrange("e s (g r) i -> r g (e s) i", r=4))
        load_words(1, W3, 1, 3)
        load_x(LAST, HALF, T)
        for s in (LAST - 1, LAST):
            load_words(1, W1, s, s + 1)
            load_words(1, W3, s, s + 1)
        load_scales(0, W1)
        load_words(0, W1, 0, PASSES)
        load_scales(0, W3)
        load_words(0, W3, 1, 3)
        load_words(0, W3, 0, 1)
        load_words(0, W3, 3, PASSES)
        nc.sync.dma_start(
            out=w2_codes[:].bitcast(I32), in_=w2_words[:, 0].rearrange("e p b -> p e b").bitcast(I32)
        )

        nc.vector.memset(tok_scales[:].bitcast(I32), 0)
        nc.vector.memset(tok_codes[:, PASSES * T :].bitcast(I32), 0)
        nc.vector.memset(tok_codes[:, HALF:T].bitcast(I32), 0)
        make_identity(nc, identity[:])

        by_slot = psum.tile([P, P], F32, name="by_slot", tag="spare")
        nc.tensor.transpose(by_slot[:], gate_rows[:], identity[:])
        gate_cols = held.tile([P, TILES], F32, name="gate_cols")
        nc.scalar.copy(gate_cols[:], by_slot[:, 0:TILES])
        spread = psum.tile([P, TILES, P], F32, name="spread", tag="spread")
        for m in range(TILES):
            nc.tensor.transpose(spread[:, m, :], gate_cols[:, m : m + 1].to_broadcast([P, P]), identity[:])

        def first_col(s):
            return (LAST - s) * T

        def rounded_at(s, token=0):
            return ROUNDED_BYTES * (T * s + token)

        def quantise_tokens(s, piece):
            first, cut, end = PIECES[s][piece]
            x_bf = rounded.tile(
                [P, end - first, 4], BF16, name=f"x_bf{s}_{first}", align_bytes=256, offset=rounded_at(s, first)
            )
            if s == 0:
                nc.vector.tensor_copy(*interleave(x_pairs[0][:], x_bf[:, :, 0:2]))
                rows, place = x_pairs[1], x_bf[:, :, 2:4]
            else:
                rows, place = x_raw[s, first], x_bf[:]
            dst, src = interleave(rows[:, :, 0 : cut - first], place[:, 0 : cut - first, :])
            nc.scalar.activation(dst, src, COPY)
            if cut < end:
                dst, src = interleave(rows[:, :, cut - first : end - first], place[:, cut - first : end - first, :])
                nc.vector.tensor_copy(dst, src)
            cols = slice(first_col(s) + first, first_col(s) + end)
            nc.vector.quantize_mx(
                out=tok_codes[:, cols].bitcast(E4M3),
                scales=tok_scales[:, cols],
                in_=x_bf[:].rearrange("p w d -> p (w d)"),
            )

        def gather(table, found, s, first, end, pool=None, offset=None):
            name = f"slots{int(table.dtype == U8)}_{s}_{first}"
            shape = [P, P * (end - first)]
            if pool is None:
                picked = sbuf(shape, table.dtype, name)
            else:
                picked = pool.tile(shape, table.dtype, name=name, align_bytes=256, offset=offset)
            window = table[:, first_col(s) : first_col(s) + T + SPARE]
            nc.vector.tensor_copy(picked[:], window.indirect(offsets[:, 8 * first : 8 * end]))
            for m in range(first, end):
                found[s, m] = picked[:, P * (m - first) : P * (m - first + 1)]
            return picked

        def gather_words(s, first, end, pool=None, offset=None):
            gather(tok_codes[:], slot_codes, s, first, end, pool, offset)

        def gather_scales(s, first, end, pool=None, offset=None):
            return gather(tok_scales[:], slot_scales, s, first, end, pool, offset)

        def multiply(s, m, w):
            e = TILE_EXPERT[m]
            nc.tensor.matmul_mx(
                out=banks[m, w][:],
                lhsT=slot_codes[s, m].bitcast(E4M3),
                lhsT_scale=slot_scales[s, m],
                rhs=words[e, w, s].bitcast(E2M1),
                rhs_scale=planes[e][w][:, s, :],
                start=(s == 0),
                stop=(s == LAST),
            )

        all_scales = {}
        for s in range(PASSES):
            quantise_tokens(s, 0)
            if s > 0:
                gather_words(s - 1, 0, 1)
            if s == LAST - 1:
                gates = rounded.tile([P, T], F32, name="gates", align_bytes=256, offset=rounded_at(s, HALF))
                nc.scalar.copy(gates[:], spread[:].rearrange("p m j -> p (m j)"))
            if s < LAST:
                all_scales[s] = gather_scales(s, int(s >= 1), TILES)
                gather_words(s, 1, TILES)
        h, a_pos, h_in, hidden, sums, y_slots = {}, {}, {}, {}, {}, {}
        y_tokens = [sbuf([P, T], F32, f"y_tokens{t}") for t in range(2)]
        WHOLE, HALVES = (slice(0, 2),), (slice(0, 1), slice(1, 2))

        def relu(m, parts=WHOLE):
            a_pos[m] = sbuf([P, H], F32, f"a_pos{m}")
            a_values = a_pos[m][:].rearrange("p (u q v) -> p u q v", u=2, v=2)
            for u in parts:
                nc.scalar.activation(a_values[:, u], by_pairs(banks[m, W1][:])[:, u], RELU)

        def gated(m, parts=WHOLE):
            h[m] = sbuf([P, 2, P, 2], BF16, f"h{m}")
            a_values = a_pos[m][:].rearrange("p (u q v) -> p u q v", u=2, v=2)
            for u in parts:
                nc.vector.tensor_tensor(h[m][:, u], by_pairs(banks[m, W3][:])[:, u], a_values[:, u], MULT)

        def turn(m, bank):
            turned = psum.tile([P, 2, P], F32, name=f"turned{m}", tag=bank)
            pairs = h[m][:].rearrange("p u q v -> p (u q v)").bitcast(F32)
            for u in range(2):
                nc.tensor.transpose(turned[:, u, :], pairs[:, P * u : P * (u + 1)], identity[:])
            h_in[m] = sbuf([P, 4 * P], BF16, f"h_in{m}")
            nc.scalar.copy(
                h_in[m][:].bitcast(F32).rearrange("p (c u) -> p c u", u=2),
                turned[:].rearrange("p u c -> p c u"),
            )

        def quantise_hidden(m):
            codes = sbuf([P, P], U32, f"h_codes{m}")
            scales = sbuf([P, P], U8, f"h_scales{m}")
            nc.vector.quantize_mx(out=codes[:].bitcast(E4M3), scales=scales[:], in_=h_in[m][:])
            hidden[m] = codes, scales

        def second_product(m, bank_tags):
            codes, scales = hidden[m]
            e = TILE_EXPERT[m]
            for t, tag in enumerate(bank_tags):
                sums[m, t] = psum.tile([P, P], F32, name=f"y{m}_{t}", tag=tag)
                nc.tensor.matmul_mx(
                    out=sums[m, t][:],
                    lhsT=w2_codes[:, e, 2 * P * t : 2 * P * (t + 1)].bitcast(E2M1),
                    lhsT_scale=w2_plane[:, e, P * t : P * (t + 1)],
                    rhs=codes[:].bitcast(E4M3),
                    rhs_scale=scales[:],
                    start=True,
                    stop=True,
                )

        def leave_bank(m, t, by_vector, first=0, end=P):
            y_slots[m, t, first] = sbuf([P, end - first], F32, f"y_slots{m}_{t}_{first}")
            if by_vector:
                nc.scalar.copy(y_slots[m, t, first][:], sums[m, t][:, first:end])
            else:
                nc.vector.tensor_tensor(
                    y_slots[m, t, first][:], sums[m, t][:, first:end], gates[:, P * m + first : P * m + end], MULT
                )

        def scatter(m, t, by_vector, first=0, end=P):
            window = y_tokens[t][:].indirect(offsets[:, (P * m + first) // 16 : (P * m + end) // 16])
            if by_vector:
                nc.vector.tensor_tensor(window, y_slots[m, t, first][:], gates[:, P * m + first : P * m + end], MULT)
            else:
                nc.scalar.activation(window, y_slots[m, t, first][:], COPY)

        def new_bank(m, w, tag):
            banks[m, w] = psum.tile([P, H], F32, name=f"bank{w}_{m}", tag=tag)

        gather_scales(LAST, 1, 2)
        gather_words(LAST, 1, 2)
        warm = psum.tile([P, H], F32, name="warm", tag="spare")
        for n in range(WARM_UPS):
            nc.tensor.matmul_mx(
                out=warm[:],
                lhsT=slot_codes[0, 0].bitcast(E4M3),
                lhsT_scale=slot_scales[0, 0],
                rhs=words[1, W1, 0].bitcast(E2M1),
                rhs_scale=all_scales[0][:],
                start=True,
                stop=True,
            )


        for s in range(LAST):
            for m in FIRST + PAIR:
                for w in (W1, W3):
                    multiply(s, m, w)

        def last_pass(m):
            for w in (W1, W3):
                multiply(LAST, m, w)

        last_pass(1)
        quantise_tokens(LAST, 1)
        gather_scales(1, 0, 1)
        for m in PAIR:
            gather_scales(LAST, m, m + 1)
            gather_words(LAST, m, m + 1)
        for m in PAIR:
            last_pass(m)
        relu(1)
        relu(2)
        relu(3)
        gated(1)
        for s in range(2, PASSES):
            gather_scales(s, 0, 1)
        gather_words(LAST, 0, 1)
        turn(1, "spare")
        new_bank(0, W1, "spread")
        for s in range(PASSES):
            multiply(s, 0, W1)
        relu(0)
        gated(2)
        new_bank(0, W3, "bank1_1")
        for s in range(PASSES):
            multiply(s, 0, W3)
        gated(3)
        turn(2, "bank1_3")
        turn(3, "bank0_2")
        quantise_hidden(1)
        second_product(1, ("bank0_1", "bank1_2"))
        gated(0, HALVES)
        turn(0, "spare")
        banks_of = {2: ("bank0_3", "spread"), 3: ("bank1_3", "bank0_2"), 0: ("bank1_1", "spare")}
        for m in PAIR + FINAL:
            quantise_hidden(m)
            second_product(m, banks_of[m])
        for m in FIRST + PAIR + FINAL:
            leave_bank(m, 0, False)
            leave_bank(m, 1, m not in FINAL)
        for m in FIRST + PAIR + FINAL:
            scatter(m, 0, False)
            if m in FINAL:
                window = y_tokens[1][:].indirect(offsets[:, 8 * m : 8 * (m + 1)])
                nc.vector.tensor_copy(window, y_slots[m, 1, 0][:])
            else:
                scatter(m, 1, True)
        nc.sync.dma_start(out=out[P:, :], in_=y_tokens[1][:])
        nc.scalar.dma_start(out=out[:P, :], in_=y_tokens[0][:])
